import numpy as np
import ml_dtypes


def mxq(x, axis, fmt="e4m3"):
    dtype, down = {"e4m3": (ml_dtypes.float8_e4m3fn, 7), "e5m2": (ml_dtypes.float8_e5m2, 14)}[fmt]
    v = np.moveaxis(np.asarray(x, np.float32).astype(ml_dtypes.bfloat16).astype(np.float64), axis, -1)
    blocks = v.reshape(v.shape[:-1] + (-1, 32))
    amax = np.abs(blocks).max(-1, keepdims=True)
    byte = np.maximum(np.where(amax > 0, np.frexp(amax)[1] - 1 + 127, 0) - down, 1)
    scale = np.exp2(byte - 127.0)
    codes = (blocks / scale).astype(np.float32).astype(dtype).astype(np.float64)
    return np.moveaxis((codes * scale).reshape(v.shape), -1, axis)


WIDE = False


def mx_kscale(k):
    if not WIDE:
        return np.ones(k)
    levels = np.array([10, -10, 5, -5, 0])
    if k % 512:
        return np.exp2(np.random.permutation(np.resize(levels, k // 32))).repeat(32)
    a = np.empty((k // 512, 16))
    for p in range(k // 512):
        a[p, :8] = np.random.permutation(np.resize(levels, 8))
        for g in range(8):
            far = levels[np.abs(levels - a[p, g]) >= 10]
            a[p, g + 8] = far[np.random.randint(len(far))]
    return np.exp2(a.ravel()).repeat(32)


def f64(x):
    return np.asarray(x).astype(np.float64)


def striped(idx):
    return np.tile(idx.reshape(-1, 16).T, (8, 1)).astype(np.uint16)


def unstriped(offs):
    return offs[:16].T.reshape(-1).astype(np.int64)


E2M1 = np.array([0.0, 0.5, 1.0, 1.5, 2.0, 3.0, 4.0, 6.0, -0.0, -0.5, -1.0, -1.5, -2.0, -3.0, -4.0, -6.0])


def pack_weight(w, fmt):
    k, n = w.shape
    w = f64(np.asarray(w, np.float32).astype(ml_dtypes.bfloat16)).reshape(k // 32, 32, n)
    amax = np.abs(w).max(1)
    if fmt == "e4m3":
        byte = np.frexp(amax)[1] - 1 + 127 - 7
    else:
        mant, ex = np.frexp(amax / 6.0)
        byte = np.where(mant > 0.5, ex, ex - 1) + 127
    byte = np.clip(np.where(amax > 0, byte, 1), 1, 254)
    scaled = (w * np.exp2(127.0 - byte)[:, None, :]).reshape(k, n).astype(np.float32)
    by_word = np.ascontiguousarray(scaled.reshape(k // 512, 128, 4, n).transpose(0, 1, 3, 2))
    if fmt == "e4m3":
        words = by_word.astype(ml_dtypes.float8_e4m3fn).view(np.uint8)
    else:
        c = by_word.astype(ml_dtypes.float4_e2m1fn).view(np.uint8) & 0xF
        words = (c[..., 0::2] | (c[..., 1::2] << 4)).reshape(k // 512, 128, 2 * n)
    return np.ascontiguousarray(words), np.ascontiguousarray(byte.astype(np.uint8).reshape(k // 512, 16, n))


def unpack_weight(words, scales, fmt):
    g, _, n = scales.shape
    words = np.ascontiguousarray(words).reshape(g, 128, n, -1)
    if fmt == "e4m3":
        vals = words.view(ml_dtypes.float8_e4m3fn).astype(np.float64)
    else:
        nib = np.empty((g, 128, n, 4), np.uint8)
        nib[..., 0::2] = words & 0xF
        nib[..., 1::2] = words >> 4
        vals = E2M1[nib]
    vals = vals * np.repeat(np.exp2(scales.astype(np.float64) - 127.0), 8, axis=1)[..., None]
    return vals.transpose(0, 1, 3, 2).reshape(g * 512, n)


def gelu(v):
    return 0.5 * v * (1.0 + np.tanh(np.sqrt(2.0 / np.pi) * (v + 0.044715 * v**3)))


K, H, T, S, T2, S2 = 1024, 512, 2048, 1024, 2048, 512

def setup_inputs():
    n = np.random.standard_normal
    s = mx_kscale(K)[:, None]
    u = mx_kscale(H)[:, None]
    tab_words, tab_scales = pack_weight(n((K, T)) * s, "e4m3")
    wa = (n((K, H)) / np.sqrt(K) / s * u.T).astype(np.float32)
    wb_words, wb_scales = pack_weight(n((K, H)) / np.sqrt(K) / s * u.T, "e4m3")
    wg_words, wg_scales = pack_weight(n((K, H)) / np.sqrt(K) / s, "e2m1")
    tab2_words, tab2_scales = pack_weight(n((H, T2)) / np.sqrt(H) / u, "e4m3")
    return {
        "tab_words": tab_words, "tab_scales": tab_scales,
        "offs": striped(np.random.permutation(T)[:S]),
        "wa": wa,
        "wb_words": wb_words, "wb_scales": wb_scales,
        "wg_words": wg_words, "wg_scales": wg_scales,
        "tab2_words": tab2_words, "tab2_scales": tab2_scales,
        "offs2": striped(np.random.permutation(T2)[:S2]),
        "bias": (0.5 * n(S2)).astype(np.float32),
    }

def reference(tab_words, tab_scales, offs, wa, wb_words, wb_scales, wg_words, wg_scales,
              tab2_words, tab2_scales, offs2, bias):
    v = unpack_weight(tab_words, tab_scales, "e4m3")[:, unstriped(offs)]
    v2 = unpack_weight(tab2_words, tab2_scales, "e4m3")[:, unstriped(offs2)]
    a = mxq(f64(wa), 0, "e4m3").T @ v
    b = unpack_weight(wb_words, wb_scales, "e4m3").T @ v
    z = unpack_weight(wg_words, wg_scales, "e2m1").T @ v
    g = 1.0 / (1.0 + np.exp(-z))
    h = b + g * (a - b)
    y = v2.T @ mxq(h, 0, "e4m3")
    return y + f64(bias)[:, None]

@@ -1,0 +1,238 @@
+from contextlib import ExitStack
+
+import concourse.mybir as mybir
+from concourse.masks import make_identity
+
+K, H, T, S, T2, S2 = 1024, 512, 2048, 1024, 2048, 512
+FLOPS = 2 * (3 * K * H * S + H * S2 * S)
+
+F32 = mybir.dt.float32
+BF16 = mybir.dt.bfloat16
+I32 = mybir.dt.int32
+U32 = mybir.dt.uint32
+U16 = mybir.dt.uint16
+U8 = mybir.dt.uint8
+FP8X4 = mybir.dt.float8_e4m3fn_x4
+FP4X4 = mybir.dt.float4_e2m1fn_x4
+ALU = mybir.AluOpType
+ACT = mybir.ActivationFunctionType
+
+P = 128
+PASSES = K // 512
+SLICE = 256
+UNITS = S // P
+WB_ROW = 4
+V2_ROW = 8
+
+
+def tile_list_gated_link_logits_kernel(tc, tab_words, tab_scales, offs, wa, wb_words, wb_scales,
+                                                wg_words, wg_scales, tab2_words, tab2_scales, offs2, bias, out):
+    nc = tc.nc
+    with ExitStack() as ctx:
+        keep = ctx.enter_context(tc.tile_pool(name="keep", bufs=1))
+        ring = ctx.enter_context(tc.tile_pool(name="ring", bufs=3))
+        psum = ctx.enter_context(tc.psum_pool(name="psum", bufs=8))
+
+        def bank(name):
+            return psum.tile([P, 512], F32, name=name, tag="bank")
+
+        idx = keep.tile([P, S // 16], U16, name="idx")
+        idx2 = keep.tile([P, S2 // 16], U16, name="idx2")
+        tab_plane = keep.tile([P, PASSES, T // 4], I32, name="tab_plane", tag="early_plane_then_wa", align_bytes=64)
+        w_plane = keep.tile([P, PASSES, H // 4], I32, name="w_plane", align_bytes=64)
+        tab2_plane = keep.tile([P, T2 // 4], I32, name="tab2_plane", tag="plane_then_words2", align_bytes=64)
+        tab_w = [keep.tile([P, T], I32, name="tab_w%d" % a, tag="words_then_wa%d" % a, align_bytes=64) for a in range(PASSES)]
+        wb_w = keep.tile([P, PASSES, H], I32, name="wb_w", align_bytes=64)
+        wg_w = keep.tile([P, PASSES, H // 2], I32, name="wg_w", align_bytes=64)
+        wa_bf = {}
+        wa_w = [keep.tile([P, H], U32, name="wa_w%d" % a, align_bytes=64) for a in range(PASSES)]
+        wa_s = [keep.tile([P, H], U8, name="wa_s%d" % a, align_bytes=64) for a in range(PASSES)]
+        bias_col = keep.tile([P, S2 // P], F32, name="bias_col")
+        ident = keep.tile([P, P], F32, name="ident", align_bytes=64)
+
+        nc.vector.memset(tab_plane[:], 0)
+        nc.gpsimd.memset(w_plane[:], 0)
+        nc.vector.memset(tab2_plane[:], 0)
+
+        def load_plane(queue, plane, row, scales):
+            for q in range(4):
+                queue.dma_start(out=plane[32 * q + row: 32 * q + row + 4, :, :],
+                                in_=scales[:, 4 * q: 4 * q + 4, :].bitcast(I32).rearrange("a r t -> r a t"))
+
+        def words(w):
+            return w.rearrange("p t i -> p (t i)").bitcast(I32)
+
+        nc.sync.dma_start(idx[:], offs)
+        load_plane(nc.sync, tab_plane, 0, tab_scales)
+        nc.sync.dma_start(idx2[:], offs2)
+        for a in range(PASSES):
+            nc.sync.dma_start(out=tab_w[a][:], in_=words(tab_words[a]))
+        nc.sync.dma_start(out=wg_w[:], in_=wg_words.bitcast(I32).rearrange("a p c -> p a c"))
+        nc.sync.dma_start(out=wb_w[:], in_=wb_words.rearrange("a p c i -> p a (c i)").bitcast(I32))
+        load_plane(nc.gpsimd, w_plane, 0, wg_scales)
+        load_plane(nc.gpsimd, w_plane, WB_ROW, wb_scales)
+        for q in range(4):
+            nc.sync.dma_start(out=tab2_plane[32 * q + V2_ROW: 32 * q + V2_ROW + 4, :],
+                              in_=tab2_scales[0, 4 * q: 4 * q + 4, :].bitcast(I32))
+        with nc.allow_non_contiguous_dma(reason="one bias value to a partition"):
+            nc.gpsimd.dma_start(out=bias_col[:], in_=bias.rearrange("(m p) -> p m", p=P))
+        make_identity(nc, ident[:])
+
+        late = {}
+
+        def load_wa():
+            late["wa"] = keep.tile([P, PASSES, 4, H], F32, name="wa_raw", tag="early_plane_then_wa", align_bytes=64)
+            for a in range(PASSES):
+                nc.sync.dma_start(out=late["wa"][:, a], in_=wa[512 * a: 512 * (a + 1), :].rearrange("(p i) c -> p i c", i=4))
+
+        def load_tab2():
+            late["tab2"] = keep.tile([P, T2], I32, name="tab2_w", tag="plane_then_words2", align_bytes=64)
+            nc.sync.dma_start(out=late["tab2"][:], in_=words(tab2_words[0]))
+
+        v_w, v_s = {}, {}
+
+        def gather_scales(s):
+            for a in range(PASSES):
+                v_s[s, a] = keep.tile([P, SLICE], U8, name="v_s%d_%d" % (s, a), align_bytes=64)
+                nc.vector.tensor_copy(v_s[s, a][:], tab_plane[:, a, :].bitcast(U8).indirect(idx[:, s * SLICE // 16: (s + 1) * SLICE // 16]))
+
+        def gather_words(s):
+            for a in range(PASSES):
+                v_w[s, a] = keep.tile([P, SLICE], U32, name="v_w%d_%d" % (s, a), align_bytes=64)
+                nc.vector.tensor_copy(v_w[s, a][:], tab_w[a][:].bitcast(U32).indirect(idx[:, s * SLICE // 16: (s + 1) * SLICE // 16]))
+
+        def project(u, acc, a, rhs, rhs_scale):
+            s, c = divmod(u * P, SLICE)
+            nc.tensor.matmul_mx(out=acc[:], lhsT=v_w[s, a][:, c: c + P].bitcast(FP8X4), lhsT_scale=v_s[s, a][:, c: c + P],
+                                rhs=rhs, rhs_scale=rhs_scale, start=(a == 0), stop=(a == PASSES - 1))
+
+        def by_pairs(acc):
+            return acc[:].rearrange("j (p u e) -> j u p e", u=2, e=2)
+
+        def pairs(t):
+            return t[:].rearrange("j (u p e) -> j u p e", u=2, e=2)
+
+        gate, b_part, b_acc = {}, {}, {}
+
+        def gate_stage(u):
+            z, b = bank("z"), bank("b")
+            for a in range(PASSES):
+                project(u, z, a, wg_w[:, a, :].bitcast(U8).bitcast(FP4X4), w_plane[:, a, :].bitcast(U8))
+                project(u, b, a, wb_w[:, a, :].bitcast(FP8X4), w_plane[WB_ROW:, a, :].bitcast(U8))
+            gate[u] = keep.tile([P, H], F32, name="gate%d" % u)
+            nc.scalar.activation(out=pairs(gate[u]), in_=by_pairs(z), func=ACT.Sigmoid)
+            b_acc[u] = b
+
+        def b_stage(u):
+            b = b_acc[u]
+            b_part[u] = keep.tile([P, H], F32, name="b_part%d" % u)
+            for w in range(2):
+                nc.vector.scalar_tensor_tensor(out=pairs(b_part[u])[:, w], in0=pairs(gate[u])[:, w], scalar=1.0,
+                                               in1=by_pairs(b)[:, w], op0=ALU.subtract, op1=ALU.mult)
+
+        def round_wa(a):
+            half = H // 2
+            wa_bf[a] = keep.tile([P, 4 * H], BF16, name="wa_bf%d" % a, tag="words_then_wa%d" % a, align_bytes=64)
+            dst = [wa_bf[a][:, 4 * half * c: 4 * half * (c + 1)].rearrange("p (c x i) -> p c i x", x=4, i=4) for c in range(2)]
+            src = [late["wa"][:, a, :, half * c: half * (c + 1)].rearrange("p i (c x) -> p c i x", x=4) for c in range(2)]
+            nc.scalar.copy(out=dst[0], in_=src[0])
+            nc.gpsimd.tensor_scalar(out=wa_bf[a][:, 4 * half:].rearrange("p (c i) -> p c i", i=4), in0=late["wa"][:, a, :, half:].rearrange("p i c -> p c i"), scalar1=1.0, scalar2=0.0, op0=ALU.mult, op1=ALU.add)
+
+        def quantise_wa(a):
+            nc.vector.quantize_mx(out=wa_w[a][:].bitcast(FP8X4), scales=wa_s[a][:], in_=wa_bf[a][:])
+
+        v2_s = keep.tile([P, S2], U8, name="v2_s", align_bytes=64)
+
+        h_rows = {}
+        add_engine = lambda u: nc.gpsimd if u < 6 else nc.vector
+
+        def blend_stage(u):
+            acc = bank("acc")
+            for a in range(PASSES):
+                project(u, acc, a, wa_w[a][:].bitcast(FP8X4), wa_s[a][:])
+            a_part = ring.tile([P, H], F32, name="a_part")
+            nc.vector.tensor_tensor(out=pairs(a_part), in0=by_pairs(acc), in1=pairs(gate[u]), op=ALU.mult)
+            h_rows[u] = ring.tile([P, H], BF16, name="h_rows", align_bytes=64, bufs=4)
+            add_engine(u).tensor_tensor(out=h_rows[u][:], in0=a_part[:], in1=b_part[u][:], op=ALU.subtract)
+
+        h_bf = {}
+
+        def turn_stage(us):
+            n = len(us) * P
+            turned = bank("turned")
+            for t, u in enumerate(us):
+                for w in range(2):
+                    nc.tensor.transpose(turned[:, (2 * t + w) * P: (2 * t + w + 1) * P],
+                                        h_rows[u][:].bitcast(F32)[:, w * P: (w + 1) * P], ident[:])
+            h_bf[us] = ring.tile([P, 4 * n], BF16, name="h_bf", align_bytes=64)
+            nc.scalar.copy(out=h_bf[us][:].bitcast(F32).rearrange("p (t j w) -> p t j w", j=P, w=2),
+                           in_=turned[:, 0: 2 * n].rearrange("p (t w j) -> p t j w", j=P, w=2))
+
+        def score_stage(us):
+            n = len(us) * P
+            h_w = ring.tile([P, n], U32, name="h_w", align_bytes=64)
+            h_s = ring.tile([P, n], U8, name="h_s", align_bytes=64)
+            nc.vector.quantize_mx(out=h_w[:].bitcast(FP8X4), scales=h_s[:], in_=h_bf[us][:])
+            logits = ring.tile([P, S2 // P, n], F32, name="logits")
+            per_bank = 512 // n
+            for m0 in range(0, S2 // P, per_bank):
+                y = bank("y")
+                for m in range(m0, m0 + per_bank):
+                    nc.tensor.matmul_mx(out=y[:, (m - m0) * n: (m - m0 + 1) * n],
+                                        lhsT=late["v2"][:, m * P: (m + 1) * P].bitcast(FP8X4), lhsT_scale=v2_s[V2_ROW:, m * P: (m + 1) * P],
+                                        rhs=h_w[:].bitcast(FP8X4), rhs_scale=h_s[:], start=True, stop=True)
+                for m in range(m0, m0 + per_bank):
+                    nc.scalar.activation(out=logits[:, m, :], in_=y[:, (m - m0) * n: (m - m0 + 1) * n], func=ACT.Identity,
+                                         bias=bias_col[:, m: m + 1])
+            j0 = us[0] * P
+            nc.sync.dma_start(out=out[:, j0: j0 + n].rearrange("(m p) j -> p m j", p=P), in_=logits[:])
+
+        for s in range(S // SLICE):
+            gather_scales(s)
+        load_wa()
+        gather_words(0)
+        gate_stage(0)
+        gate_stage(1)
+        gather_words(1)
+        gate_stage(2)
+        nc.vector.tensor_copy(v2_s[:], tab2_plane[:].bitcast(U8).indirect(idx2[:]))
+        load_tab2()
+        gather_words(2)
+        gather_words(3)
+        round_wa(0)
+        b_stage(0)
+        gate_stage(3)
+        b_stage(1)
+        gate_stage(4)
+        quantise_wa(0)
+        round_wa(1)
+        b_stage(2)
+        gate_stage(5)
+        b_stage(3)
+        quantise_wa(1)
+        b_stage(4)
+        blend_stage(0)
+        gate_stage(6)
+        b_stage(5)
+        blend_stage(1)
+        gate_stage(7)
+        late["v2"] = keep.tile([P, S2], U32, name="v2_w", tag="words_then_wa1", align_bytes=64)
+        nc.vector.tensor_copy(late["v2"][:], late["tab2"][:].bitcast(U32).indirect(idx2[:]))
+        blend_stage(2)
+        turn_stage((0, 1))
+        b_stage(6)
+        blend_stage(3)
+        b_stage(7)
+        blend_stage(4)
+        score_stage((0, 1))
+        turn_stage((2, 3))
+        blend_stage(5)
+        blend_stage(6)
+        score_stage((2, 3))
+        turn_stage((4, 5))
+        blend_stage(7)
+        turn_stage((6,))
+        score_stage((4, 5))
+        turn_stage((7,))
+        score_stage((6,))
+        score_stage((7,))

@@ -20,7 +20,6 @@ ACT = mybir.ActivationFunctionType
 P = 128
 PASSES = K // 512
 SLICE = 256
-UNITS = S // P
 WB_ROW = 4
 V2_ROW = 8
 
@@ -30,7 +29,7 @@ def tile_list_gated_link_logits_kernel(tc, tab_words, tab_scales, offs, wa, wb_w
     nc = tc.nc
     with ExitStack() as ctx:
         keep = ctx.enter_context(tc.tile_pool(name="keep", bufs=1))
-        ring = ctx.enter_context(tc.tile_pool(name="ring", bufs=3))
+        ring = ctx.enter_context(tc.tile_pool(name="ring", bufs=4))
         psum = ctx.enter_context(tc.psum_pool(name="psum", bufs=8))
 
         def bank(name):
@@ -38,21 +37,19 @@ def tile_list_gated_link_logits_kernel(tc, tab_words, tab_scales, offs, wa, wb_w
 
         idx = keep.tile([P, S // 16], U16, name="idx")
         idx2 = keep.tile([P, S2 // 16], U16, name="idx2")
-        tab_plane = keep.tile([P, PASSES, T // 4], I32, name="tab_plane", tag="early_plane_then_wa", align_bytes=64)
-        w_plane = keep.tile([P, PASSES, H // 4], I32, name="w_plane", align_bytes=64)
-        tab2_plane = keep.tile([P, T2 // 4], I32, name="tab2_plane", tag="plane_then_words2", align_bytes=64)
+        tab_plane = keep.tile([P, PASSES, T // 4], I32, name="tab_plane", tag="plane_then_v2_scales", align_bytes=64)
+        wg_plane = keep.tile([P, PASSES, H // 4], I32, name="wg_plane", align_bytes=64)
+        wb_plane = keep.tile([P, PASSES, H // 4], I32, name="wb_plane", align_bytes=64)
+        tab2_plane = keep.tile([P, 1, T2 // 4], I32, name="tab2_plane", align_bytes=64)
         tab_w = [keep.tile([P, T], I32, name="tab_w%d" % a, tag="words_then_wa%d" % a, align_bytes=64) for a in range(PASSES)]
+        tab2_w = keep.tile([P, T2], I32, name="tab2_w", align_bytes=64)
         wb_w = keep.tile([P, PASSES, H], I32, name="wb_w", align_bytes=64)
         wg_w = keep.tile([P, PASSES, H // 2], I32, name="wg_w", align_bytes=64)
-        wa_bf = {}
+        wa_raw = [keep.tile([P, 4, H], F32, name="wa_raw%d" % a, align_bytes=64) for a in range(PASSES)]
         wa_w = [keep.tile([P, H], U32, name="wa_w%d" % a, align_bytes=64) for a in range(PASSES)]
         wa_s = [keep.tile([P, H], U8, name="wa_s%d" % a, align_bytes=64) for a in range(PASSES)]
         bias_col = keep.tile([P, S2 // P], F32, name="bias_col")
         ident = keep.tile([P, P], F32, name="ident", align_bytes=64)
-
-        nc.vector.memset(tab_plane[:], 0)
-        nc.gpsimd.memset(w_plane[:], 0)
-        nc.vector.memset(tab2_plane[:], 0)
 
         def load_plane(queue, plane, row, scales):
             for q in range(4):
@@ -62,177 +59,264 @@ def tile_list_gated_link_logits_kernel(tc, tab_words, tab_scales, offs, wa, wb_w
         def words(w):
             return w.rearrange("p t i -> p (t i)").bitcast(I32)
 
+        nc.vector.memset(tab_plane[:], 0)
+        nc.gpsimd.memset(wg_plane[:], 0)
+        nc.gpsimd.memset(wb_plane[:], 0)
+        nc.vector.memset(tab2_plane[:], 0)
         nc.sync.dma_start(idx[:], offs)
-        load_plane(nc.sync, tab_plane, 0, tab_scales)
         nc.sync.dma_start(idx2[:], offs2)
+        load_plane(nc.scalar, tab_plane, 0, tab_scales)
         for a in range(PASSES):
             nc.sync.dma_start(out=tab_w[a][:], in_=words(tab_words[a]))
         nc.sync.dma_start(out=wg_w[:], in_=wg_words.bitcast(I32).rearrange("a p c -> p a c"))
         nc.sync.dma_start(out=wb_w[:], in_=wb_words.rearrange("a p c i -> p a (c i)").bitcast(I32))
-        load_plane(nc.gpsimd, w_plane, 0, wg_scales)
-        load_plane(nc.gpsimd, w_plane, WB_ROW, wb_scales)
-        for q in range(4):
-            nc.sync.dma_start(out=tab2_plane[32 * q + V2_ROW: 32 * q + V2_ROW + 4, :],
-                              in_=tab2_scales[0, 4 * q: 4 * q + 4, :].bitcast(I32))
+        load_plane(nc.gpsimd, wg_plane, 0, wg_scales)
+        load_plane(nc.gpsimd, wb_plane, WB_ROW, wb_scales)
+        load_plane(nc.sync, tab2_plane, V2_ROW, tab2_scales)
+        for a in range(PASSES):
+            nc.gpsimd.dma_start(out=wa_raw[a][:], in_=wa[512 * a: 512 * (a + 1), :].rearrange("(p i) c -> p i c", i=4))
+        nc.gpsimd.dma_start(out=tab2_w[:], in_=words(tab2_words[0]))
         with nc.allow_non_contiguous_dma(reason="one bias value to a partition"):
             nc.gpsimd.dma_start(out=bias_col[:], in_=bias.rearrange("(m p) -> p m", p=P))
         make_identity(nc, ident[:])
 
-        late = {}
+        v_w, v_s, acc, gate, a_part, b_part, wa_bf, v2, h_rows, turned, h_bf, h_w, h_s, y, logits = [{} for n in range(15)]
+        half = H // 2
 
-        def load_wa():
-            late["wa"] = keep.tile([P, PASSES, 4, H], F32, name="wa_raw", tag="early_plane_then_wa", align_bytes=64)
-            for a in range(PASSES):
-                nc.sync.dma_start(out=late["wa"][:, a], in_=wa[512 * a: 512 * (a + 1), :].rearrange("(p i) c -> p i c", i=4))
+        def offsets(s):
+            return idx[:, s * SLICE // 16: (s + 1) * SLICE // 16]
 
-        def load_tab2():
-            late["tab2"] = keep.tile([P, T2], I32, name="tab2_w", tag="plane_then_words2", align_bytes=64)
-            nc.sync.dma_start(out=late["tab2"][:], in_=words(tab2_words[0]))
+        def gather_scales(s, a):
+            v_s[s, a] = keep.tile([P, SLICE], U8, name="v_s%d_%d" % (s, a), align_bytes=64)
+            nc.vector.tensor_copy(v_s[s, a][:], tab_plane[:, a, :].bitcast(U8).indirect(offsets(s)))
 
-        v_w, v_s = {}, {}
+        def gather_words(s, a):
+            v_w[s, a] = keep.tile([P, SLICE], U32, name="v_w%d_%d" % (s, a), align_bytes=64)
+            nc.vector.tensor_copy(v_w[s, a][:], tab_w[a][:].bitcast(U32).indirect(offsets(s)))
 
-        def gather_scales(s):
-            for a in range(PASSES):
-                v_s[s, a] = keep.tile([P, SLICE], U8, name="v_s%d_%d" % (s, a), align_bytes=64)
-                nc.vector.tensor_copy(v_s[s, a][:], tab_plane[:, a, :].bitcast(U8).indirect(idx[:, s * SLICE // 16: (s + 1) * SLICE // 16]))
+        def gather_v2_scales():
+            v2["s"] = keep.tile([P, S2], U8, name="v2_s", tag="plane_then_v2_scales", align_bytes=64)
+            nc.vector.tensor_copy(v2["s"][:], tab2_plane[:, 0, :].bitcast(U8).indirect(idx2[:]))
 
-        def gather_words(s):
-            for a in range(PASSES):
-                v_w[s, a] = keep.tile([P, SLICE], U32, name="v_w%d_%d" % (s, a), align_bytes=64)
-                nc.vector.tensor_copy(v_w[s, a][:], tab_w[a][:].bitcast(U32).indirect(idx[:, s * SLICE // 16: (s + 1) * SLICE // 16]))
+        def gather_v2_words():
+            v2["w"] = keep.tile([P, S2], U32, name="v2_w", tag="words_then_wa1", align_bytes=64)
+            nc.vector.tensor_copy(v2["w"][:], tab2_w[:].bitcast(U32).indirect(idx2[:]))
 
-        def project(u, acc, a, rhs, rhs_scale):
+        def weight(kind, a):
+            if kind == "z":
+                return wg_w[:, a, :].bitcast(U8).bitcast(FP4X4), wg_plane[:, a, :].bitcast(U8)
+            if kind == "b":
+                return wb_w[:, a, :].bitcast(FP8X4), wb_plane[WB_ROW:, a, :].bitcast(U8)
+            return wa_w[a][:].bitcast(FP8X4), wa_s[a][:]
+
+        def product(kind, u):
             s, c = divmod(u * P, SLICE)
-            nc.tensor.matmul_mx(out=acc[:], lhsT=v_w[s, a][:, c: c + P].bitcast(FP8X4), lhsT_scale=v_s[s, a][:, c: c + P],
-                                rhs=rhs, rhs_scale=rhs_scale, start=(a == 0), stop=(a == PASSES - 1))
+            acc[kind, u] = bank(kind)
+            for a in range(PASSES):
+                rhs, rhs_scale = weight(kind, a)
+                nc.tensor.matmul_mx(out=acc[kind, u][:], lhsT=v_w[s, a][:, c: c + P].bitcast(FP8X4),
+                                    lhsT_scale=v_s[s, a][:, c: c + P], rhs=rhs, rhs_scale=rhs_scale,
+                                    start=(a == 0), stop=(a == PASSES - 1))
 
-        def by_pairs(acc):
-            return acc[:].rearrange("j (p u e) -> j u p e", u=2, e=2)
+        def by_pairs(t):
+            return t[:].rearrange("j (p w e) -> j w p e", w=2, e=2)
 
         def pairs(t):
-            return t[:].rearrange("j (u p e) -> j u p e", u=2, e=2)
+            return t[:].rearrange("j (w p e) -> j w p e", w=2, e=2)
 
-        gate, b_part, b_acc = {}, {}, {}
-
-        def gate_stage(u):
-            z, b = bank("z"), bank("b")
-            for a in range(PASSES):
-                project(u, z, a, wg_w[:, a, :].bitcast(U8).bitcast(FP4X4), w_plane[:, a, :].bitcast(U8))
-                project(u, b, a, wb_w[:, a, :].bitcast(FP8X4), w_plane[WB_ROW:, a, :].bitcast(U8))
+        def sigmoid(u):
             gate[u] = keep.tile([P, H], F32, name="gate%d" % u)
-            nc.scalar.activation(out=pairs(gate[u]), in_=by_pairs(z), func=ACT.Sigmoid)
-            b_acc[u] = b
+            nc.scalar.activation(out=pairs(gate[u]), in_=by_pairs(acc["z", u]), func=ACT.Sigmoid)
 
-        def b_stage(u):
-            b = b_acc[u]
-            b_part[u] = keep.tile([P, H], F32, name="b_part%d" % u)
+        def b_term(u):
+            b_part[u] = ring.tile([P, H], F32, name="b_part")
             for w in range(2):
                 nc.vector.scalar_tensor_tensor(out=pairs(b_part[u])[:, w], in0=pairs(gate[u])[:, w], scalar=1.0,
-                                               in1=by_pairs(b)[:, w], op0=ALU.subtract, op1=ALU.mult)
+                                               in1=by_pairs(acc["b", u])[:, w], op0=ALU.subtract, op1=ALU.mult)
 
-        def round_wa(a):
-            half = H // 2
+        def a_term(u):
+            a_part[u] = ring.tile([P, H], F32, name="a_part")
+            nc.vector.tensor_tensor(out=pairs(a_part[u]), in0=by_pairs(acc["a", u]), in1=pairs(gate[u]), op=ALU.mult)
+
+        def blend(u, engine):
+            h_rows[u] = ring.tile([P, H], BF16, name="h_rows", align_bytes=64)
+            engine.tensor_tensor(out=h_rows[u][:], in0=a_part[u][:], in1=b_part[u][:], op=ALU.subtract)
+
+        def round_wa_left(a):
             wa_bf[a] = keep.tile([P, 4 * H], BF16, name="wa_bf%d" % a, tag="words_then_wa%d" % a, align_bytes=64)
-            dst = [wa_bf[a][:, 4 * half * c: 4 * half * (c + 1)].rearrange("p (c x i) -> p c i x", x=4, i=4) for c in range(2)]
-            src = [late["wa"][:, a, :, half * c: half * (c + 1)].rearrange("p i (c x) -> p c i x", x=4) for c in range(2)]
-            nc.scalar.copy(out=dst[0], in_=src[0])
-            nc.gpsimd.tensor_scalar(out=wa_bf[a][:, 4 * half:].rearrange("p (c i) -> p c i", i=4), in0=late["wa"][:, a, :, half:].rearrange("p i c -> p c i"), scalar1=1.0, scalar2=0.0, op0=ALU.mult, op1=ALU.add)
+            nc.scalar.copy(out=wa_bf[a][:, : 4 * half].rearrange("p (c x i) -> p c i x", x=4, i=4),
+                           in_=wa_raw[a][:, :, :half].rearrange("p i (c x) -> p c i x", x=4))
+
+        def round_wa_right(a):
+            nc.gpsimd.tensor_scalar(out=wa_bf[a][:, 4 * half:].rearrange("p (c i) -> p c i", i=4),
+                                    in0=wa_raw[a][:, :, half:].rearrange("p i c -> p c i"),
+                                    scalar1=1.0, scalar2=0.0, op0=ALU.mult, op1=ALU.add)
 
         def quantise_wa(a):
             nc.vector.quantize_mx(out=wa_w[a][:].bitcast(FP8X4), scales=wa_s[a][:], in_=wa_bf[a][:])
 
-        v2_s = keep.tile([P, S2], U8, name="v2_s", align_bytes=64)
-
-        h_rows = {}
-        add_engine = lambda u: nc.gpsimd if u < 6 else nc.vector
-
-        def blend_stage(u):
-            acc = bank("acc")
-            for a in range(PASSES):
-                project(u, acc, a, wa_w[a][:].bitcast(FP8X4), wa_s[a][:])
-            a_part = ring.tile([P, H], F32, name="a_part")
-            nc.vector.tensor_tensor(out=pairs(a_part), in0=by_pairs(acc), in1=pairs(gate[u]), op=ALU.mult)
-            h_rows[u] = ring.tile([P, H], BF16, name="h_rows", align_bytes=64, bufs=4)
-            add_engine(u).tensor_tensor(out=h_rows[u][:], in0=a_part[:], in1=b_part[u][:], op=ALU.subtract)
-
-        h_bf = {}
-
-        def turn_stage(us):
-            n = len(us) * P
-            turned = bank("turned")
+        def turn(us):
+            turned[us] = bank("turned")
             for t, u in enumerate(us):
                 for w in range(2):
-                    nc.tensor.transpose(turned[:, (2 * t + w) * P: (2 * t + w + 1) * P],
+                    nc.tensor.transpose(turned[us][:, (2 * t + w) * P: (2 * t + w + 1) * P],
                                         h_rows[u][:].bitcast(F32)[:, w * P: (w + 1) * P], ident[:])
+
+        def interleave(us):
+            n = len(us) * P
             h_bf[us] = ring.tile([P, 4 * n], BF16, name="h_bf", align_bytes=64)
             nc.scalar.copy(out=h_bf[us][:].bitcast(F32).rearrange("p (t j w) -> p t j w", j=P, w=2),
-                           in_=turned[:, 0: 2 * n].rearrange("p (t w j) -> p t j w", j=P, w=2))
+                           in_=turned[us][:, 0: 2 * n].rearrange("p (t w j) -> p t j w", j=P, w=2))
 
-        def score_stage(us):
+        def quantise_h(us):
             n = len(us) * P
-            h_w = ring.tile([P, n], U32, name="h_w", align_bytes=64)
-            h_s = ring.tile([P, n], U8, name="h_s", align_bytes=64)
-            nc.vector.quantize_mx(out=h_w[:].bitcast(FP8X4), scales=h_s[:], in_=h_bf[us][:])
-            logits = ring.tile([P, S2 // P, n], F32, name="logits")
-            per_bank = 512 // n
-            for m0 in range(0, S2 // P, per_bank):
-                y = bank("y")
-                for m in range(m0, m0 + per_bank):
-                    nc.tensor.matmul_mx(out=y[:, (m - m0) * n: (m - m0 + 1) * n],
-                                        lhsT=late["v2"][:, m * P: (m + 1) * P].bitcast(FP8X4), lhsT_scale=v2_s[V2_ROW:, m * P: (m + 1) * P],
-                                        rhs=h_w[:].bitcast(FP8X4), rhs_scale=h_s[:], start=True, stop=True)
-                for m in range(m0, m0 + per_bank):
-                    nc.scalar.activation(out=logits[:, m, :], in_=y[:, (m - m0) * n: (m - m0 + 1) * n], func=ACT.Identity,
-                                         bias=bias_col[:, m: m + 1])
-            j0 = us[0] * P
-            nc.sync.dma_start(out=out[:, j0: j0 + n].rearrange("(m p) j -> p m j", p=P), in_=logits[:])
+            h_w[us] = ring.tile([P, n], U32, name="h_w", align_bytes=64)
+            h_s[us] = ring.tile([P, n], U8, name="h_s", align_bytes=64)
+            nc.vector.quantize_mx(out=h_w[us][:].bitcast(FP8X4), scales=h_s[us][:], in_=h_bf[us][:])
+            logits[us] = ring.tile([P, S2 // P, n], F32, name="logits")
 
-        for s in range(S // SLICE):
-            gather_scales(s)
-        load_wa()
-        gather_words(0)
-        gate_stage(0)
-        gate_stage(1)
-        gather_words(1)
-        gate_stage(2)
-        nc.vector.tensor_copy(v2_s[:], tab2_plane[:].bitcast(U8).indirect(idx2[:]))
-        load_tab2()
-        gather_words(2)
-        gather_words(3)
-        round_wa(0)
-        b_stage(0)
-        gate_stage(3)
-        b_stage(1)
-        gate_stage(4)
+        def score(us, i):
+            n = len(us) * P
+            y[us, i] = bank("y")
+            for t in range(2):
+                m = 2 * i + t
+                nc.tensor.matmul_mx(out=y[us, i][:, t * n: (t + 1) * n],
+                                    lhsT=v2["w"][:, m * P: (m + 1) * P].bitcast(FP8X4),
+                                    lhsT_scale=v2["s"][V2_ROW:, m * P: (m + 1) * P],
+                                    rhs=h_w[us][:].bitcast(FP8X4), rhs_scale=h_s[us][:], start=True, stop=True)
+
+        def add_bias(us, i, on_vector):
+            n = len(us) * P
+            for t in range(2):
+                m = 2 * i + t
+                src = y[us, i][:, t * n: (t + 1) * n]
+                if on_vector:
+                    nc.vector.tensor_scalar(out=logits[us][:, m, :], in0=src, scalar1=bias_col[:, m: m + 1], scalar2=None, op0=ALU.add)
+                else:
+                    nc.scalar.activation(out=logits[us][:, m, :], in_=src, func=ACT.Identity, bias=bias_col[:, m: m + 1])
+
+        def store(us):
+            n = len(us) * P
+            j0 = us[0] * P
+            nc.sync.dma_start(out=out[:, j0: j0 + n].rearrange("(m p) j -> p m j", p=P), in_=logits[us][:])
+
+        gather_scales(0, 0)
+        gather_scales(0, 1)
+        gather_scales(1, 0)
+        gather_scales(1, 1)
+        gather_words(0, 0)
+        gather_words(0, 1)
+        product("z", 0)
+        product("z", 1)
+        product("b", 0)
+        product("b", 1)
+        sigmoid(0)
+        sigmoid(1)
+        gather_words(1, 0)
+        gather_words(1, 1)
+        gather_scales(2, 0)
+        gather_scales(2, 1)
+        product("z", 2)
+        product("z", 3)
+        product("b", 2)
+        product("b", 3)
+        gather_words(2, 0)
+        gather_words(3, 0)
+        round_wa_left(0)
+        round_wa_right(0)
+        gather_words(2, 1)
+        gather_words(3, 1)
+        round_wa_left(1)
+        round_wa_right(1)
+        gather_scales(3, 0)
+        gather_scales(3, 1)
+        product("z", 4)
+        product("z", 5)
+        sigmoid(2)
+        sigmoid(3)
         quantise_wa(0)
-        round_wa(1)
-        b_stage(2)
-        gate_stage(5)
-        b_stage(3)
+        b_term(0)
         quantise_wa(1)
-        b_stage(4)
-        blend_stage(0)
-        gate_stage(6)
-        b_stage(5)
-        blend_stage(1)
-        gate_stage(7)
-        late["v2"] = keep.tile([P, S2], U32, name="v2_w", tag="words_then_wa1", align_bytes=64)
-        nc.vector.tensor_copy(late["v2"][:], late["tab2"][:].bitcast(U32).indirect(idx2[:]))
-        blend_stage(2)
-        turn_stage((0, 1))
-        b_stage(6)
-        blend_stage(3)
-        b_stage(7)
-        blend_stage(4)
-        score_stage((0, 1))
-        turn_stage((2, 3))
-        blend_stage(5)
-        blend_stage(6)
-        score_stage((2, 3))
-        turn_stage((4, 5))
-        blend_stage(7)
-        turn_stage((6,))
-        score_stage((4, 5))
-        turn_stage((7,))
-        score_stage((6,))
-        score_stage((7,))
+        sigmoid(4)
+        sigmoid(5)
+        gather_v2_scales()
+        product("a", 0)
+        product("a", 1)
+        a_term(0)
+        blend(0, nc.gpsimd)
+        product("a", 2)
+        b_term(1)
+        a_term(1)
+        blend(1, nc.gpsimd)
+        product("a", 3)
+        product("b", 4)
+        b_term(2)
+        a_term(2)
+        blend(2, nc.gpsimd)
+        product("a", 4)
+        product("z", 6)
+        b_term(3)
+        a_term(3)
+        blend(3, nc.gpsimd)
+        product("b", 5)
+        product("a", 5)
+        sigmoid(6)
+        turn((0, 1))
+        interleave((0, 1))
+        b_term(4)
+        a_term(4)
+        blend(4, nc.gpsimd)
+        product("z", 7)
+        product("b", 6)
+        sigmoid(7)
+        product("a", 6)
+        b_term(5)
+        a_term(5)
+        blend(5, nc.gpsimd)
+        quantise_h((0, 1))
+        gather_v2_words()
+        turn((2, 3))
+        interleave((2, 3))
+        product("b", 7)
+        product("a", 7)
+        score((0, 1), 0)
+        score((0, 1), 1)
+        b_term(6)
+        a_term(6)
+        blend(6, nc.gpsimd)
+        add_bias((0, 1), 0, False)
+        add_bias((0, 1), 1, False)
+        store((0, 1))
+        quantise_h((2, 3))
+        turn((4, 5))
+        interleave((4, 5))
+        score((2, 3), 0)
+        score((2, 3), 1)
+        b_term(7)
+        a_term(7)
+        add_bias((2, 3), 0, False)
+        quantise_h((4, 5))
+        blend(7, nc.vector)
+        add_bias((2, 3), 1, False)
+        store((2, 3))
+        turn((6,))
+        interleave((6,))
+        score((4, 5), 0)
+        score((4, 5), 1)
+        turn((7,))
+        add_bias((4, 5), 0, False)
+        quantise_h((6,))
+        add_bias((4, 5), 1, True)
+        store((4, 5))
+        interleave((7,))
+        score((6,), 0)
+        score((6,), 1)
+        quantise_h((7,))
+        add_bias((6,), 0, False)
+        add_bias((6,), 1, True)
+        store((6,))
+        score((7,), 0)
+        score((7,), 1)
+        add_bias((7,), 0, False)
+        add_bias((7,), 1, True)
+        store((7,))

@@ -37,18 +37,14 @@ def tile_list_gated_link_logits_kernel(tc, tab_words, tab_scales, offs, wa, wb_w
 
         idx = keep.tile([P, S // 16], U16, name="idx")
         idx2 = keep.tile([P, S2 // 16], U16, name="idx2")
-        tab_plane = keep.tile([P, PASSES, T // 4], I32, name="tab_plane", tag="plane_then_v2_scales", align_bytes=64)
+        tab_plane = keep.tile([P, PASSES, T // 4], I32, name="tab_plane", tag="plane_then_plane2", align_bytes=64)
         wg_plane = keep.tile([P, PASSES, H // 4], I32, name="wg_plane", align_bytes=64)
         wb_plane = keep.tile([P, PASSES, H // 4], I32, name="wb_plane", align_bytes=64)
-        tab2_plane = keep.tile([P, 1, T2 // 4], I32, name="tab2_plane", align_bytes=64)
-        tab_w = [keep.tile([P, T], I32, name="tab_w%d" % a, tag="words_then_wa%d" % a, align_bytes=64) for a in range(PASSES)]
-        tab2_w = keep.tile([P, T2], I32, name="tab2_w", align_bytes=64)
+        tab_w = [keep.tile([P, T], I32, name="tab_w%d" % a, tag=("words0_then_wa_then_bias", "words1_then_words2")[a], align_bytes=64) for a in range(PASSES)]
         wb_w = keep.tile([P, PASSES, H], I32, name="wb_w", align_bytes=64)
         wg_w = keep.tile([P, PASSES, H // 2], I32, name="wg_w", align_bytes=64)
-        wa_raw = [keep.tile([P, 4, H], F32, name="wa_raw%d" % a, align_bytes=64) for a in range(PASSES)]
         wa_w = [keep.tile([P, H], U32, name="wa_w%d" % a, align_bytes=64) for a in range(PASSES)]
         wa_s = [keep.tile([P, H], U8, name="wa_s%d" % a, align_bytes=64) for a in range(PASSES)]
-        bias_col = keep.tile([P, S2 // P], F32, name="bias_col")
         ident = keep.tile([P, P], F32, name="ident", align_bytes=64)
 
         def load_plane(queue, plane, row, scales):
@@ -61,8 +57,7 @@ def tile_list_gated_link_logits_kernel(tc, tab_words, tab_scales, offs, wa, wb_w
 
         nc.vector.memset(tab_plane[:], 0)
         nc.gpsimd.memset(wg_plane[:], 0)
-        nc.gpsimd.memset(wb_plane[:], 0)
-        nc.vector.memset(tab2_plane[:], 0)
+        nc.vector.memset(wb_plane[:], 0)
         nc.sync.dma_start(idx[:], offs)
         nc.sync.dma_start(idx2[:], offs2)
         load_plane(nc.scalar, tab_plane, 0, tab_scales)
@@ -71,14 +66,30 @@ def tile_list_gated_link_logits_kernel(tc, tab_words, tab_scales, offs, wa, wb_w
         nc.sync.dma_start(out=wg_w[:], in_=wg_words.bitcast(I32).rearrange("a p c -> p a c"))
         nc.sync.dma_start(out=wb_w[:], in_=wb_words.rearrange("a p c i -> p a (c i)").bitcast(I32))
         load_plane(nc.gpsimd, wg_plane, 0, wg_scales)
-        load_plane(nc.gpsimd, wb_plane, WB_ROW, wb_scales)
-        load_plane(nc.sync, tab2_plane, V2_ROW, tab2_scales)
-        for a in range(PASSES):
-            nc.gpsimd.dma_start(out=wa_raw[a][:], in_=wa[512 * a: 512 * (a + 1), :].rearrange("(p i) c -> p i c", i=4))
-        nc.gpsimd.dma_start(out=tab2_w[:], in_=words(tab2_words[0]))
-        with nc.allow_non_contiguous_dma(reason="one bias value to a partition"):
-            nc.gpsimd.dma_start(out=bias_col[:], in_=bias.rearrange("(m p) -> p m", p=P))
+        load_plane(nc.scalar, wb_plane, WB_ROW, wb_scales)
         make_identity(nc, ident[:])
+        late = {}
+
+        def load_wa():
+            late["wa"] = keep.tile([P, PASSES, 4, H], F32, name="wa_raw", tag="words0_then_wa_then_bias", align_bytes=64)
+            for a in range(PASSES):
+                for c in range(2):
+                    cols = slice(c * H // 2, (c + 1) * H // 2)
+                    nc.sync.dma_start(out=late["wa"][:, a, :, cols], in_=wa[512 * a: 512 * (a + 1), cols].rearrange("(p i) c -> p i c", i=4))
+
+        def load_tab2_plane():
+            late["plane2"] = keep.tile([P, 1, T2 // 4], I32, name="tab2_plane", tag="plane_then_plane2", align_bytes=64)
+            nc.gpsimd.memset(late["plane2"][:], 0)
+            load_plane(nc.sync, late["plane2"], V2_ROW, tab2_scales)
+
+        def load_tab2_words():
+            late["words2"] = keep.tile([P, T2], I32, name="tab2_w", tag="words1_then_words2", align_bytes=64)
+            nc.sync.dma_start(out=late["words2"][:], in_=words(tab2_words[0]))
+
+        def load_bias():
+            late["bias"] = keep.tile([P, S2 // P], F32, name="bias_col", tag="words0_then_wa_then_bias", align_bytes=64)
+            with nc.allow_non_contiguous_dma(reason="one bias value to a partition"):
+                nc.sync.dma_start(out=late["bias"][:], in_=bias.rearrange("(m p) -> p m", p=P))
 
         v_w, v_s, acc, gate, a_part, b_part, wa_bf, v2, h_rows, turned, h_bf, h_w, h_s, y, logits = [{} for n in range(15)]
         half = H // 2
@@ -95,12 +106,12 @@ def tile_list_gated_link_logits_kernel(tc, tab_words, tab_scales, offs, wa, wb_w
             nc.vector.tensor_copy(v_w[s, a][:], tab_w[a][:].bitcast(U32).indirect(offsets(s)))
 
         def gather_v2_scales():
-            v2["s"] = keep.tile([P, S2], U8, name="v2_s", tag="plane_then_v2_scales", align_bytes=64)
-            nc.vector.tensor_copy(v2["s"][:], tab2_plane[:, 0, :].bitcast(U8).indirect(idx2[:]))
+            v2["s"] = keep.tile([P, S2], U8, name="v2_s", align_bytes=64)
+            nc.vector.tensor_copy(v2["s"][:], late["plane2"][:, 0, :].bitcast(U8).indirect(idx2[:]))
 
         def gather_v2_words():
-            v2["w"] = keep.tile([P, S2], U32, name="v2_w", tag="words_then_wa1", align_bytes=64)
-            nc.vector.tensor_copy(v2["w"][:], tab2_w[:].bitcast(U32).indirect(idx2[:]))
+            v2["w"] = keep.tile([P, S2], U32, name="v2_w", tag="wa_bf1", align_bytes=64)
+            nc.vector.tensor_copy(v2["w"][:], late["words2"][:].bitcast(U32).indirect(idx2[:]))
 
         def weight(kind, a):
             if kind == "z":
@@ -109,10 +120,11 @@ def tile_list_gated_link_logits_kernel(tc, tab_words, tab_scales, offs, wa, wb_w
                 return wb_w[:, a, :].bitcast(FP8X4), wb_plane[WB_ROW:, a, :].bitcast(U8)
             return wa_w[a][:].bitcast(FP8X4), wa_s[a][:]
 
-        def product(kind, u):
+        def product(kind, u, passes):
             s, c = divmod(u * P, SLICE)
-            acc[kind, u] = bank(kind)
-            for a in range(PASSES):
+            if 0 in passes:
+                acc[kind, u] = bank(kind)
+            for a in passes:
                 rhs, rhs_scale = weight(kind, a)
                 nc.tensor.matmul_mx(out=acc[kind, u][:], lhsT=v_w[s, a][:, c: c + P].bitcast(FP8X4),
                                     lhsT_scale=v_s[s, a][:, c: c + P], rhs=rhs, rhs_scale=rhs_scale,
@@ -143,14 +155,13 @@ def tile_list_gated_link_logits_kernel(tc, tab_words, tab_scales, offs, wa, wb_w
             engine.tensor_tensor(out=h_rows[u][:], in0=a_part[u][:], in1=b_part[u][:], op=ALU.subtract)
 
         def round_wa_left(a):
-            wa_bf[a] = keep.tile([P, 4 * H], BF16, name="wa_bf%d" % a, tag="words_then_wa%d" % a, align_bytes=64)
+            wa_bf[a] = keep.tile([P, 4 * H], BF16, name="wa_bf%d" % a, tag="wa_bf%d" % a, align_bytes=64)
             nc.scalar.copy(out=wa_bf[a][:, : 4 * half].rearrange("p (c x i) -> p c i x", x=4, i=4),
-                           in_=wa_raw[a][:, :, :half].rearrange("p i (c x) -> p c i x", x=4))
+                           in_=late["wa"][:, a, :, :half].rearrange("p i (c x) -> p c i x", x=4))
 
         def round_wa_right(a):
-            nc.gpsimd.tensor_scalar(out=wa_bf[a][:, 4 * half:].rearrange("p (c i) -> p c i", i=4),
-                                    in0=wa_raw[a][:, :, half:].rearrange("p i c -> p c i"),
-                                    scalar1=1.0, scalar2=0.0, op0=ALU.mult, op1=ALU.add)
+            nc.scalar.copy(out=wa_bf[a][:, 4 * half:].rearrange("p (c x i) -> p c i x", x=4, i=4),
+                           in_=late["wa"][:, a, :, half:].rearrange("p i (c x) -> p c i x", x=4))
 
         def quantise_wa(a):
             nc.vector.quantize_mx(out=wa_w[a][:].bitcast(FP8X4), scales=wa_s[a][:], in_=wa_bf[a][:])
@@ -191,9 +202,9 @@ def tile_list_gated_link_logits_kernel(tc, tab_words, tab_scales, offs, wa, wb_w
                 m = 2 * i + t
                 src = y[us, i][:, t * n: (t + 1) * n]
                 if on_vector:
-                    nc.vector.tensor_scalar(out=logits[us][:, m, :], in0=src, scalar1=bias_col[:, m: m + 1], scalar2=None, op0=ALU.add)
+                    nc.vector.tensor_scalar(out=logits[us][:, m, :], in0=src, scalar1=late["bias"][:, m: m + 1], scalar2=None, op0=ALU.add)
                 else:
-                    nc.scalar.activation(out=logits[us][:, m, :], in_=src, func=ACT.Identity, bias=bias_col[:, m: m + 1])
+                    nc.scalar.activation(out=logits[us][:, m, :], in_=src, func=ACT.Identity, bias=late["bias"][:, m: m + 1])
 
         def store(us):
             n = len(us) * P
@@ -201,75 +212,86 @@ def tile_list_gated_link_logits_kernel(tc, tab_words, tab_scales, offs, wa, wb_w
             nc.sync.dma_start(out=out[:, j0: j0 + n].rearrange("(m p) j -> p m j", p=P), in_=logits[us][:])
 
         gather_scales(0, 0)
-        gather_scales(0, 1)
-        gather_scales(1, 0)
-        gather_scales(1, 1)
         gather_words(0, 0)
-        gather_words(0, 1)
-        product("z", 0)
-        product("z", 1)
-        product("b", 0)
-        product("b", 1)
-        sigmoid(0)
-        sigmoid(1)
         gather_words(1, 0)
-        gather_words(1, 1)
-        gather_scales(2, 0)
-        gather_scales(2, 1)
-        product("z", 2)
-        product("z", 3)
-        product("b", 2)
-        product("b", 3)
         gather_words(2, 0)
         gather_words(3, 0)
+        load_wa()
+        gather_words(0, 1)
+        gather_scales(0, 1)
+        product("z", 0, (0,))
+        product("z", 1, (0,))
+        product("z", 0, (1,))
+        product("z", 1, (1,))
+        gather_scales(1, 0)
+        gather_words(1, 1)
+        gather_scales(1, 1)
+        sigmoid(0)
+        sigmoid(1)
+        product("z", 2, (0,))
+        product("b", 0, (0, 1))
+        product("b", 1, (0, 1))
+        product("z", 3, (0,))
+        product("z", 2, (1,))
+        product("z", 3, (1,))
+        gather_scales(2, 0)
+        gather_scales(2, 1)
+        gather_words(2, 1)
         round_wa_left(0)
         round_wa_right(0)
-        gather_words(2, 1)
-        gather_words(3, 1)
         round_wa_left(1)
         round_wa_right(1)
+        load_bias()
+        product("b", 2, (0, 1))
+        product("b", 3, (0, 1))
+        gather_words(3, 1)
+        load_tab2_words()
         gather_scales(3, 0)
         gather_scales(3, 1)
-        product("z", 4)
-        product("z", 5)
+        load_tab2_plane()
+        product("z", 4, (0,))
+        product("z", 4, (1,))
+        product("z", 5, (0,))
+        product("z", 5, (1,))
+        b_term(0)
+        b_term(1)
+        quantise_wa(0)
+        quantise_wa(1)
         sigmoid(2)
         sigmoid(3)
-        quantise_wa(0)
-        b_term(0)
-        quantise_wa(1)
         sigmoid(4)
         sigmoid(5)
-        gather_v2_scales()
-        product("a", 0)
-        product("a", 1)
+        product("a", 0, (0, 1))
+        product("a", 1, (0, 1))
+        b_term(2)
+        b_term(3)
         a_term(0)
         blend(0, nc.gpsimd)
-        product("a", 2)
-        b_term(1)
+        product("a", 2, (0, 1))
         a_term(1)
         blend(1, nc.gpsimd)
-        product("a", 3)
-        product("b", 4)
-        b_term(2)
+        product("a", 3, (0, 1))
+        gather_v2_scales()
+        product("b", 4, (0, 1))
+        product("a", 4, (0, 1))
         a_term(2)
         blend(2, nc.gpsimd)
-        product("a", 4)
-        product("z", 6)
-        b_term(3)
+        product("b", 5, (0, 1))
+        product("z", 6, (0,))
+        product("z", 6, (1,))
         a_term(3)
         blend(3, nc.gpsimd)
-        product("b", 5)
-        product("a", 5)
-        sigmoid(6)
+        product("a", 5, (0, 1))
         turn((0, 1))
         interleave((0, 1))
+        sigmoid(6)
         b_term(4)
         a_term(4)
         blend(4, nc.gpsimd)
-        product("z", 7)
-        product("b", 6)
-        sigmoid(7)
-        product("a", 6)
+        product("z", 7, (0,))
+        product("z", 7, (1,))
+        product("b", 6, (0, 1))
+        product("a", 6, (0, 1))
         b_term(5)
         a_term(5)
         blend(5, nc.gpsimd)
@@ -277,8 +299,9 @@ def tile_list_gated_link_logits_kernel(tc, tab_words, tab_scales, offs, wa, wb_w
         gather_v2_words()
         turn((2, 3))
         interleave((2, 3))
-        product("b", 7)
-        product("a", 7)
+        sigmoid(7)
+        product("b", 7, (0, 1))
+        product("a", 7, (0, 1))
         score((0, 1), 0)
         score((0, 1), 1)
         b_term(6)

@@ -20,98 +20,110 @@ ACT = mybir.ActivationFunctionType
 P = 128
 PASSES = K // 512
 SLICE = 256
+HALF_LIST = S // 2
+PASS1_ROW = 16
 WB_ROW = 4
 V2_ROW = 8
+KB = 1024
 
 
 def tile_list_gated_link_logits_kernel(tc, tab_words, tab_scales, offs, wa, wb_words, wb_scales,
-                                                wg_words, wg_scales, tab2_words, tab2_scales, offs2, bias, out):
+                                                   wg_words, wg_scales, tab2_words, tab2_scales, offs2, bias, out):
     nc = tc.nc
     with ExitStack() as ctx:
         keep = ctx.enter_context(tc.tile_pool(name="keep", bufs=1))
+        staged = ctx.enter_context(tc.tile_pool(name="staged", bufs=1))
         ring = ctx.enter_context(tc.tile_pool(name="ring", bufs=4))
-        psum = ctx.enter_context(tc.psum_pool(name="psum", bufs=8))
+        psum = ctx.enter_context(tc.psum_pool(name="psum", bufs=1))
 
-        def bank(name):
-            return psum.tile([P, 512], F32, name=name, tag="bank")
+        def bank(name, b):
+            return psum.tile([P, 512], F32, name=name, tag="bank%d" % b)
 
         idx = keep.tile([P, S // 16], U16, name="idx")
         idx2 = keep.tile([P, S2 // 16], U16, name="idx2")
-        tab_plane = keep.tile([P, PASSES, T // 4], I32, name="tab_plane", tag="plane_then_plane2", align_bytes=64)
+        tab_plane = staged.tile([P, T // 4], I32, name="tab_plane", offset=3 * KB, align_bytes=64)
+        tab_w = [staged.tile([P, T], I32, name="tab_w%d" % a, offset=(8 + 12 * a) * KB, align_bytes=64) for a in range(PASSES)]
         wg_plane = keep.tile([P, PASSES, H // 4], I32, name="wg_plane", align_bytes=64)
         wb_plane = keep.tile([P, PASSES, H // 4], I32, name="wb_plane", align_bytes=64)
-        tab_w = [keep.tile([P, T], I32, name="tab_w%d" % a, tag=("words0_then_wa_then_bias", "words1_then_words2")[a], align_bytes=64) for a in range(PASSES)]
+        tab2_plane = keep.tile([P, T2 // 4], I32, name="tab2_plane", align_bytes=64)
         wb_w = keep.tile([P, PASSES, H], I32, name="wb_w", align_bytes=64)
         wg_w = keep.tile([P, PASSES, H // 2], I32, name="wg_w", align_bytes=64)
         wa_w = [keep.tile([P, H], U32, name="wa_w%d" % a, align_bytes=64) for a in range(PASSES)]
         wa_s = [keep.tile([P, H], U8, name="wa_s%d" % a, align_bytes=64) for a in range(PASSES)]
+        moved = keep.tile([P, S // 4], I32, name="moved", align_bytes=64)
+        v_s = keep.tile([P, S], U8, name="v_s", align_bytes=64)
         ident = keep.tile([P, P], F32, name="ident", align_bytes=64)
-
-        def load_plane(queue, plane, row, scales):
-            for q in range(4):
-                queue.dma_start(out=plane[32 * q + row: 32 * q + row + 4, :, :],
-                                in_=scales[:, 4 * q: 4 * q + 4, :].bitcast(I32).rearrange("a r t -> r a t"))
 
         def words(w):
             return w.rearrange("p t i -> p (t i)").bitcast(I32)
 
-        nc.vector.memset(tab_plane[:], 0)
-        nc.gpsimd.memset(wg_plane[:], 0)
+        def load_weight_plane(queue, plane, row, scales):
+            rows = scales.bitcast(I32).rearrange("a (q r) t -> r q a t", r=4)
+            for r in range(4):
+                queue.dma_start(out=plane[row + r: P: 32, :, :], in_=rows[r])
+
+        nc.gpsimd.memset(tab_plane[:], 0)
+        nc.vector.memset(wg_plane[:], 0)
         nc.vector.memset(wb_plane[:], 0)
+        nc.vector.memset(moved[:], 0)
         nc.sync.dma_start(idx[:], offs)
         nc.sync.dma_start(idx2[:], offs2)
-        load_plane(nc.scalar, tab_plane, 0, tab_scales)
-        for a in range(PASSES):
-            nc.sync.dma_start(out=tab_w[a][:], in_=words(tab_words[a]))
+        tab_rows = tab_scales.bitcast(I32).rearrange("a (q r) t -> r q a t", r=4)
+        for r in range(4):
+            nc.sync.dma_start(out=tab_plane[r: P: PASS1_ROW, :], in_=tab_rows[r])
+        nc.sync.dma_start(out=tab_w[0][:], in_=words(tab_words[0]))
         nc.sync.dma_start(out=wg_w[:], in_=wg_words.bitcast(I32).rearrange("a p c -> p a c"))
-        nc.sync.dma_start(out=wb_w[:], in_=wb_words.rearrange("a p c i -> p a (c i)").bitcast(I32))
-        load_plane(nc.gpsimd, wg_plane, 0, wg_scales)
-        load_plane(nc.scalar, wb_plane, WB_ROW, wb_scales)
+        load_weight_plane(nc.sync, wg_plane, 0, wg_scales)
+        nc.sync.dma_start(out=tab_w[1][:], in_=words(tab_words[1]))
+        nc.gpsimd.memset(tab2_plane[:], 0)
         make_identity(nc, ident[:])
-        late = {}
+        warm = keep.tile([P, 8], F32, name="warm")
+        nc.vector.memset(warm[:, 0:1], 0.0)
+        nc.scalar.activation(out=warm[:, 1:2], in_=warm[:, 0:1], func=ACT.Sigmoid)
 
-        def load_wa():
-            late["wa"] = keep.tile([P, PASSES, 4, H], F32, name="wa_raw", tag="words0_then_wa_then_bias", align_bytes=64)
-            for a in range(PASSES):
-                for c in range(2):
-                    cols = slice(c * H // 2, (c + 1) * H // 2)
-                    nc.sync.dma_start(out=late["wa"][:, a, :, cols], in_=wa[512 * a: 512 * (a + 1), cols].rearrange("(p i) c -> p i c", i=4))
+        v_w, acc, gate, a_part, b_part, wa_raw, wa_bf, v2, h_rows, turned, h_bf, h_w, h_s, y, logits = [{} for n in range(15)]
+        half = H // 2
+        late_gates = {}
 
-        def load_tab2_plane():
-            late["plane2"] = keep.tile([P, 1, T2 // 4], I32, name="tab2_plane", tag="plane_then_plane2", align_bytes=64)
-            nc.gpsimd.memset(late["plane2"][:], 0)
-            load_plane(nc.sync, late["plane2"], V2_ROW, tab2_scales)
+        def load_wa(a, c):
+            wa_raw[a, c] = staged.tile([P, 4, half], F32, name="wa_raw%d_%d" % (a, c), offset=4 * KB * (2 * a + c), align_bytes=64)
+            nc.sync.dma_start(out=wa_raw[a, c][:], in_=wa[512 * a: 512 * (a + 1), c * half: (c + 1) * half].rearrange("(p i) c -> p i c", i=4))
+
+        def load_tab2_scales():
+            rows = tab2_scales[0].bitcast(I32).rearrange("(q r) t -> r q t", r=4)
+            for r in range(4):
+                nc.sync.dma_start(out=tab2_plane[V2_ROW + r: P: 32, :], in_=rows[r])
 
         def load_tab2_words():
-            late["words2"] = keep.tile([P, T2], I32, name="tab2_w", tag="words1_then_words2", align_bytes=64)
-            nc.sync.dma_start(out=late["words2"][:], in_=words(tab2_words[0]))
-
-        def load_bias():
-            late["bias"] = keep.tile([P, S2 // P], F32, name="bias_col", tag="words0_then_wa_then_bias", align_bytes=64)
+            v2["table"] = staged.tile([P, T2], I32, name="tab2_w", offset=25 * KB, align_bytes=64)
+            nc.sync.dma_start(out=v2["table"][:], in_=words(tab2_words[0]))
+            v2["bias"] = staged.tile([P, S2 // P], F32, name="bias_col", offset=22 * KB, align_bytes=64)
             with nc.allow_non_contiguous_dma(reason="one bias value to a partition"):
-                nc.sync.dma_start(out=late["bias"][:], in_=bias.rearrange("(m p) -> p m", p=P))
+                nc.sync.dma_start(out=v2["bias"][:], in_=bias.rearrange("(m p) -> p m", p=P))
 
-        v_w, v_s, acc, gate, a_part, b_part, wa_bf, v2, h_rows, turned, h_bf, h_w, h_s, y, logits = [{} for n in range(15)]
-        half = H // 2
+        def gather_scales():
+            nc.vector.tensor_copy(v_s[:], tab_plane[:].bitcast(U8).indirect(idx[:]))
 
-        def offsets(s):
-            return idx[:, s * SLICE // 16: (s + 1) * SLICE // 16]
+        def load_wb():
+            nc.sync.dma_start(out=wb_w[:], in_=wb_words.rearrange("a p c i -> p a (c i)").bitcast(I32))
 
-        def gather_scales(s, a):
-            v_s[s, a] = keep.tile([P, SLICE], U8, name="v_s%d_%d" % (s, a), align_bytes=64)
-            nc.vector.tensor_copy(v_s[s, a][:], tab_plane[:, a, :].bitcast(U8).indirect(offsets(s)))
+        def load_wb_scales():
+            load_weight_plane(nc.sync, wb_plane, WB_ROW, wb_scales)
+
+        def move_scales():
+            nc.sync.dma_start(out=moved[0: P - PASS1_ROW, :], in_=v_s[PASS1_ROW:, :].bitcast(I32))
 
         def gather_words(s, a):
             v_w[s, a] = keep.tile([P, SLICE], U32, name="v_w%d_%d" % (s, a), align_bytes=64)
-            nc.vector.tensor_copy(v_w[s, a][:], tab_w[a][:].bitcast(U32).indirect(offsets(s)))
+            nc.vector.tensor_copy(v_w[s, a][:], tab_w[a][:].bitcast(U32).indirect(idx[:, s * SLICE // 16: (s + 1) * SLICE // 16]))
 
         def gather_v2_scales():
-            v2["s"] = keep.tile([P, S2], U8, name="v2_s", align_bytes=64)
-            nc.vector.tensor_copy(v2["s"][:], late["plane2"][:, 0, :].bitcast(U8).indirect(idx2[:]))
+            v2["s"] = staged.tile([P, S2], U8, name="v2_s", offset=20 * KB, align_bytes=64)
+            nc.vector.tensor_copy(v2["s"][:], tab2_plane[:].bitcast(U8).indirect(idx2[:]))
 
         def gather_v2_words():
-            v2["w"] = keep.tile([P, S2], U32, name="v2_w", tag="wa_bf1", align_bytes=64)
-            nc.vector.tensor_copy(v2["w"][:], late["words2"][:].bitcast(U32).indirect(idx2[:]))
+            v2["w"] = keep.tile([P, S2], U32, name="v2_w", align_bytes=64)
+            nc.vector.tensor_copy(v2["w"][:], v2["table"][:].bitcast(U32).indirect(idx2[:]))
 
         def weight(kind, a):
             if kind == "z":
@@ -120,15 +132,23 @@ def tile_list_gated_link_logits_kernel(tc, tab_words, tab_scales, offs, wa, wb_w
                 return wb_w[:, a, :].bitcast(FP8X4), wb_plane[WB_ROW:, a, :].bitcast(U8)
             return wa_w[a][:].bitcast(FP8X4), wa_s[a][:]
 
-        def product(kind, u, passes):
+        def product(kind, u, passes, b=None):
             s, c = divmod(u * P, SLICE)
             if 0 in passes:
-                acc[kind, u] = bank(kind)
+                acc[kind, u] = bank(kind, b)
             for a in passes:
                 rhs, rhs_scale = weight(kind, a)
+                plane = (v_s[:], moved[:].bitcast(U8))[a]
                 nc.tensor.matmul_mx(out=acc[kind, u][:], lhsT=v_w[s, a][:, c: c + P].bitcast(FP8X4),
-                                    lhsT_scale=v_s[s, a][:, c: c + P], rhs=rhs, rhs_scale=rhs_scale,
+                                    lhsT_scale=plane[:, u * P: (u + 1) * P], rhs=rhs, rhs_scale=rhs_scale,
                                     start=(a == 0), stop=(a == PASSES - 1))
+
+        def gate_tile(u):
+            if u < 4:
+                return keep.tile([P, H], F32, name="gate%d" % u)[:]
+            if u % 2 == 0:
+                late_gates[u] = staged.tile([P, 2 * H], F32, name="gates%d" % u, offset=(23 * KB + 4 * KB * (u - 4)) // 2, align_bytes=64)
+            return late_gates[u - u % 2][:, (u % 2) * H: (u % 2 + 1) * H]
 
         def by_pairs(t):
             return t[:].rearrange("j (p w e) -> j w p e", w=2, e=2)
@@ -137,11 +157,11 @@ def tile_list_gated_link_logits_kernel(tc, tab_words, tab_scales, offs, wa, wb_w
             return t[:].rearrange("j (w p e) -> j w p e", w=2, e=2)
 
         def sigmoid(u):
-            gate[u] = keep.tile([P, H], F32, name="gate%d" % u)
+            gate[u] = gate_tile(u)
             nc.scalar.activation(out=pairs(gate[u]), in_=by_pairs(acc["z", u]), func=ACT.Sigmoid)
 
         def b_term(u):
-            b_part[u] = ring.tile([P, H], F32, name="b_part")
+            b_part[u] = keep.tile([P, H], F32, name="b_part%d" % u)
             for w in range(2):
                 nc.vector.scalar_tensor_tensor(out=pairs(b_part[u])[:, w], in0=pairs(gate[u])[:, w], scalar=1.0,
                                                in1=by_pairs(acc["b", u])[:, w], op0=ALU.subtract, op1=ALU.mult)
@@ -154,20 +174,63 @@ def tile_list_gated_link_logits_kernel(tc, tab_words, tab_scales, offs, wa, wb_w
             h_rows[u] = ring.tile([P, H], BF16, name="h_rows", align_bytes=64)
             engine.tensor_tensor(out=h_rows[u][:], in0=a_part[u][:], in1=b_part[u][:], op=ALU.subtract)
 
-        def round_wa_left(a):
-            wa_bf[a] = keep.tile([P, 4 * H], BF16, name="wa_bf%d" % a, tag="wa_bf%d" % a, align_bytes=64)
-            nc.scalar.copy(out=wa_bf[a][:, : 4 * half].rearrange("p (c x i) -> p c i x", x=4, i=4),
-                           in_=late["wa"][:, a, :, :half].rearrange("p i (c x) -> p c i x", x=4))
+        def by_slot(t):
+            return t[:].rearrange("j (p t) -> j t p", t=4)
 
-        def round_wa_right(a):
-            nc.scalar.copy(out=wa_bf[a][:, 4 * half:].rearrange("p (c x i) -> p c i x", x=4, i=4),
-                           in_=late["wa"][:, a, :, half:].rearrange("p i (c x) -> p c i x", x=4))
+        def slots(t):
+            return t[:].rearrange("j (t p) -> j t p", t=4)
 
-        def quantise_wa(a):
-            nc.vector.quantize_mx(out=wa_w[a][:].bitcast(FP8X4), scales=wa_s[a][:], in_=wa_bf[a][:])
+        def sigmoid_last(u):
+            gate[u] = gate_tile(u)
+            nc.scalar.activation(out=slots(gate[u]), in_=by_slot(acc["z", u]), func=ACT.Sigmoid)
 
-        def turn(us):
-            turned[us] = bank("turned")
+        def b_term_last(u):
+            b_part[u] = keep.tile([P, H], F32, name="b_part%d" % u)
+            nc.vector.scalar_tensor_tensor(out=slots(b_part[u]), in0=slots(gate[u]), scalar=1.0, in1=by_slot(acc["b", u]),
+                                           op0=ALU.subtract, op1=ALU.mult)
+
+        def a_term_last(u):
+            a_part[u] = ring.tile([P, H], F32, name="a_part")
+            nc.vector.scalar_tensor_tensor(out=slots(a_part[u]), in0=slots(gate[u]), scalar=-1.0, in1=by_slot(acc["a", u]),
+                                           op0=ALU.mult, op1=ALU.mult)
+
+        def turn_sum(u, b):
+            turned[u] = bank("turned", b)
+            for n, part in enumerate((b_part[u], a_part[u])):
+                for t in range(4):
+                    nc.tensor.matmul(turned[u][:, t * P: (t + 1) * P], part[:, t * P: (t + 1) * P], ident[:], is_transpose=True,
+                                     start=(n == 0 and t == 0), stop=(n == 1 and t == 3))
+
+        def interleave_part(u, us):
+            if u == us[0]:
+                h_bf[us] = ring.tile([P, 4 * P * len(us)], BF16, name="h_bf", align_bytes=64)
+            at = 4 * P * (u - us[0])
+            nc.scalar.activation(out=h_bf[us][:, at: at + 4 * P].rearrange("p (j t) -> p j t", t=4),
+                                 in_=turned[u][:].rearrange("p (t j) -> p j t", t=4), func=ACT.Copy, scale=-1.0)
+
+        def interleave_last(u):
+            interleave_part(u, (u,))
+
+        def round_wa(a, c, on_scalar, lo=0, hi=half):
+            if (a, c) == (0, 0):
+                wa_bf[a, c] = staged.tile([P, 4 * half], BF16, name="wa_bf0_0", offset=23 * KB, align_bytes=64)
+            elif (a, c) not in wa_bf:
+                wa_bf[a, c] = keep.tile([P, 4 * half], BF16, name="wa_bf%d_%d" % (a, c), align_bytes=64)
+            dst = wa_bf[a, c][:, 4 * lo: 4 * hi].rearrange("p (c x i) -> p c i x", x=4, i=4)
+            src = wa_raw[a, c][:, :, lo:hi].rearrange("p i (c x) -> p c i x", x=4)
+            if on_scalar:
+                nc.scalar.copy(out=dst, in_=src)
+            else:
+                dst = wa_bf[a, c][:, 4 * lo: 4 * hi].rearrange("p (c i) -> p c i", i=4)
+                src = wa_raw[a, c][:, :, lo:hi].rearrange("p i c -> p c i")
+                nc.gpsimd.tensor_scalar(out=dst, in0=src, scalar1=1.0, scalar2=0.0, op0=ALU.mult, op1=ALU.add)
+
+        def quantise_wa(a, c):
+            cols = slice(c * half, (c + 1) * half)
+            nc.vector.quantize_mx(out=wa_w[a][:, cols].bitcast(FP8X4), scales=wa_s[a][:, cols], in_=wa_bf[a, c][:])
+
+        def turn(us, b):
+            turned[us] = bank("turned", b)
             for t, u in enumerate(us):
                 for w in range(2):
                     nc.tensor.transpose(turned[us][:, (2 * t + w) * P: (2 * t + w + 1) * P],
@@ -186,9 +249,9 @@ def tile_list_gated_link_logits_kernel(tc, tab_words, tab_scales, offs, wa, wb_w
             nc.vector.quantize_mx(out=h_w[us][:].bitcast(FP8X4), scales=h_s[us][:], in_=h_bf[us][:])
             logits[us] = ring.tile([P, S2 // P, n], F32, name="logits")
 
-        def score(us, i):
+        def score(us, i, b):
             n = len(us) * P
-            y[us, i] = bank("y")
+            y[us, i] = bank("y", b)
             for t in range(2):
                 m = 2 * i + t
                 nc.tensor.matmul_mx(out=y[us, i][:, t * n: (t + 1) * n],
@@ -202,144 +265,114 @@ def tile_list_gated_link_logits_kernel(tc, tab_words, tab_scales, offs, wa, wb_w
                 m = 2 * i + t
                 src = y[us, i][:, t * n: (t + 1) * n]
                 if on_vector:
-                    nc.vector.tensor_scalar(out=logits[us][:, m, :], in0=src, scalar1=late["bias"][:, m: m + 1], scalar2=None, op0=ALU.add)
+                    nc.vector.tensor_scalar(out=logits[us][:, m, :], in0=src, scalar1=v2["bias"][:, m: m + 1], scalar2=None, op0=ALU.add)
                 else:
-                    nc.scalar.activation(out=logits[us][:, m, :], in_=src, func=ACT.Identity, bias=late["bias"][:, m: m + 1])
+                    nc.scalar.activation(out=logits[us][:, m, :], in_=src, func=ACT.Identity, bias=v2["bias"][:, m: m + 1])
 
         def store(us):
             n = len(us) * P
             j0 = us[0] * P
             nc.sync.dma_start(out=out[:, j0: j0 + n].rearrange("(m p) j -> p m j", p=P), in_=logits[us][:])
 
-        gather_scales(0, 0)
-        gather_words(0, 0)
-        gather_words(1, 0)
-        gather_words(2, 0)
-        gather_words(3, 0)
-        load_wa()
-        gather_words(0, 1)
-        gather_scales(0, 1)
-        product("z", 0, (0,))
-        product("z", 1, (0,))
-        product("z", 0, (1,))
-        product("z", 1, (1,))
-        gather_scales(1, 0)
-        gather_words(1, 1)
-        gather_scales(1, 1)
-        sigmoid(0)
-        sigmoid(1)
-        product("z", 2, (0,))
-        product("b", 0, (0, 1))
-        product("b", 1, (0, 1))
-        product("z", 3, (0,))
-        product("z", 2, (1,))
-        product("z", 3, (1,))
-        gather_scales(2, 0)
-        gather_scales(2, 1)
-        gather_words(2, 1)
-        round_wa_left(0)
-        round_wa_right(0)
-        round_wa_left(1)
-        round_wa_right(1)
-        load_bias()
-        product("b", 2, (0, 1))
-        product("b", 3, (0, 1))
-        gather_words(3, 1)
+        gather_scales()
+        move_scales()
+        load_tab2_scales()
+        load_wb()
+        load_wa(0, 0)
+        load_wb_scales()
+        load_wa(0, 1)
+        for s in range(4):
+            gather_words(s, 0)
+        load_wa(1, 0)
+        load_wa(1, 1)
+        for u in range(6):
+            product("z", u, (0,), u)
+        for s in range(4):
+            gather_words(s, 1)
         load_tab2_words()
-        gather_scales(3, 0)
-        gather_scales(3, 1)
-        load_tab2_plane()
-        product("z", 4, (0,))
-        product("z", 4, (1,))
-        product("z", 5, (0,))
-        product("z", 5, (1,))
-        b_term(0)
-        b_term(1)
-        quantise_wa(0)
-        quantise_wa(1)
-        sigmoid(2)
-        sigmoid(3)
-        sigmoid(4)
-        sigmoid(5)
-        product("a", 0, (0, 1))
-        product("a", 1, (0, 1))
-        b_term(2)
-        b_term(3)
-        a_term(0)
-        blend(0, nc.gpsimd)
-        product("a", 2, (0, 1))
-        a_term(1)
-        blend(1, nc.gpsimd)
-        product("a", 3, (0, 1))
         gather_v2_scales()
-        product("b", 4, (0, 1))
-        product("a", 4, (0, 1))
-        a_term(2)
-        blend(2, nc.gpsimd)
-        product("b", 5, (0, 1))
-        product("z", 6, (0,))
-        product("z", 6, (1,))
-        a_term(3)
-        blend(3, nc.gpsimd)
-        product("a", 5, (0, 1))
-        turn((0, 1))
-        interleave((0, 1))
-        sigmoid(6)
-        b_term(4)
-        a_term(4)
-        blend(4, nc.gpsimd)
-        product("z", 7, (0,))
-        product("z", 7, (1,))
-        product("b", 6, (0, 1))
-        product("a", 6, (0, 1))
-        b_term(5)
-        a_term(5)
-        blend(5, nc.gpsimd)
-        quantise_h((0, 1))
+        round_wa(0, 0, False)
+        round_wa(0, 1, False)
+        for u in range(6):
+            product("z", u, (1,))
+        for u in range(4):
+            sigmoid(u)
+        for u in range(4):
+            product("b", u, (0, 1), (6, 7, 0, 1)[u])
+        round_wa(1, 0, True)
+        round_wa(1, 1, True)
+        for u in range(4):
+            b_term(u)
+        for a in range(2):
+            for c in range(2):
+                quantise_wa(a, c)
+        for u in (4, 5):
+            sigmoid_last(u)
+        for u in (4, 5):
+            product("b", u, (0, 1), u - 2)
+        for u in (6, 7):
+            product("z", u, (0, 1), u)
+        for u in range(4):
+            product("a", u, (0, 1), (0, 1, 4, 5)[u])
+        sigmoid_last(6)
+        sigmoid_last(7)
+        b_term_last(4)
+        for u in range(4):
+            a_term(u)
+            blend(u, nc.gpsimd)
+        product("a", 4, (0, 1), 6)
+        product("a", 5, (0, 1), 2)
+        product("b", 6, (0, 1), 3)
+        product("a", 6, (0, 1), 0)
+        product("b", 7, (0, 1), 1)
         gather_v2_words()
-        turn((2, 3))
+        turn((0, 1), 4)
+        interleave((0, 1))
+        product("a", 7, (0, 1), 5)
+        a_term_last(4)
+        b_term_last(5)
+        a_term_last(5)
+        quantise_h((0, 1))
+        turn_sum(4, 6)
+        turn_sum(5, 7)
+        score((0, 1), 0, 4)
+        score((0, 1), 1, 2)
+        turn((2, 3), 6)
+        interleave_part(4, (4, 5))
+        interleave_part(5, (4, 5))
         interleave((2, 3))
-        sigmoid(7)
-        product("b", 7, (0, 1))
-        product("a", 7, (0, 1))
-        score((0, 1), 0)
-        score((0, 1), 1)
-        b_term(6)
-        a_term(6)
-        blend(6, nc.gpsimd)
         add_bias((0, 1), 0, False)
         add_bias((0, 1), 1, False)
         store((0, 1))
-        quantise_h((2, 3))
-        turn((4, 5))
-        interleave((4, 5))
-        score((2, 3), 0)
-        score((2, 3), 1)
-        b_term(7)
-        a_term(7)
-        add_bias((2, 3), 0, False)
+        b_term_last(6)
+        a_term_last(6)
         quantise_h((4, 5))
-        blend(7, nc.vector)
-        add_bias((2, 3), 1, False)
-        store((2, 3))
-        turn((6,))
-        interleave((6,))
-        score((4, 5), 0)
-        score((4, 5), 1)
-        turn((7,))
-        add_bias((4, 5), 0, False)
+        b_term_last(7)
+        quantise_h((2, 3))
+        a_term_last(7)
+        turn_sum(6, 3)
+        score((4, 5), 0, 7)
+        score((4, 5), 1, 0)
+        score((2, 3), 0, 6)
+        score((2, 3), 1, 1)
+        turn_sum(7, 4)
+        interleave_last(6)
+        interleave_last(7)
+        add_bias((4, 5), 0, True)
         quantise_h((6,))
         add_bias((4, 5), 1, True)
         store((4, 5))
-        interleave((7,))
-        score((6,), 0)
-        score((6,), 1)
         quantise_h((7,))
+        add_bias((2, 3), 0, False)
+        add_bias((2, 3), 1, True)
+        store((2, 3))
+        score((6,), 0, 2)
+        score((6,), 1, 5)
+        score((7,), 0, 3)
+        score((7,), 1, 4)
         add_bias((6,), 0, False)
         add_bias((6,), 1, True)
         store((6,))
-        score((7,), 0)
-        score((7,), 1)
         add_bias((7,), 0, False)
         add_bias((7,), 1, True)
         store((7,))

@@ -25,6 +25,7 @@ PASS1_ROW = 16
 WB_ROW = 4
 V2_ROW = 8
 KB = 1024
+GATE_AT = {4: 0, 5: 8, 6: 10, 7: 12}
 
 
 def tile_list_gated_link_logits_kernel(tc, tab_words, tab_scales, offs, wa, wb_words, wb_scales,
@@ -63,6 +64,7 @@ def tile_list_gated_link_logits_kernel(tc, tab_words, tab_scales, offs, wa, wb_w
                 queue.dma_start(out=plane[row + r: P: 32, :, :], in_=rows[r])
 
         nc.gpsimd.memset(tab_plane[:], 0)
+        nc.gpsimd.memset(tab2_plane[:], 0)
         nc.vector.memset(wg_plane[:], 0)
         nc.vector.memset(wb_plane[:], 0)
         nc.vector.memset(moved[:], 0)
@@ -75,24 +77,19 @@ def tile_list_gated_link_logits_kernel(tc, tab_words, tab_scales, offs, wa, wb_w
         nc.sync.dma_start(out=wg_w[:], in_=wg_words.bitcast(I32).rearrange("a p c -> p a c"))
         load_weight_plane(nc.sync, wg_plane, 0, wg_scales)
         nc.sync.dma_start(out=tab_w[1][:], in_=words(tab_words[1]))
-        nc.gpsimd.memset(tab2_plane[:], 0)
+        tab2_rows = tab2_scales[0].bitcast(I32).rearrange("(q r) t -> r q t", r=4)
+        for r in range(4):
+            nc.gpsimd.dma_start(out=tab2_plane[V2_ROW + r: P: 32, :], in_=tab2_rows[r])
         make_identity(nc, ident[:])
         warm = keep.tile([P, 8], F32, name="warm")
         nc.vector.memset(warm[:, 0:1], 0.0)
         nc.scalar.activation(out=warm[:, 1:2], in_=warm[:, 0:1], func=ACT.Sigmoid)
 
         v_w, acc, gate, a_part, b_part, wa_raw, wa_bf, v2, h_rows, turned, h_bf, h_w, h_s, y, logits = [{} for n in range(15)]
-        half = H // 2
-        late_gates = {}
 
-        def load_wa(a, c):
-            wa_raw[a, c] = staged.tile([P, 4, half], F32, name="wa_raw%d_%d" % (a, c), offset=4 * KB * (2 * a + c), align_bytes=64)
-            nc.sync.dma_start(out=wa_raw[a, c][:], in_=wa[512 * a: 512 * (a + 1), c * half: (c + 1) * half].rearrange("(p i) c -> p i c", i=4))
-
-        def load_tab2_scales():
-            rows = tab2_scales[0].bitcast(I32).rearrange("(q r) t -> r q t", r=4)
-            for r in range(4):
-                nc.sync.dma_start(out=tab2_plane[V2_ROW + r: P: 32, :], in_=rows[r])
+        def load_wa_pass(a):
+            wa_raw[a] = staged.tile([P, 4, H], F32, name="wa_raw%d" % a, offset=8 * KB * a, align_bytes=64)
+            nc.sync.dma_start(out=wa_raw[a][:], in_=wa[512 * a: 512 * (a + 1), :].rearrange("(p i) c -> p i c", i=4))
 
         def load_tab2_words():
             v2["table"] = staged.tile([P, T2], I32, name="tab2_w", offset=25 * KB, align_bytes=64)
@@ -145,10 +142,16 @@ def tile_list_gated_link_logits_kernel(tc, tab_words, tab_scales, offs, wa, wb_w
 
         def gate_tile(u):
             if u < 4:
-                return keep.tile([P, H], F32, name="gate%d" % u)[:]
-            if u % 2 == 0:
-                late_gates[u] = staged.tile([P, 2 * H], F32, name="gates%d" % u, offset=(23 * KB + 4 * KB * (u - 4)) // 2, align_bytes=64)
-            return late_gates[u - u % 2][:, (u % 2) * H: (u % 2 + 1) * H]
+                return keep.tile([P, H], F32, name="gate%d" % u)
+            return staged.tile([P, H], F32, name="gate%d" % u, offset=GATE_AT[u] * KB, align_bytes=64)
+
+        def b_part_tile(u):
+            if u in (3, 4):
+                return staged.tile([P, H], F32, name="b_part%d" % u, offset=(34 + 2 * (u - 3)) * KB, align_bytes=64)
+            return keep.tile([P, H], F32, name="b_part%d" % u, tag="part0" if u == 5 else "b_part%d" % u)
+
+        def a_part_tile(u):
+            return keep.tile([P, H], F32, name="a_part%d" % u, tag="part%d" % u)
 
         def by_pairs(t):
             return t[:].rearrange("j (p w e) -> j w p e", w=2, e=2)
@@ -161,13 +164,13 @@ def tile_list_gated_link_logits_kernel(tc, tab_words, tab_scales, offs, wa, wb_w
             nc.scalar.activation(out=pairs(gate[u]), in_=by_pairs(acc["z", u]), func=ACT.Sigmoid)
 
         def b_term(u):
-            b_part[u] = keep.tile([P, H], F32, name="b_part%d" % u)
+            b_part[u] = b_part_tile(u)
             for w in range(2):
                 nc.vector.scalar_tensor_tensor(out=pairs(b_part[u])[:, w], in0=pairs(gate[u])[:, w], scalar=1.0,
                                                in1=by_pairs(acc["b", u])[:, w], op0=ALU.subtract, op1=ALU.mult)
 
         def a_term(u):
-            a_part[u] = ring.tile([P, H], F32, name="a_part")
+            a_part[u] = a_part_tile(u)
             nc.vector.tensor_tensor(out=pairs(a_part[u]), in0=by_pairs(acc["a", u]), in1=pairs(gate[u]), op=ALU.mult)
 
         def blend(u, engine):
@@ -185,12 +188,12 @@ def tile_list_gated_link_logits_kernel(tc, tab_words, tab_scales, offs, wa, wb_w
             nc.scalar.activation(out=slots(gate[u]), in_=by_slot(acc["z", u]), func=ACT.Sigmoid)
 
         def b_term_last(u):
-            b_part[u] = keep.tile([P, H], F32, name="b_part%d" % u)
+            b_part[u] = b_part_tile(u)
             nc.vector.scalar_tensor_tensor(out=slots(b_part[u]), in0=slots(gate[u]), scalar=1.0, in1=by_slot(acc["b", u]),
                                            op0=ALU.subtract, op1=ALU.mult)
 
         def a_term_last(u):
-            a_part[u] = ring.tile([P, H], F32, name="a_part")
+            a_part[u] = a_part_tile(u)
             nc.vector.scalar_tensor_tensor(out=slots(a_part[u]), in0=slots(gate[u]), scalar=-1.0, in1=by_slot(acc["a", u]),
                                            op0=ALU.mult, op1=ALU.mult)
 
@@ -211,23 +214,19 @@ def tile_list_gated_link_logits_kernel(tc, tab_words, tab_scales, offs, wa, wb_w
         def interleave_last(u):
             interleave_part(u, (u,))
 
-        def round_wa(a, c, on_scalar, lo=0, hi=half):
-            if (a, c) == (0, 0):
-                wa_bf[a, c] = staged.tile([P, 4 * half], BF16, name="wa_bf0_0", offset=23 * KB, align_bytes=64)
-            elif (a, c) not in wa_bf:
-                wa_bf[a, c] = keep.tile([P, 4 * half], BF16, name="wa_bf%d_%d" % (a, c), align_bytes=64)
-            dst = wa_bf[a, c][:, 4 * lo: 4 * hi].rearrange("p (c x i) -> p c i x", x=4, i=4)
-            src = wa_raw[a, c][:, :, lo:hi].rearrange("p i (c x) -> p c i x", x=4)
+        def round_cols(a, on_scalar, lo, hi):
+            if a not in wa_bf:
+                wa_bf[a] = staged.tile([P, 4 * H], BF16, name="wa_bf%d" % a, offset=(34 + 4 * a) * KB, align_bytes=64)
             if on_scalar:
-                nc.scalar.copy(out=dst, in_=src)
+                nc.scalar.copy(out=wa_bf[a][:, 4 * lo: 4 * hi].rearrange("p (c x i) -> p c i x", x=4, i=4),
+                               in_=wa_raw[a][:, :, lo:hi].rearrange("p i (c x) -> p c i x", x=4))
             else:
-                dst = wa_bf[a, c][:, 4 * lo: 4 * hi].rearrange("p (c i) -> p c i", i=4)
-                src = wa_raw[a, c][:, :, lo:hi].rearrange("p i c -> p c i")
-                nc.gpsimd.tensor_scalar(out=dst, in0=src, scalar1=1.0, scalar2=0.0, op0=ALU.mult, op1=ALU.add)
+                nc.gpsimd.tensor_scalar(out=wa_bf[a][:, 4 * lo: 4 * hi].rearrange("p (c i) -> p c i", i=4),
+                                        in0=wa_raw[a][:, :, lo:hi].rearrange("p i c -> p c i"),
+                                        scalar1=1.0, scalar2=0.0, op0=ALU.mult, op1=ALU.add)
 
-        def quantise_wa(a, c):
-            cols = slice(c * half, (c + 1) * half)
-            nc.vector.quantize_mx(out=wa_w[a][:, cols].bitcast(FP8X4), scales=wa_s[a][:, cols], in_=wa_bf[a, c][:])
+        def quantise_pass(a):
+            nc.vector.quantize_mx(out=wa_w[a][:].bitcast(FP8X4), scales=wa_s[a][:], in_=wa_bf[a][:])
 
         def turn(us, b):
             turned[us] = bank("turned", b)
@@ -242,12 +241,14 @@ def tile_list_gated_link_logits_kernel(tc, tab_words, tab_scales, offs, wa, wb_w
             nc.scalar.copy(out=h_bf[us][:].bitcast(F32).rearrange("p (t j w) -> p t j w", j=P, w=2),
                            in_=turned[us][:, 0: 2 * n].rearrange("p (t w j) -> p t j w", j=P, w=2))
 
-        def quantise_h(us):
+        def quantise_h(us, at):
             n = len(us) * P
-            h_w[us] = ring.tile([P, n], U32, name="h_w", align_bytes=64)
+            if at is None:
+                h_w[us] = ring.tile([P, n], U32, name="h_w", align_bytes=64)
+            else:
+                h_w[us] = staged.tile([P, n], U32, name="h_w%d" % us[0], offset=GATE_AT[at] * KB, align_bytes=64)
             h_s[us] = ring.tile([P, n], U8, name="h_s", align_bytes=64)
             nc.vector.quantize_mx(out=h_w[us][:].bitcast(FP8X4), scales=h_s[us][:], in_=h_bf[us][:])
-            logits[us] = ring.tile([P, S2 // P, n], F32, name="logits")
 
         def score(us, i, b):
             n = len(us) * P
@@ -261,13 +262,36 @@ def tile_list_gated_link_logits_kernel(tc, tab_words, tab_scales, offs, wa, wb_w
 
         def add_bias(us, i, on_vector):
             n = len(us) * P
+            if n == P:
+                if i == 0:
+                    logits[us] = keep.tile([P, 4, n], F32, name="logits%d" % us[0])
+                dst = logits[us][:, 2 * i: 2 * i + 2, :]
+            else:
+                logits[us, i] = keep.tile([P, 2, n], F32, name="logits%d_%d" % (us[0], i))
+                dst = logits[us, i][:]
             for t in range(2):
                 m = 2 * i + t
                 src = y[us, i][:, t * n: (t + 1) * n]
                 if on_vector:
-                    nc.vector.tensor_scalar(out=logits[us][:, m, :], in0=src, scalar1=v2["bias"][:, m: m + 1], scalar2=None, op0=ALU.add)
+                    nc.vector.tensor_scalar(out=dst[:, t, :], in0=src, scalar1=v2["bias"][:, m: m + 1], scalar2=None, op0=ALU.add)
                 else:
-                    nc.scalar.activation(out=logits[us][:, m, :], in_=src, func=ACT.Identity, bias=v2["bias"][:, m: m + 1])
+                    nc.scalar.activation(out=dst[:, t, :], in_=src, func=ACT.Identity, bias=v2["bias"][:, m: m + 1])
+
+        def store_half(us, i):
+            n = len(us) * P
+            j0 = us[0] * P
+            nc.sync.dma_start(out=out[2 * P * i: 2 * P * (i + 1), j0: j0 + n].rearrange("(m p) j -> p m j", p=P), in_=logits[us, i][:])
+
+        def finish(c, banks, onv, at=None):
+            quantise_h(c, at)
+            for i in range(2):
+                score(c, i, banks[i])
+            for i in range(2):
+                add_bias(c, i, onv[i])
+                if len(c) == 2:
+                    store_half(c, i)
+            if len(c) == 1:
+                store(c)
 
         def store(us):
             n = len(us) * P
@@ -276,103 +300,79 @@ def tile_list_gated_link_logits_kernel(tc, tab_words, tab_scales, offs, wa, wb_w
 
         gather_scales()
         move_scales()
-        load_tab2_scales()
         load_wb()
-        load_wa(0, 0)
         load_wb_scales()
-        load_wa(0, 1)
+        load_wa_pass(0)
         for s in range(4):
             gather_words(s, 0)
-        load_wa(1, 0)
-        load_wa(1, 1)
+        load_wa_pass(1)
         for u in range(6):
             product("z", u, (0,), u)
         for s in range(4):
             gather_words(s, 1)
         load_tab2_words()
         gather_v2_scales()
-        round_wa(0, 0, False)
-        round_wa(0, 1, False)
         for u in range(6):
             product("z", u, (1,))
         for u in range(4):
             sigmoid(u)
         for u in range(4):
             product("b", u, (0, 1), (6, 7, 0, 1)[u])
-        round_wa(1, 0, True)
-        round_wa(1, 1, True)
-        for u in range(4):
-            b_term(u)
         for a in range(2):
-            for c in range(2):
-                quantise_wa(a, c)
+            round_cols(a, True, 0, 288)
+            round_cols(a, False, 288, 512)
+        for u in range(3):
+            b_term(u)
+        quantise_pass(0)
+        quantise_pass(1)
+        b_term(3)
         for u in (4, 5):
-            sigmoid_last(u)
-        for u in (4, 5):
+            sigmoid(u)
             product("b", u, (0, 1), u - 2)
+        b_term(4)
         for u in (6, 7):
             product("z", u, (0, 1), u)
+            (sigmoid_last if u == 6 else sigmoid)(u)
         for u in range(4):
-            product("a", u, (0, 1), (0, 1, 4, 5)[u])
-        sigmoid_last(6)
-        sigmoid_last(7)
-        b_term_last(4)
-        for u in range(4):
-            a_term(u)
-            blend(u, nc.gpsimd)
-        product("a", 4, (0, 1), 6)
-        product("a", 5, (0, 1), 2)
-        product("b", 6, (0, 1), 3)
-        product("a", 6, (0, 1), 0)
-        product("b", 7, (0, 1), 1)
+            product("a", u, (0, 1), (0, 4, 1, 2)[u])
+
+        a_term(0)
+        blend(0, nc.gpsimd)
+        a_term(1)
+        blend(1, nc.gpsimd)
         gather_v2_words()
-        turn((0, 1), 4)
+        product("a", 4, (0, 1), 5)
+        product("b", 6, (0, 1), 6)
+        product("a", 5, (0, 1), 7)
+        product("a", 6, (0, 1), 0)
+        a_term(2)
+        blend(2, nc.gpsimd)
+        a_term(3)
+        blend(3, nc.gpsimd)
+        turn((0, 1), 1)
         interleave((0, 1))
-        product("a", 7, (0, 1), 5)
-        a_term_last(4)
-        b_term_last(5)
-        a_term_last(5)
-        quantise_h((0, 1))
-        turn_sum(4, 6)
-        turn_sum(5, 7)
-        score((0, 1), 0, 4)
-        score((0, 1), 1, 2)
-        turn((2, 3), 6)
-        interleave_part(4, (4, 5))
-        interleave_part(5, (4, 5))
+        product("b", 7, (0, 1), 4)
+        a_term(4)
+        blend(4, nc.gpsimd)
+        b_term(5)
+        product("a", 7, (0, 1), 2)
+        a_term(5)
+        blend(5, nc.gpsimd)
+        finish((0, 1), (5, 1), (False, False), 5)
+        turn((2, 3), 3)
         interleave((2, 3))
-        add_bias((0, 1), 0, False)
-        add_bias((0, 1), 1, False)
-        store((0, 1))
         b_term_last(6)
         a_term_last(6)
-        quantise_h((4, 5))
-        b_term_last(7)
-        quantise_h((2, 3))
-        a_term_last(7)
-        turn_sum(6, 3)
-        score((4, 5), 0, 7)
-        score((4, 5), 1, 0)
-        score((2, 3), 0, 6)
-        score((2, 3), 1, 1)
-        turn_sum(7, 4)
-        interleave_last(6)
-        interleave_last(7)
-        add_bias((4, 5), 0, True)
-        quantise_h((6,))
-        add_bias((4, 5), 1, True)
-        store((4, 5))
-        quantise_h((7,))
-        add_bias((2, 3), 0, False)
-        add_bias((2, 3), 1, True)
-        store((2, 3))
-        score((6,), 0, 2)
-        score((6,), 1, 5)
-        score((7,), 0, 3)
-        score((7,), 1, 4)
-        add_bias((6,), 0, False)
-        add_bias((6,), 1, True)
-        store((6,))
-        add_bias((7,), 0, False)
-        add_bias((7,), 1, True)
-        store((7,))
+        turn_sum(6, 7)
+        interleave_part(6, (6,))
+        b_term(7)
+        a_term(7)
+        finish((2, 3), (6, 0), (False, False), 7)
+        blend(7, nc.vector)
+        turn((4, 5), 4)
+        interleave((4, 5))
+        finish((6,), (3, 2), (True, True))
+        turn((7,), 5)
+        interleave((7,))
+        finish((4, 5), (1, 7), (True, False))
+        finish((7,), (6, 0), (True, False))

@@ -25,7 +25,9 @@ PASS1_ROW = 16
 WB_ROW = 4
 V2_ROW = 8
 KB = 1024
-GATE_AT = {4: 0, 5: 8, 6: 10, 7: 12}
+PLACE = {"gate0": 44, "gate1": 46, "gate4": 0, "gate5": 8, "gate6": 10, "gate7": 12, "b_part3": 38, "v2_w": 44, "b_part4": 46,
+         "h_bf0": 48, "b_part5": 48, "b_part6": 0}
+SUMMED = (0, 1, 2, 3, 6)
 
 
 def tile_list_gated_link_logits_kernel(tc, tab_words, tab_scales, offs, wa, wb_words, wb_scales,
@@ -77,15 +79,17 @@ def tile_list_gated_link_logits_kernel(tc, tab_words, tab_scales, offs, wa, wb_w
         nc.sync.dma_start(out=wg_w[:], in_=wg_words.bitcast(I32).rearrange("a p c -> p a c"))
         load_weight_plane(nc.sync, wg_plane, 0, wg_scales)
         nc.sync.dma_start(out=tab_w[1][:], in_=words(tab_words[1]))
-        tab2_rows = tab2_scales[0].bitcast(I32).rearrange("(q r) t -> r q t", r=4)
-        for r in range(4):
-            nc.gpsimd.dma_start(out=tab2_plane[V2_ROW + r: P: 32, :], in_=tab2_rows[r])
         make_identity(nc, ident[:])
         warm = keep.tile([P, 8], F32, name="warm")
         nc.vector.memset(warm[:, 0:1], 0.0)
         nc.scalar.activation(out=warm[:, 1:2], in_=warm[:, 0:1], func=ACT.Sigmoid)
 
         v_w, acc, gate, a_part, b_part, wa_raw, wa_bf, v2, h_rows, turned, h_bf, h_w, h_s, y, logits = [{} for n in range(15)]
+
+        def load_tab2_scales():
+            rows = tab2_scales[0].bitcast(I32).rearrange("(q r) t -> r q t", r=4)
+            for r in range(4):
+                nc.sync.dma_start(out=tab2_plane[V2_ROW + r: P: 32, :], in_=rows[r])
 
         def load_wa_pass(a):
             wa_raw[a] = staged.tile([P, 4, H], F32, name="wa_raw%d" % a, offset=8 * KB * a, align_bytes=64)
@@ -119,7 +123,7 @@ def tile_list_gated_link_logits_kernel(tc, tab_words, tab_scales, offs, wa, wb_w
             nc.vector.tensor_copy(v2["s"][:], tab2_plane[:].bitcast(U8).indirect(idx2[:]))
 
         def gather_v2_words():
-            v2["w"] = keep.tile([P, S2], U32, name="v2_w", align_bytes=64)
+            v2["w"] = placed("v2_w", [P, S2], U32)
             nc.vector.tensor_copy(v2["w"][:], v2["table"][:].bitcast(U32).indirect(idx2[:]))
 
         def weight(kind, a):
@@ -140,18 +144,19 @@ def tile_list_gated_link_logits_kernel(tc, tab_words, tab_scales, offs, wa, wb_w
                                     lhsT_scale=plane[:, u * P: (u + 1) * P], rhs=rhs, rhs_scale=rhs_scale,
                                     start=(a == 0), stop=(a == PASSES - 1))
 
+        def placed(name, shape, dtype):
+            if name in PLACE:
+                return staged.tile(shape, dtype, name=name, offset=PLACE[name] * KB, align_bytes=64)
+            return keep.tile(shape, dtype, name=name, align_bytes=64)
+
         def gate_tile(u):
-            if u < 4:
-                return keep.tile([P, H], F32, name="gate%d" % u)
-            return staged.tile([P, H], F32, name="gate%d" % u, offset=GATE_AT[u] * KB, align_bytes=64)
+            return placed("gate%d" % u, [P, H], F32)
 
         def b_part_tile(u):
-            if u in (3, 4):
-                return staged.tile([P, H], F32, name="b_part%d" % u, offset=(34 + 2 * (u - 3)) * KB, align_bytes=64)
-            return keep.tile([P, H], F32, name="b_part%d" % u, tag="part0" if u == 5 else "b_part%d" % u)
+            return placed("b_part%d" % u, [P, H], F32)
 
         def a_part_tile(u):
-            return keep.tile([P, H], F32, name="a_part%d" % u, tag="part%d" % u)
+            return placed("a_part%d" % u, [P, H], F32)
 
         def by_pairs(t):
             return t[:].rearrange("j (p w e) -> j w p e", w=2, e=2)
@@ -160,16 +165,22 @@ def tile_list_gated_link_logits_kernel(tc, tab_words, tab_scales, offs, wa, wb_w
             return t[:].rearrange("j (w p e) -> j w p e", w=2, e=2)
 
         def sigmoid(u):
+            if u in SUMMED:
+                return sigmoid_last(u)
             gate[u] = gate_tile(u)
             nc.scalar.activation(out=pairs(gate[u]), in_=by_pairs(acc["z", u]), func=ACT.Sigmoid)
 
         def b_term(u):
+            if u in SUMMED:
+                return b_term_last(u)
             b_part[u] = b_part_tile(u)
             for w in range(2):
                 nc.vector.scalar_tensor_tensor(out=pairs(b_part[u])[:, w], in0=pairs(gate[u])[:, w], scalar=1.0,
                                                in1=by_pairs(acc["b", u])[:, w], op0=ALU.subtract, op1=ALU.mult)
 
         def a_term(u):
+            if u in SUMMED:
+                return a_term_last(u)
             a_part[u] = a_part_tile(u)
             nc.vector.tensor_tensor(out=pairs(a_part[u]), in0=by_pairs(acc["a", u]), in1=pairs(gate[u]), op=ALU.mult)
 
@@ -206,7 +217,7 @@ def tile_list_gated_link_logits_kernel(tc, tab_words, tab_scales, offs, wa, wb_w
 
         def interleave_part(u, us):
             if u == us[0]:
-                h_bf[us] = ring.tile([P, 4 * P * len(us)], BF16, name="h_bf", align_bytes=64)
+                h_bf[us] = placed("h_bf%d" % us[0], [P, 4 * P * len(us)], BF16)
             at = 4 * P * (u - us[0])
             nc.scalar.activation(out=h_bf[us][:, at: at + 4 * P].rearrange("p (j t) -> p j t", t=4),
                                  in_=turned[u][:].rearrange("p (t j) -> p j t", t=4), func=ACT.Copy, scale=-1.0)
@@ -214,16 +225,20 @@ def tile_list_gated_link_logits_kernel(tc, tab_words, tab_scales, offs, wa, wb_w
         def interleave_last(u):
             interleave_part(u, (u,))
 
-        def round_cols(a, on_scalar, lo, hi):
+        def round_cols(a, engine, lo, hi):
             if a not in wa_bf:
                 wa_bf[a] = staged.tile([P, 4 * H], BF16, name="wa_bf%d" % a, offset=(34 + 4 * a) * KB, align_bytes=64)
-            if on_scalar:
-                nc.scalar.copy(out=wa_bf[a][:, 4 * lo: 4 * hi].rearrange("p (c x i) -> p c i x", x=4, i=4),
-                               in_=wa_raw[a][:, :, lo:hi].rearrange("p i (c x) -> p c i x", x=4))
-            else:
+            if engine == "G":
                 nc.gpsimd.tensor_scalar(out=wa_bf[a][:, 4 * lo: 4 * hi].rearrange("p (c i) -> p c i", i=4),
                                         in0=wa_raw[a][:, :, lo:hi].rearrange("p i c -> p c i"),
                                         scalar1=1.0, scalar2=0.0, op0=ALU.mult, op1=ALU.add)
+                return
+            dst = wa_bf[a][:, 4 * lo: 4 * hi].rearrange("p (c x i) -> p c i x", x=4, i=4)
+            src = wa_raw[a][:, :, lo:hi].rearrange("p i (c x) -> p c i x", x=4)
+            if engine == "A":
+                nc.scalar.copy(out=dst, in_=src)
+            else:
+                nc.vector.tensor_copy(dst, src)
 
         def quantise_pass(a):
             nc.vector.quantize_mx(out=wa_w[a][:].bitcast(FP8X4), scales=wa_s[a][:], in_=wa_bf[a][:])
@@ -237,17 +252,14 @@ def tile_list_gated_link_logits_kernel(tc, tab_words, tab_scales, offs, wa, wb_w
 
         def interleave(us):
             n = len(us) * P
-            h_bf[us] = ring.tile([P, 4 * n], BF16, name="h_bf", align_bytes=64)
+            h_bf[us] = placed("h_bf%d" % us[0], [P, 4 * n], BF16)
             nc.scalar.copy(out=h_bf[us][:].bitcast(F32).rearrange("p (t j w) -> p t j w", j=P, w=2),
                            in_=turned[us][:, 0: 2 * n].rearrange("p (t w j) -> p t j w", j=P, w=2))
 
-        def quantise_h(us, at):
+        def quantise_h(us):
             n = len(us) * P
-            if at is None:
-                h_w[us] = ring.tile([P, n], U32, name="h_w", align_bytes=64)
-            else:
-                h_w[us] = staged.tile([P, n], U32, name="h_w%d" % us[0], offset=GATE_AT[at] * KB, align_bytes=64)
-            h_s[us] = ring.tile([P, n], U8, name="h_s", align_bytes=64)
+            h_w[us] = placed("h_w%d" % us[0], [P, n], U32)
+            h_s[us] = placed("h_s%d" % us[0], [P, n], U8)
             nc.vector.quantize_mx(out=h_w[us][:].bitcast(FP8X4), scales=h_s[us][:], in_=h_bf[us][:])
 
         def score(us, i, b):
@@ -282,17 +294,6 @@ def tile_list_gated_link_logits_kernel(tc, tab_words, tab_scales, offs, wa, wb_w
             j0 = us[0] * P
             nc.sync.dma_start(out=out[2 * P * i: 2 * P * (i + 1), j0: j0 + n].rearrange("(m p) j -> p m j", p=P), in_=logits[us, i][:])
 
-        def finish(c, banks, onv, at=None):
-            quantise_h(c, at)
-            for i in range(2):
-                score(c, i, banks[i])
-            for i in range(2):
-                add_bias(c, i, onv[i])
-                if len(c) == 2:
-                    store_half(c, i)
-            if len(c) == 1:
-                store(c)
-
         def store(us):
             n = len(us) * P
             j0 = us[0] * P
@@ -300,6 +301,7 @@ def tile_list_gated_link_logits_kernel(tc, tab_words, tab_scales, offs, wa, wb_w
 
         gather_scales()
         move_scales()
+        load_tab2_scales()
         load_wb()
         load_wb_scales()
         load_wa_pass(0)
@@ -318,9 +320,10 @@ def tile_list_gated_link_logits_kernel(tc, tab_words, tab_scales, offs, wa, wb_w
             sigmoid(u)
         for u in range(4):
             product("b", u, (0, 1), (6, 7, 0, 1)[u])
-        for a in range(2):
-            round_cols(a, True, 0, 288)
-            round_cols(a, False, 288, 512)
+        round_cols(0, 'A', 0, 352)
+        round_cols(0, 'G', 352, 512)
+        round_cols(1, 'A', 0, 192)
+        round_cols(1, 'V', 192, 512)
         for u in range(3):
             b_term(u)
         quantise_pass(0)
@@ -329,50 +332,77 @@ def tile_list_gated_link_logits_kernel(tc, tab_words, tab_scales, offs, wa, wb_w
         for u in (4, 5):
             sigmoid(u)
             product("b", u, (0, 1), u - 2)
-        b_term(4)
         for u in (6, 7):
             product("z", u, (0, 1), u)
-            (sigmoid_last if u == 6 else sigmoid)(u)
+            sigmoid(u)
+        product("b", 6, (0, 1), 0)
         for u in range(4):
-            product("a", u, (0, 1), (0, 4, 1, 2)[u])
+            product("a", u, (0, 1), (4, 5, 6, 1)[u])
 
         a_term(0)
-        blend(0, nc.gpsimd)
         a_term(1)
-        blend(1, nc.gpsimd)
         gather_v2_words()
+        turn_sum(0, 7)
+        interleave_part(0, (0, 1))
+        turn_sum(1, 4)
+        interleave_part(1, (0, 1))
         product("a", 4, (0, 1), 5)
-        product("b", 6, (0, 1), 6)
-        product("a", 5, (0, 1), 7)
-        product("a", 6, (0, 1), 0)
         a_term(2)
-        blend(2, nc.gpsimd)
         a_term(3)
-        blend(3, nc.gpsimd)
-        turn((0, 1), 1)
-        interleave((0, 1))
-        product("b", 7, (0, 1), 4)
+        b_term(4)
+        turn_sum(2, 7)
+        interleave_part(2, (2, 3))
+        turn_sum(3, 6)
+        interleave_part(3, (2, 3))
+        quantise_h((0, 1))
+        score((0, 1), 0, 1)
+        score((0, 1), 1, 4)
+        product("a", 5, (0, 1), 2)
         a_term(4)
         blend(4, nc.gpsimd)
         b_term(5)
-        product("a", 7, (0, 1), 2)
+        for i in range(2):
+            add_bias((0, 1), i, False)
+            store_half((0, 1), i)
+        product("a", 6, (0, 1), 5)
+        quantise_h((2, 3))
         a_term(5)
+        b_term(6)
         blend(5, nc.gpsimd)
-        finish((0, 1), (5, 1), (False, False), 5)
-        turn((2, 3), 3)
-        interleave((2, 3))
-        b_term_last(6)
-        a_term_last(6)
-        turn_sum(6, 7)
+        score((2, 3), 0, 7)
+        score((2, 3), 1, 6)
+        product("b", 7, (0, 1), 3)
+        product("a", 7, (0, 1), 1)
+        add_bias((2, 3), 0, False)
+        store_half((2, 3), 0)
+        add_bias((2, 3), 1, False)
+        store_half((2, 3), 1)
+        a_term(6)
+        turn_sum(6, 0)
         interleave_part(6, (6,))
+        turn((4, 5), 2)
+        interleave((4, 5))
         b_term(7)
         a_term(7)
-        finish((2, 3), (6, 0), (False, False), 7)
         blend(7, nc.vector)
-        turn((4, 5), 4)
-        interleave((4, 5))
-        finish((6,), (3, 2), (True, True))
-        turn((7,), 5)
+        quantise_h((6,))
+        score((6,), 0, 6)
+        score((6,), 1, 4)
+        quantise_h((4, 5))
+        score((4, 5), 0, 5)
+        score((4, 5), 1, 3)
+        turn((7,), 7)
         interleave((7,))
-        finish((4, 5), (1, 7), (True, False))
-        finish((7,), (6, 0), (True, False))
+        add_bias((6,), 0, True)
+        add_bias((6,), 1, True)
+        store((6,))
+        quantise_h((7,))
+        add_bias((4, 5), 0, True)
+        store_half((4, 5), 0)
+        add_bias((4, 5), 1, False)
+        store_half((4, 5), 1)
+        score((7,), 0, 2)
+        score((7,), 1, 1)
+        add_bias((7,), 0, True)
+        add_bias((7,), 1, False)
+        store((7,))

@@ -19,8 +19,6 @@ ACT = mybir.ActivationFunctionType
 
 P = 128
 PASSES = K // 512
-SLICE = 256
-HALF_LIST = S // 2
 PASS1_ROW = 16
 WB_ROW = 4
 V2_ROW = 8
@@ -114,9 +112,11 @@ def tile_list_gated_link_logits_kernel(tc, tab_words, tab_scales, offs, wa, wb_w
         def move_scales():
             nc.sync.dma_start(out=moved[0: P - PASS1_ROW, :], in_=v_s[PASS1_ROW:, :].bitcast(I32))
 
-        def gather_words(s, a):
-            v_w[s, a] = keep.tile([P, SLICE], U32, name="v_w%d_%d" % (s, a), align_bytes=64)
-            nc.vector.tensor_copy(v_w[s, a][:], tab_w[a][:].bitcast(U32).indirect(idx[:, s * SLICE // 16: (s + 1) * SLICE // 16]))
+        def gather_words(a, lo, hi):
+            tile = keep.tile([P, (hi - lo) * P], U32, name="v_w%d_%d" % (a, lo), align_bytes=64)
+            nc.vector.tensor_copy(tile[:], tab_w[a][:].bitcast(U32).indirect(idx[:, lo * P // 16: hi * P // 16]))
+            for u in range(lo, hi):
+                v_w[u, a] = tile[:, (u - lo) * P: (u - lo + 1) * P]
 
         def gather_v2_scales():
             v2["s"] = staged.tile([P, S2], U8, name="v2_s", offset=20 * KB, align_bytes=64)
@@ -134,13 +134,12 @@ def tile_list_gated_link_logits_kernel(tc, tab_words, tab_scales, offs, wa, wb_w
             return wa_w[a][:].bitcast(FP8X4), wa_s[a][:]
 
         def product(kind, u, passes, b=None):
-            s, c = divmod(u * P, SLICE)
             if 0 in passes:
                 acc[kind, u] = bank(kind, b)
             for a in passes:
                 rhs, rhs_scale = weight(kind, a)
                 plane = (v_s[:], moved[:].bitcast(U8))[a]
-                nc.tensor.matmul_mx(out=acc[kind, u][:], lhsT=v_w[s, a][:, c: c + P].bitcast(FP8X4),
+                nc.tensor.matmul_mx(out=acc[kind, u][:], lhsT=v_w[u, a].bitcast(FP8X4),
                                     lhsT_scale=plane[:, u * P: (u + 1) * P], rhs=rhs, rhs_scale=rhs_scale,
                                     start=(a == 0), stop=(a == PASSES - 1))
 
@@ -305,13 +304,14 @@ def tile_list_gated_link_logits_kernel(tc, tab_words, tab_scales, offs, wa, wb_w
         load_wb()
         load_wb_scales()
         load_wa_pass(0)
-        for s in range(4):
-            gather_words(s, 0)
+        gather_words(0, 0, 2)
+        gather_words(0, 2, 8)
         load_wa_pass(1)
         for u in range(6):
             product("z", u, (0,), u)
-        for s in range(4):
-            gather_words(s, 1)
+        gather_words(1, 0, 2)
+        gather_words(1, 2, 4)
+        gather_words(1, 4, 8)
         load_tab2_words()
         gather_v2_scales()
         for u in range(6):
@@ -355,9 +355,9 @@ def tile_list_gated_link_logits_kernel(tc, tab_words, tab_scales, offs, wa, wb_w
         turn_sum(3, 6)
         interleave_part(3, (2, 3))
         quantise_h((0, 1))
+        product("a", 5, (0, 1), 2)
         score((0, 1), 0, 1)
         score((0, 1), 1, 4)
-        product("a", 5, (0, 1), 2)
         a_term(4)
         blend(4, nc.gpsimd)
         b_term(5)
@@ -369,9 +369,9 @@ def tile_list_gated_link_logits_kernel(tc, tab_words, tab_scales, offs, wa, wb_w
         a_term(5)
         b_term(6)
         blend(5, nc.gpsimd)
+        product("b", 7, (0, 1), 3)
         score((2, 3), 0, 7)
         score((2, 3), 1, 6)
-        product("b", 7, (0, 1), 3)
         product("a", 7, (0, 1), 1)
         add_bias((2, 3), 0, False)
         store_half((2, 3), 0)
@@ -393,8 +393,8 @@ def tile_list_gated_link_logits_kernel(tc, tab_words, tab_scales, offs, wa, wb_w
         score((4, 5), 1, 3)
         turn((7,), 7)
         interleave((7,))
-        add_bias((6,), 0, True)
-        add_bias((6,), 1, True)
+        add_bias((6,), 0, False)
+        add_bias((6,), 1, False)
         store((6,))
         quantise_h((7,))
         add_bias((4, 5), 0, True)

@@ -16,115 +16,88 @@ FP8X4 = mybir.dt.float8_e4m3fn_x4
 FP4X4 = mybir.dt.float4_e2m1fn_x4
 ALU = mybir.AluOpType
 ACT = mybir.ActivationFunctionType
+WIDTH = {F32: 4, I32: 4, U32: 4, BF16: 2, U8: 1}
 
 P = 128
-PASSES = K // 512
-PASS1_ROW = 16
+PASS_K = 4 * P
+PASSES = K // PASS_K
+UNITS = S // P
+BANKS = 8
+BANK_COLUMNS = 512
+LIST_ROWS = 16
 WB_ROW = 4
 V2_ROW = 8
-KB = 1024
-PLACE = {"gate0": 44, "gate1": 46, "gate4": 0, "gate5": 8, "gate6": 10, "gate7": 12, "b_part3": 38, "v2_w": 44, "b_part4": 46,
-         "h_bf0": 48, "b_part5": 48, "b_part6": 0}
+PASS1_ROW = 16
+EARLY_GATES = BANKS - 2
 SUMMED = (0, 1, 2, 3, 6)
+SCALAR_COLUMNS = (352, 192)
 
 
 def tile_list_gated_link_logits_kernel(tc, tab_words, tab_scales, offs, wa, wb_words, wb_scales,
                                                    wg_words, wg_scales, tab2_words, tab2_scales, offs2, bias, out):
     nc = tc.nc
     with ExitStack() as ctx:
-        keep = ctx.enter_context(tc.tile_pool(name="keep", bufs=1))
-        staged = ctx.enter_context(tc.tile_pool(name="staged", bufs=1))
-        ring = ctx.enter_context(tc.tile_pool(name="ring", bufs=4))
+        lists = ctx.enter_context(tc.tile_pool(name="lists", bufs=1))
+        sb = ctx.enter_context(tc.tile_pool(name="sb", bufs=1))
         psum = ctx.enter_context(tc.psum_pool(name="psum", bufs=1))
 
-        def bank(name, b):
-            return psum.tile([P, 512], F32, name=name, tag="bank%d" % b)
+        address = {"free": 0}
 
-        idx = keep.tile([P, S // 16], U16, name="idx")
-        idx2 = keep.tile([P, S2 // 16], U16, name="idx2")
-        tab_plane = staged.tile([P, T // 4], I32, name="tab_plane", offset=3 * KB, align_bytes=64)
-        tab_w = [staged.tile([P, T], I32, name="tab_w%d" % a, offset=(8 + 12 * a) * KB, align_bytes=64) for a in range(PASSES)]
-        wg_plane = keep.tile([P, PASSES, H // 4], I32, name="wg_plane", align_bytes=64)
-        wb_plane = keep.tile([P, PASSES, H // 4], I32, name="wb_plane", align_bytes=64)
-        tab2_plane = keep.tile([P, T2 // 4], I32, name="tab2_plane", align_bytes=64)
-        wb_w = keep.tile([P, PASSES, H], I32, name="wb_w", align_bytes=64)
-        wg_w = keep.tile([P, PASSES, H // 2], I32, name="wg_w", align_bytes=64)
-        wa_w = [keep.tile([P, H], U32, name="wa_w%d" % a, align_bytes=64) for a in range(PASSES)]
-        wa_s = [keep.tile([P, H], U8, name="wa_s%d" % a, align_bytes=64) for a in range(PASSES)]
-        moved = keep.tile([P, S // 4], I32, name="moved", align_bytes=64)
-        v_s = keep.tile([P, S], U8, name="v_s", align_bytes=64)
-        ident = keep.tile([P, P], F32, name="ident", align_bytes=64)
+        def sbuf(name, shape, dtype, over=None, skip=0, room=0):
+            if over is None:
+                size = WIDTH[dtype]
+                for n in shape[1:]:
+                    size *= n
+                address[name] = address["free"]
+                address["free"] += max(size, room)
+            else:
+                address[name] = address[over] + skip
+            return sb.tile(shape, dtype, name=name, offset=address[name], align_bytes=64)
+
+        free_banks = list(range(BANKS))
+        bank_of = {}
+
+        def take_bank(key):
+            bank_of[key] = free_banks.pop(0)
+            return psum.tile([P, BANK_COLUMNS], F32, name=key[0], tag="bank%d" % bank_of[key])
+
+        def leave_bank(key):
+            free_banks.append(bank_of.pop(key))
+
+        table_bytes = 4 * T
+        term_bytes = 4 * H
+        idx = lists.tile([P, S // LIST_ROWS], U16, name="idx")
+        idx2 = lists.tile([P, S2 // LIST_ROWS], U16, name="idx2")
+        tab_plane = sbuf("tab_plane", [P, T // 4], I32, room=table_bytes)
+        tab_w = [sbuf("tab_w0", [P, T], I32), sbuf("tab_w1", [P, T], I32, room=table_bytes + 2 * S2)]
+        tab2_plane = sbuf("tab2_plane", [P, T2 // 4], I32)
+        wg_plane = sbuf("wg_plane", [P, PASSES, H // 4], I32)
+        wb_plane = sbuf("wb_plane", [P, PASSES, H // 4], I32)
+        wg_w = sbuf("wg_w", [P, PASSES, H // 2], I32)
+        wb_w = sbuf("wb_w", [P, PASSES, H], I32)
+        v_plane0 = sbuf("v_plane0", [P, S], U8)
+        v_plane1 = sbuf("v_plane1", [P, S // 4], I32)
+        ident = sbuf("ident", [P, P], F32)
+        v_w, acc, gate, a_part, b_part, wa_raw, wa_bf, wa_w, wa_s, v2, h_rows, h_bf, h_w, h_s = [{} for n in range(14)]
 
         def words(w):
             return w.rearrange("p t i -> p (t i)").bitcast(I32)
 
-        def load_weight_plane(queue, plane, row, scales):
-            rows = scales.bitcast(I32).rearrange("a (q r) t -> r q a t", r=4)
-            for r in range(4):
-                queue.dma_start(out=plane[row + r: P: 32, :, :], in_=rows[r])
+        def load_weight_plane(plane, row, scales):
+            rows = scales.bitcast(I32).rearrange("a (q s) c -> s q a c", s=4)
+            for s in range(4):
+                nc.sync.dma_start(out=plane[row + s: P: 32, :, :], in_=rows[s])
 
-        nc.gpsimd.memset(tab_plane[:], 0)
-        nc.gpsimd.memset(tab2_plane[:], 0)
-        nc.vector.memset(wg_plane[:], 0)
-        nc.vector.memset(wb_plane[:], 0)
-        nc.vector.memset(moved[:], 0)
-        nc.sync.dma_start(idx[:], offs)
-        nc.sync.dma_start(idx2[:], offs2)
-        tab_rows = tab_scales.bitcast(I32).rearrange("a (q r) t -> r q a t", r=4)
-        for r in range(4):
-            nc.sync.dma_start(out=tab_plane[r: P: PASS1_ROW, :], in_=tab_rows[r])
-        nc.sync.dma_start(out=tab_w[0][:], in_=words(tab_words[0]))
-        nc.sync.dma_start(out=wg_w[:], in_=wg_words.bitcast(I32).rearrange("a p c -> p a c"))
-        load_weight_plane(nc.sync, wg_plane, 0, wg_scales)
-        nc.sync.dma_start(out=tab_w[1][:], in_=words(tab_words[1]))
-        make_identity(nc, ident[:])
-        warm = keep.tile([P, 8], F32, name="warm")
-        nc.vector.memset(warm[:, 0:1], 0.0)
-        nc.scalar.activation(out=warm[:, 1:2], in_=warm[:, 0:1], func=ACT.Sigmoid)
+        def load_wa(a):
+            wa_raw[a] = sbuf("wa_raw%d" % a, [P, 4, H], F32, over=("tab_plane", "tab_w0")[a])
+            nc.sync.dma_start(out=wa_raw[a][:], in_=wa[PASS_K * a: PASS_K * (a + 1), :].rearrange("(p t) c -> p t c", t=4))
 
-        v_w, acc, gate, a_part, b_part, wa_raw, wa_bf, v2, h_rows, turned, h_bf, h_w, h_s, y, logits = [{} for n in range(15)]
-
-        def load_tab2_scales():
-            rows = tab2_scales[0].bitcast(I32).rearrange("(q r) t -> r q t", r=4)
-            for r in range(4):
-                nc.sync.dma_start(out=tab2_plane[V2_ROW + r: P: 32, :], in_=rows[r])
-
-        def load_wa_pass(a):
-            wa_raw[a] = staged.tile([P, 4, H], F32, name="wa_raw%d" % a, offset=8 * KB * a, align_bytes=64)
-            nc.sync.dma_start(out=wa_raw[a][:], in_=wa[512 * a: 512 * (a + 1), :].rearrange("(p i) c -> p i c", i=4))
-
-        def load_tab2_words():
-            v2["table"] = staged.tile([P, T2], I32, name="tab2_w", offset=25 * KB, align_bytes=64)
-            nc.sync.dma_start(out=v2["table"][:], in_=words(tab2_words[0]))
-            v2["bias"] = staged.tile([P, S2 // P], F32, name="bias_col", offset=22 * KB, align_bytes=64)
-            with nc.allow_non_contiguous_dma(reason="one bias value to a partition"):
-                nc.sync.dma_start(out=v2["bias"][:], in_=bias.rearrange("(m p) -> p m", p=P))
-
-        def gather_scales():
-            nc.vector.tensor_copy(v_s[:], tab_plane[:].bitcast(U8).indirect(idx[:]))
-
-        def load_wb():
-            nc.sync.dma_start(out=wb_w[:], in_=wb_words.rearrange("a p c i -> p a (c i)").bitcast(I32))
-
-        def load_wb_scales():
-            load_weight_plane(nc.sync, wb_plane, WB_ROW, wb_scales)
-
-        def move_scales():
-            nc.sync.dma_start(out=moved[0: P - PASS1_ROW, :], in_=v_s[PASS1_ROW:, :].bitcast(I32))
-
-        def gather_words(a, lo, hi):
-            tile = keep.tile([P, (hi - lo) * P], U32, name="v_w%d_%d" % (a, lo), align_bytes=64)
-            nc.vector.tensor_copy(tile[:], tab_w[a][:].bitcast(U32).indirect(idx[:, lo * P // 16: hi * P // 16]))
-            for u in range(lo, hi):
-                v_w[u, a] = tile[:, (u - lo) * P: (u - lo + 1) * P]
-
-        def gather_v2_scales():
-            v2["s"] = staged.tile([P, S2], U8, name="v2_s", offset=20 * KB, align_bytes=64)
-            nc.vector.tensor_copy(v2["s"][:], tab2_plane[:].bitcast(U8).indirect(idx2[:]))
-
-        def gather_v2_words():
-            v2["w"] = placed("v2_w", [P, S2], U32)
-            nc.vector.tensor_copy(v2["w"][:], v2["table"][:].bitcast(U32).indirect(idx2[:]))
+        def gather_words(a, first, end):
+            tile = sbuf("v_w%d_%d" % (a, first), [P, (end - first) * P], U32)
+            offsets = idx[:, first * P // LIST_ROWS: end * P // LIST_ROWS]
+            nc.vector.tensor_copy(tile[:], tab_w[a][:].bitcast(U32).indirect(offsets))
+            for u in range(first, end):
+                v_w[u, a] = tile[:, (u - first) * P: (u - first + 1) * P]
 
         def weight(kind, a):
             if kind == "z":
@@ -133,276 +106,237 @@ def tile_list_gated_link_logits_kernel(tc, tab_words, tab_scales, offs, wa, wb_w
                 return wb_w[:, a, :].bitcast(FP8X4), wb_plane[WB_ROW:, a, :].bitcast(U8)
             return wa_w[a][:].bitcast(FP8X4), wa_s[a][:]
 
-        def product(kind, u, passes, b=None):
-            if 0 in passes:
-                acc[kind, u] = bank(kind, b)
+        def product(kind, u, passes=range(PASSES)):
             for a in passes:
+                if a == 0:
+                    acc[kind, u] = take_bank((kind, u))
                 rhs, rhs_scale = weight(kind, a)
-                plane = (v_s[:], moved[:].bitcast(U8))[a]
+                v_plane = (v_plane0[:], v_plane1[:].bitcast(U8))[a]
                 nc.tensor.matmul_mx(out=acc[kind, u][:], lhsT=v_w[u, a].bitcast(FP8X4),
-                                    lhsT_scale=plane[:, u * P: (u + 1) * P], rhs=rhs, rhs_scale=rhs_scale,
+                                    lhsT_scale=v_plane[:, u * P: (u + 1) * P], rhs=rhs, rhs_scale=rhs_scale,
                                     start=(a == 0), stop=(a == PASSES - 1))
 
-        def placed(name, shape, dtype):
-            if name in PLACE:
-                return staged.tile(shape, dtype, name=name, offset=PLACE[name] * KB, align_bytes=64)
-            return keep.tile(shape, dtype, name=name, align_bytes=64)
-
-        def gate_tile(u):
-            return placed("gate%d" % u, [P, H], F32)
-
-        def b_part_tile(u):
-            return placed("b_part%d" % u, [P, H], F32)
-
-        def a_part_tile(u):
-            return placed("a_part%d" % u, [P, H], F32)
-
-        def by_pairs(t):
-            return t[:].rearrange("j (p w e) -> j w p e", w=2, e=2)
-
-        def pairs(t):
-            return t[:].rearrange("j (w p e) -> j w p e", w=2, e=2)
-
-        def sigmoid(u):
+        def from_bank(u, tile):
             if u in SUMMED:
-                return sigmoid_last(u)
-            gate[u] = gate_tile(u)
-            nc.scalar.activation(out=pairs(gate[u]), in_=by_pairs(acc["z", u]), func=ACT.Sigmoid)
+                return tile[:].rearrange("j (p t) -> j t p", t=4)
+            return tile[:].rearrange("j (p w e) -> j w p e", w=2, e=2)
 
-        def b_term(u):
+        def stored(u, tile):
             if u in SUMMED:
-                return b_term_last(u)
-            b_part[u] = b_part_tile(u)
-            for w in range(2):
-                nc.vector.scalar_tensor_tensor(out=pairs(b_part[u])[:, w], in0=pairs(gate[u])[:, w], scalar=1.0,
-                                               in1=by_pairs(acc["b", u])[:, w], op0=ALU.subtract, op1=ALU.mult)
+                return tile[:].rearrange("j (t p) -> j t p", t=4)
+            return tile[:].rearrange("j (w p e) -> j w p e", w=2, e=2)
+
+        def sigmoid(u, over=None, skip=0):
+            gate[u] = sbuf("gate%d" % u, [P, H], F32, over=over, skip=skip)
+            nc.scalar.activation(out=stored(u, gate[u]), in_=from_bank(u, acc["z", u]), func=ACT.Sigmoid)
+            leave_bank(("z", u))
+
+        def b_term(u, over=None):
+            b_part[u] = sbuf("b_part%d" % u, [P, H], F32, over=over)
+            dst, g, b = stored(u, b_part[u]), stored(u, gate[u]), from_bank(u, acc["b", u])
+            parts = [(dst, g, b)] if u in SUMMED else [(dst[:, w], g[:, w], b[:, w]) for w in range(2)]
+            for dst_part, g_part, b_bank in parts:
+                nc.vector.scalar_tensor_tensor(out=dst_part, in0=g_part, scalar=1.0, in1=b_bank,
+                                               op0=ALU.subtract, op1=ALU.mult)
+            leave_bank(("b", u))
 
         def a_term(u):
+            a_part[u] = sbuf("a_part%d" % u, [P, H], F32)
+            dst, g, a_bank = stored(u, a_part[u]), stored(u, gate[u]), from_bank(u, acc["a", u])
             if u in SUMMED:
-                return a_term_last(u)
-            a_part[u] = a_part_tile(u)
-            nc.vector.tensor_tensor(out=pairs(a_part[u]), in0=by_pairs(acc["a", u]), in1=pairs(gate[u]), op=ALU.mult)
-
-        def blend(u, engine):
-            h_rows[u] = ring.tile([P, H], BF16, name="h_rows", align_bytes=64)
-            engine.tensor_tensor(out=h_rows[u][:], in0=a_part[u][:], in1=b_part[u][:], op=ALU.subtract)
-
-        def by_slot(t):
-            return t[:].rearrange("j (p t) -> j t p", t=4)
-
-        def slots(t):
-            return t[:].rearrange("j (t p) -> j t p", t=4)
-
-        def sigmoid_last(u):
-            gate[u] = gate_tile(u)
-            nc.scalar.activation(out=slots(gate[u]), in_=by_slot(acc["z", u]), func=ACT.Sigmoid)
-
-        def b_term_last(u):
-            b_part[u] = b_part_tile(u)
-            nc.vector.scalar_tensor_tensor(out=slots(b_part[u]), in0=slots(gate[u]), scalar=1.0, in1=by_slot(acc["b", u]),
-                                           op0=ALU.subtract, op1=ALU.mult)
-
-        def a_term_last(u):
-            a_part[u] = a_part_tile(u)
-            nc.vector.scalar_tensor_tensor(out=slots(a_part[u]), in0=slots(gate[u]), scalar=-1.0, in1=by_slot(acc["a", u]),
-                                           op0=ALU.mult, op1=ALU.mult)
-
-        def turn_sum(u, b):
-            turned[u] = bank("turned", b)
-            for n, part in enumerate((b_part[u], a_part[u])):
-                for t in range(4):
-                    nc.tensor.matmul(turned[u][:, t * P: (t + 1) * P], part[:, t * P: (t + 1) * P], ident[:], is_transpose=True,
-                                     start=(n == 0 and t == 0), stop=(n == 1 and t == 3))
-
-        def interleave_part(u, us):
-            if u == us[0]:
-                h_bf[us] = placed("h_bf%d" % us[0], [P, 4 * P * len(us)], BF16)
-            at = 4 * P * (u - us[0])
-            nc.scalar.activation(out=h_bf[us][:, at: at + 4 * P].rearrange("p (j t) -> p j t", t=4),
-                                 in_=turned[u][:].rearrange("p (t j) -> p j t", t=4), func=ACT.Copy, scale=-1.0)
-
-        def interleave_last(u):
-            interleave_part(u, (u,))
-
-        def round_cols(a, engine, lo, hi):
-            if a not in wa_bf:
-                wa_bf[a] = staged.tile([P, 4 * H], BF16, name="wa_bf%d" % a, offset=(34 + 4 * a) * KB, align_bytes=64)
-            if engine == "G":
-                nc.gpsimd.tensor_scalar(out=wa_bf[a][:, 4 * lo: 4 * hi].rearrange("p (c i) -> p c i", i=4),
-                                        in0=wa_raw[a][:, :, lo:hi].rearrange("p i c -> p c i"),
-                                        scalar1=1.0, scalar2=0.0, op0=ALU.mult, op1=ALU.add)
-                return
-            dst = wa_bf[a][:, 4 * lo: 4 * hi].rearrange("p (c x i) -> p c i x", x=4, i=4)
-            src = wa_raw[a][:, :, lo:hi].rearrange("p i (c x) -> p c i x", x=4)
-            if engine == "A":
-                nc.scalar.copy(out=dst, in_=src)
+                nc.vector.scalar_tensor_tensor(out=dst, in0=g, scalar=-1.0, in1=a_bank, op0=ALU.mult, op1=ALU.mult)
             else:
-                nc.vector.tensor_copy(dst, src)
+                nc.vector.tensor_tensor(out=dst, in0=a_bank, in1=g, op=ALU.mult)
+            leave_bank(("a", u))
 
-        def quantise_pass(a):
+        def round_wa(a, helper):
+            wa_bf[a] = sbuf("wa_bf%d" % a, [P, 4 * H], BF16)
+            split = SCALAR_COLUMNS[a]
+
+            def four_columns_at_a_time(first, end):
+                return (wa_bf[a][:, 4 * first: 4 * end].rearrange("p (c x t) -> p c t x", x=4, t=4),
+                        wa_raw[a][:, :, first:end].rearrange("p t (c x) -> p c t x", x=4))
+
+            dst, src = four_columns_at_a_time(0, split)
+            nc.scalar.copy(out=dst, in_=src)
+            if helper is nc.vector:
+                nc.vector.tensor_copy(*four_columns_at_a_time(split, H))
+            else:
+                nc.gpsimd.tensor_scalar(out=wa_bf[a][:, 4 * split:].rearrange("p (c t) -> p c t", t=4),
+                                        in0=wa_raw[a][:, :, split:].rearrange("p t c -> p c t"),
+                                        scalar1=1.0, scalar2=0.0, op0=ALU.mult, op1=ALU.add)
+
+        def quantise_wa(a):
+            wa_w[a] = sbuf("wa_w%d" % a, [P, H], U32)
+            wa_s[a] = sbuf("wa_s%d" % a, [P, H], U8)
             nc.vector.quantize_mx(out=wa_w[a][:].bitcast(FP8X4), scales=wa_s[a][:], in_=wa_bf[a][:])
 
-        def turn(us, b):
-            turned[us] = bank("turned", b)
-            for t, u in enumerate(us):
+        def h_slice(first, units):
+            pair = first // 2
+            if pair not in h_bf:
+                h_bf[pair] = sbuf("h_bf%d" % pair, [P, 2 * 4 * P], BF16)
+            start = 4 * P * (first % 2)
+            return h_bf[pair][:, start: start + 4 * P * units]
+
+        def turn_summed(u):
+            bank = take_bank(("turned", u))
+            for n, part in enumerate((b_part[u], a_part[u])):
+                for t in range(4):
+                    nc.tensor.matmul(bank[:, t * P: (t + 1) * P], part[:, t * P: (t + 1) * P], ident[:],
+                                     is_transpose=True, start=(n == 0 and t == 0), stop=(n == 1 and t == 3))
+            nc.scalar.activation(out=h_slice(u, 1).rearrange("p (j t) -> p j t", t=4),
+                                 in_=bank[:].rearrange("p (t j) -> p j t", t=4), func=ACT.Copy, scale=-1.0)
+            leave_bank(("turned", u))
+
+        def subtract(u, engine):
+            h_rows[u] = sbuf("h_rows%d" % u, [P, H], BF16)
+            engine.tensor_tensor(out=h_rows[u][:], in0=a_part[u][:], in1=b_part[u][:], op=ALU.subtract)
+
+        def turn_subtracted(first, units):
+            bank = take_bank(("turned", first))
+            for n in range(units):
                 for w in range(2):
-                    nc.tensor.transpose(turned[us][:, (2 * t + w) * P: (2 * t + w + 1) * P],
-                                        h_rows[u][:].bitcast(F32)[:, w * P: (w + 1) * P], ident[:])
+                    nc.tensor.transpose(bank[:, (2 * n + w) * P: (2 * n + w + 1) * P],
+                                        h_rows[first + n][:].bitcast(F32)[:, w * P: (w + 1) * P], ident[:])
+            nc.scalar.copy(out=h_slice(first, units).bitcast(F32).rearrange("p (n j w) -> p n j w", j=P, w=2),
+                           in_=bank[:, 0: 2 * P * units].rearrange("p (n w j) -> p n j w", j=P, w=2))
+            leave_bank(("turned", first))
 
-        def interleave(us):
-            n = len(us) * P
-            h_bf[us] = placed("h_bf%d" % us[0], [P, 4 * n], BF16)
-            nc.scalar.copy(out=h_bf[us][:].bitcast(F32).rearrange("p (t j w) -> p t j w", j=P, w=2),
-                           in_=turned[us][:, 0: 2 * n].rearrange("p (t w j) -> p t j w", j=P, w=2))
+        def quantise_h(pair):
+            h_w[pair] = sbuf("h_w%d" % pair, [P, 2 * P], U32)
+            h_s[pair] = sbuf("h_s%d" % pair, [P, 2 * P], U8)
+            nc.vector.quantize_mx(out=h_w[pair][:].bitcast(FP8X4), scales=h_s[pair][:], in_=h_bf[pair][:])
 
-        def quantise_h(us):
-            n = len(us) * P
-            h_w[us] = placed("h_w%d" % us[0], [P, n], U32)
-            h_s[us] = placed("h_s%d" % us[0], [P, n], U8)
-            nc.vector.quantize_mx(out=h_w[us][:].bitcast(FP8X4), scales=h_s[us][:], in_=h_bf[us][:])
+        def score(pair):
+            for half in range(2):
+                acc["y", pair, half] = take_bank(("y", pair, half))
+                for n in range(2):
+                    m = 2 * half + n
+                    nc.tensor.matmul_mx(out=acc["y", pair, half][:, n * 2 * P: (n + 1) * 2 * P],
+                                        lhsT=v2["w"][:, m * P: (m + 1) * P].bitcast(FP8X4),
+                                        lhsT_scale=v2["s"][V2_ROW:, m * P: (m + 1) * P],
+                                        rhs=h_w[pair][:].bitcast(FP8X4), rhs_scale=h_s[pair][:], start=True, stop=True)
 
-        def score(us, i, b):
-            n = len(us) * P
-            y[us, i] = bank("y", b)
-            for t in range(2):
-                m = 2 * i + t
-                nc.tensor.matmul_mx(out=y[us, i][:, t * n: (t + 1) * n],
-                                    lhsT=v2["w"][:, m * P: (m + 1) * P].bitcast(FP8X4),
-                                    lhsT_scale=v2["s"][V2_ROW:, m * P: (m + 1) * P],
-                                    rhs=h_w[us][:].bitcast(FP8X4), rhs_scale=h_s[us][:], start=True, stop=True)
-
-        def add_bias(us, i, on_vector):
-            n = len(us) * P
-            if n == P:
-                if i == 0:
-                    logits[us] = keep.tile([P, 4, n], F32, name="logits%d" % us[0])
-                dst = logits[us][:, 2 * i: 2 * i + 2, :]
-            else:
-                logits[us, i] = keep.tile([P, 2, n], F32, name="logits%d_%d" % (us[0], i))
-                dst = logits[us, i][:]
-            for t in range(2):
-                m = 2 * i + t
-                src = y[us, i][:, t * n: (t + 1) * n]
-                if on_vector:
-                    nc.vector.tensor_scalar(out=dst[:, t, :], in0=src, scalar1=v2["bias"][:, m: m + 1], scalar2=None, op0=ALU.add)
+        def finish(pair, half, engine):
+            for n in range(2):
+                m = 2 * half + n
+                logits = sbuf("logits%d_%d" % (pair, m), [P, 2 * P], F32)
+                src = acc["y", pair, half][:, n * 2 * P: (n + 1) * 2 * P]
+                if engine is nc.vector:
+                    nc.vector.tensor_scalar(out=logits[:], in0=src, scalar1=v2["bias"][:, m: m + 1], scalar2=None, op0=ALU.add)
                 else:
-                    nc.scalar.activation(out=dst[:, t, :], in_=src, func=ACT.Identity, bias=v2["bias"][:, m: m + 1])
+                    nc.scalar.activation(out=logits[:], in_=src, func=ACT.Identity, bias=v2["bias"][:, m: m + 1])
+                nc.sync.dma_start(out=out[m * P: (m + 1) * P, pair * 2 * P: (pair + 1) * 2 * P], in_=logits[:])
+            leave_bank(("y", pair, half))
 
-        def store_half(us, i):
-            n = len(us) * P
-            j0 = us[0] * P
-            nc.sync.dma_start(out=out[2 * P * i: 2 * P * (i + 1), j0: j0 + n].rearrange("(m p) j -> p m j", p=P), in_=logits[us, i][:])
+        nc.gpsimd.memset(tab_plane[:], 0)
+        nc.gpsimd.memset(tab2_plane[:], 0)
+        nc.vector.memset(wg_plane[:], 0)
+        nc.vector.memset(wb_plane[:], 0)
+        nc.vector.memset(v_plane1[:], 0)
 
-        def store(us):
-            n = len(us) * P
-            j0 = us[0] * P
-            nc.sync.dma_start(out=out[:, j0: j0 + n].rearrange("(m p) j -> p m j", p=P), in_=logits[us][:])
+        nc.sync.dma_start(idx[:], offs)
+        nc.sync.dma_start(idx2[:], offs2)
+        tab_rows = tab_scales.bitcast(I32).rearrange("a (q s) c -> s q a c", s=4)
+        for s in range(4):
+            nc.sync.dma_start(out=tab_plane[s: P: PASS1_ROW, :], in_=tab_rows[s])
+        nc.sync.dma_start(out=tab_w[0][:], in_=words(tab_words[0]))
+        nc.sync.dma_start(out=wg_w[:], in_=wg_words.bitcast(I32).rearrange("a p c -> p a c"))
+        load_weight_plane(wg_plane, 0, wg_scales)
+        nc.sync.dma_start(out=tab_w[1][:], in_=words(tab_words[1]))
+        make_identity(nc, ident[:])
 
-        gather_scales()
-        move_scales()
-        load_tab2_scales()
-        load_wb()
-        load_wb_scales()
-        load_wa_pass(0)
-        gather_words(0, 0, 2)
-        gather_words(0, 2, 8)
-        load_wa_pass(1)
-        for u in range(6):
-            product("z", u, (0,), u)
-        gather_words(1, 0, 2)
-        gather_words(1, 2, 4)
-        gather_words(1, 4, 8)
-        load_tab2_words()
-        gather_v2_scales()
-        for u in range(6):
+        nc.vector.tensor_copy(v_plane0[:], tab_plane[:].bitcast(U8).indirect(idx[:]))
+        nc.sync.dma_start(out=v_plane1[0: P - PASS1_ROW, :], in_=v_plane0[PASS1_ROW:, :].bitcast(I32))
+        tab2_rows = tab2_scales[0].bitcast(I32).rearrange("(q s) c -> s q c", s=4)
+        for s in range(4):
+            nc.sync.dma_start(out=tab2_plane[V2_ROW + s: P: 32, :], in_=tab2_rows[s])
+        nc.sync.dma_start(out=wb_w[:], in_=wb_words.rearrange("a p c i -> p a (c i)").bitcast(I32))
+        load_weight_plane(wb_plane, WB_ROW, wb_scales)
+        load_wa(0)
+
+        for first, end in ((0, 2), (2, 4), (4, UNITS)):
+            gather_words(0, first, end)
+        load_wa(1)
+        for u in range(EARLY_GATES):
+            product("z", u, (0,))
+        for first, end in ((0, 2), (2, 4), (4, UNITS)):
+            gather_words(1, first, end)
+        tab2_w = sbuf("tab2_w", [P, T2], I32, over="tab_w1", skip=2 * S2)
+        nc.sync.dma_start(out=tab2_w[:], in_=words(tab2_words[0]))
+        v2["bias"] = sbuf("bias_col", [P, S2 // P], F32, over="tab_w1", skip=S2)
+        with nc.allow_non_contiguous_dma(reason="one bias value to a partition"):
+            nc.sync.dma_start(out=v2["bias"][:], in_=bias.rearrange("(m p) -> p m", p=P))
+        v2["s"] = sbuf("v2_s", [P, S2], U8, over="tab_w1")
+        nc.vector.tensor_copy(v2["s"][:], tab2_plane[:].bitcast(U8).indirect(idx2[:]))
+
+        for u in range(EARLY_GATES):
             product("z", u, (1,))
         for u in range(4):
             sigmoid(u)
         for u in range(4):
-            product("b", u, (0, 1), (6, 7, 0, 1)[u])
-        round_cols(0, 'A', 0, 352)
-        round_cols(0, 'G', 352, 512)
-        round_cols(1, 'A', 0, 192)
-        round_cols(1, 'V', 192, 512)
+            product("b", u)
+        round_wa(0, nc.gpsimd)
+        round_wa(1, nc.vector)
         for u in range(3):
             b_term(u)
-        quantise_pass(0)
-        quantise_pass(1)
-        b_term(3)
-        for u in (4, 5):
-            sigmoid(u)
-            product("b", u, (0, 1), u - 2)
-        for u in (6, 7):
-            product("z", u, (0, 1), u)
-            sigmoid(u)
-        product("b", 6, (0, 1), 0)
+        for a in range(PASSES):
+            quantise_wa(a)
+        sigmoid(4, over="wa_raw0")
+        product("b", 4)
+        sigmoid(5, over="wa_raw1")
+        product("b", 5)
+        for u in range(EARLY_GATES, UNITS):
+            product("z", u)
+            sigmoid(u, over="wa_raw1", skip=(u - 5) * term_bytes)
+        product("b", 6)
         for u in range(4):
-            product("a", u, (0, 1), (4, 5, 6, 1)[u])
+            product("a", u)
+        b_term(3, over="wa_bf1")
 
         a_term(0)
         a_term(1)
-        gather_v2_words()
-        turn_sum(0, 7)
-        interleave_part(0, (0, 1))
-        turn_sum(1, 4)
-        interleave_part(1, (0, 1))
-        product("a", 4, (0, 1), 5)
+        v2["w"] = sbuf("v2_w", [P, S2], U32, over="gate0")
+        nc.vector.tensor_copy(v2["w"][:], tab2_w[:].bitcast(U32).indirect(idx2[:]))
+        turn_summed(0)
+        turn_summed(1)
+        product("a", 4)
         a_term(2)
         a_term(3)
-        b_term(4)
-        turn_sum(2, 7)
-        interleave_part(2, (2, 3))
-        turn_sum(3, 6)
-        interleave_part(3, (2, 3))
-        quantise_h((0, 1))
-        product("a", 5, (0, 1), 2)
-        score((0, 1), 0, 1)
-        score((0, 1), 1, 4)
+        b_term(4, over="gate1")
+        turn_summed(2)
+        turn_summed(3)
+        quantise_h(0)
+        product("a", 5)
+        score(0)
+
         a_term(4)
-        blend(4, nc.gpsimd)
-        b_term(5)
-        for i in range(2):
-            add_bias((0, 1), i, False)
-            store_half((0, 1), i)
-        product("a", 6, (0, 1), 5)
-        quantise_h((2, 3))
+        subtract(4, nc.gpsimd)
+        b_term(5, over="h_bf0")
+        for half in range(2):
+            finish(0, half, nc.scalar)
+        product("a", 6)
+        quantise_h(1)
         a_term(5)
-        b_term(6)
-        blend(5, nc.gpsimd)
-        product("b", 7, (0, 1), 3)
-        score((2, 3), 0, 7)
-        score((2, 3), 1, 6)
-        product("a", 7, (0, 1), 1)
-        add_bias((2, 3), 0, False)
-        store_half((2, 3), 0)
-        add_bias((2, 3), 1, False)
-        store_half((2, 3), 1)
+        b_term(6, over="gate4")
+        subtract(5, nc.gpsimd)
+        product("b", 7)
+        product("a", 7)
+        score(1)
+
         a_term(6)
-        turn_sum(6, 0)
-        interleave_part(6, (6,))
-        turn((4, 5), 2)
-        interleave((4, 5))
         b_term(7)
         a_term(7)
-        blend(7, nc.vector)
-        quantise_h((6,))
-        score((6,), 0, 6)
-        score((6,), 1, 4)
-        quantise_h((4, 5))
-        score((4, 5), 0, 5)
-        score((4, 5), 1, 3)
-        turn((7,), 7)
-        interleave((7,))
-        add_bias((6,), 0, False)
-        add_bias((6,), 1, False)
-        store((6,))
-        quantise_h((7,))
-        add_bias((4, 5), 0, True)
-        store_half((4, 5), 0)
-        add_bias((4, 5), 1, False)
-        store_half((4, 5), 1)
-        score((7,), 0, 2)
-        score((7,), 1, 1)
-        add_bias((7,), 0, True)
-        add_bias((7,), 1, False)
-        store((7,))
+        subtract(7, nc.vector)
+        finish(1, 0, nc.scalar)
+        turn_subtracted(4, 2)
+        turn_summed(6)
+        quantise_h(2)
+        turn_subtracted(7, 1)
+        finish(1, 1, nc.vector)
+        score(2)
+        quantise_h(3)
+        score(3)
+        for pair in (2, 3):
+            finish(pair, 0, nc.scalar)
+            finish(pair, 1, nc.vector)

@@ -255,12 +255,13 @@ def tile_list_gated_link_logits_kernel(tc, tab_words, tab_scales, offs, wa, wb_w
         load_weight_plane(wb_plane, WB_ROW, wb_scales)
         load_wa(0)
 
-        for first, end in ((0, 2), (2, 4), (4, UNITS)):
+        halves = ((0, UNITS // 2), (UNITS // 2, UNITS))
+        for first, end in halves:
             gather_words(0, first, end)
         load_wa(1)
         for u in range(EARLY_GATES):
             product("z", u, (0,))
-        for first, end in ((0, 2), (2, 4), (4, UNITS)):
+        for first, end in halves:
             gather_words(1, first, end)
         tab2_w = sbuf("tab2_w", [P, T2], I32, over="tab_w1", skip=2 * S2)
         nc.sync.dma_start(out=tab2_w[:], in_=words(tab2_words[0]))

@@ -29,8 +29,8 @@ WB_ROW = 4
 V2_ROW = 8
 PASS1_ROW = 16
 EARLY_GATES = BANKS - 2
-SUMMED = (0, 1, 2, 3, 6)
-SCALAR_COLUMNS = (352, 192)
+SUMMED = (0, 3, 5)
+SCALAR_COLUMNS = (256, 192)
 
 
 def tile_list_gated_link_logits_kernel(tc, tab_words, tab_scales, offs, wa, wb_words, wb_scales,
@@ -73,7 +73,7 @@ def tile_list_gated_link_logits_kernel(tc, tab_words, tab_scales, offs, wa, wb_w
         tab2_plane = sbuf("tab2_plane", [P, T2 // 4], I32)
         wg_plane = sbuf("wg_plane", [P, PASSES, H // 4], I32)
         wb_plane = sbuf("wb_plane", [P, PASSES, H // 4], I32)
-        wg_w = sbuf("wg_w", [P, PASSES, H // 2], I32)
+        wg_w = [sbuf("wg_w%d" % a, [P, H // 2], I32) for a in range(PASSES)]
         wb_w = sbuf("wb_w", [P, PASSES, H], I32)
         v_plane0 = sbuf("v_plane0", [P, S], U8)
         v_plane1 = sbuf("v_plane1", [P, S // 4], I32)
@@ -101,7 +101,7 @@ def tile_list_gated_link_logits_kernel(tc, tab_words, tab_scales, offs, wa, wb_w
 
         def weight(kind, a):
             if kind == "z":
-                return wg_w[:, a, :].bitcast(U8).bitcast(FP4X4), wg_plane[:, a, :].bitcast(U8)
+                return wg_w[a][:].bitcast(U8).bitcast(FP4X4), wg_plane[:, a, :].bitcast(U8)
             if kind == "b":
                 return wb_w[:, a, :].bitcast(FP8X4), wb_plane[WB_ROW:, a, :].bitcast(U8)
             return wa_w[a][:].bitcast(FP8X4), wa_s[a][:]
@@ -131,8 +131,8 @@ def tile_list_gated_link_logits_kernel(tc, tab_words, tab_scales, offs, wa, wb_w
             nc.scalar.activation(out=stored(u, gate[u]), in_=from_bank(u, acc["z", u]), func=ACT.Sigmoid)
             leave_bank(("z", u))
 
-        def b_term(u, over=None):
-            b_part[u] = sbuf("b_part%d" % u, [P, H], F32, over=over)
+        def b_term(u, over=None, skip=0):
+            b_part[u] = sbuf("b_part%d" % u, [P, H], F32, over=over, skip=skip)
             dst, g, b = stored(u, b_part[u]), stored(u, gate[u]), from_bank(u, acc["b", u])
             parts = [(dst, g, b)] if u in SUMMED else [(dst[:, w], g[:, w], b[:, w]) for w in range(2)]
             for dst_part, g_part, b_bank in parts:
@@ -140,8 +140,8 @@ def tile_list_gated_link_logits_kernel(tc, tab_words, tab_scales, offs, wa, wb_w
                                                op0=ALU.subtract, op1=ALU.mult)
             leave_bank(("b", u))
 
-        def a_term(u):
-            a_part[u] = sbuf("a_part%d" % u, [P, H], F32)
+        def a_term(u, over=None):
+            a_part[u] = sbuf("a_part%d" % u, [P, H], F32, over=over)
             dst, g, a_bank = stored(u, a_part[u]), stored(u, gate[u]), from_bank(u, acc["a", u])
             if u in SUMMED:
                 nc.vector.scalar_tensor_tensor(out=dst, in0=g, scalar=-1.0, in1=a_bank, op0=ALU.mult, op1=ALU.mult)
@@ -174,7 +174,7 @@ def tile_list_gated_link_logits_kernel(tc, tab_words, tab_scales, offs, wa, wb_w
         def h_slice(first, units):
             pair = first // 2
             if pair not in h_bf:
-                h_bf[pair] = sbuf("h_bf%d" % pair, [P, 2 * 4 * P], BF16)
+                h_bf[pair] = sbuf("h_bf%d" % pair, [P, 2 * 4 * P], BF16, room=2 * H + term_bytes)
             start = 4 * P * (first % 2)
             return h_bf[pair][:, start: start + 4 * P * units]
 
@@ -188,8 +188,8 @@ def tile_list_gated_link_logits_kernel(tc, tab_words, tab_scales, offs, wa, wb_w
                                  in_=bank[:].rearrange("p (t j) -> p j t", t=4), func=ACT.Copy, scale=-1.0)
             leave_bank(("turned", u))
 
-        def subtract(u, engine):
-            h_rows[u] = sbuf("h_rows%d" % u, [P, H], BF16)
+        def subtract(u, engine, over=None):
+            h_rows[u] = sbuf("h_rows%d" % u, [P, H], BF16, over=over)
             engine.tensor_tensor(out=h_rows[u][:], in0=a_part[u][:], in1=b_part[u][:], op=ALU.subtract)
 
         def turn_subtracted(first, units):
@@ -202,32 +202,43 @@ def tile_list_gated_link_logits_kernel(tc, tab_words, tab_scales, offs, wa, wb_w
                            in_=bank[:, 0: 2 * P * units].rearrange("p (n w j) -> p n j w", j=P, w=2))
             leave_bank(("turned", first))
 
-        def quantise_h(pair):
-            h_w[pair] = sbuf("h_w%d" % pair, [P, 2 * P], U32)
-            h_s[pair] = sbuf("h_s%d" % pair, [P, 2 * P], U8)
-            nc.vector.quantize_mx(out=h_w[pair][:].bitcast(FP8X4), scales=h_s[pair][:], in_=h_bf[pair][:])
+        def quantise_h(first, units=2):
+            h_w[first] = sbuf("h_w%d" % first, [P, units * P], U32)
+            h_s[first] = sbuf("h_s%d" % first, [P, units * P], U8)
+            nc.vector.quantize_mx(out=h_w[first][:].bitcast(FP8X4), scales=h_s[first][:], in_=h_slice(first, units))
 
-        def score(pair):
-            for half in range(2):
-                acc["y", pair, half] = take_bank(("y", pair, half))
-                for n in range(2):
-                    m = 2 * half + n
-                    nc.tensor.matmul_mx(out=acc["y", pair, half][:, n * 2 * P: (n + 1) * 2 * P],
-                                        lhsT=v2["w"][:, m * P: (m + 1) * P].bitcast(FP8X4),
-                                        lhsT_scale=v2["s"][V2_ROW:, m * P: (m + 1) * P],
-                                        rhs=h_w[pair][:].bitcast(FP8X4), rhs_scale=h_s[pair][:], start=True, stop=True)
+        def score(first, units=2, blocks_a_bank=2):
+            width = units * P
+            for m in range(S2 // P):
+                n = m % blocks_a_bank
+                if n == 0:
+                    bank = take_bank(("y", first, m))
+                acc["y", first, m] = bank[:, n * width: (n + 1) * width]
+                nc.tensor.matmul_mx(out=acc["y", first, m],
+                                    lhsT=v2["w"][:, m * P: (m + 1) * P].bitcast(FP8X4),
+                                    lhsT_scale=v2["s"][V2_ROW:, m * P: (m + 1) * P],
+                                    rhs=h_w[first][:].bitcast(FP8X4), rhs_scale=h_s[first][:], start=True, stop=True)
 
-        def finish(pair, half, engine):
-            for n in range(2):
-                m = 2 * half + n
-                logits = sbuf("logits%d_%d" % (pair, m), [P, 2 * P], F32)
-                src = acc["y", pair, half][:, n * 2 * P: (n + 1) * 2 * P]
+        def finish(first, blocks, engine, units=2, joined=False):
+            width = units * P
+            rows = out.rearrange("(m p) j -> p m j", p=P)
+            logits = [sbuf("logits%d_%d" % (first, m), [P, width], F32) for m in blocks]
+            if joined:
+                both = sbuf("logits%d_%d" % (first, blocks[0]), [P, len(blocks), width], F32)
+                logits = [both[:, n, :] for n in range(len(blocks))]
+            else:
+                logits = [tile[:] for tile in logits]
+            for m, dst in zip(blocks, logits):
+                src = acc["y", first, m]
                 if engine is nc.vector:
-                    nc.vector.tensor_scalar(out=logits[:], in0=src, scalar1=v2["bias"][:, m: m + 1], scalar2=None, op0=ALU.add)
+                    nc.vector.tensor_scalar(out=dst, in0=src, scalar1=v2["bias"][:, m: m + 1], scalar2=None, op0=ALU.add)
                 else:
-                    nc.scalar.activation(out=logits[:], in_=src, func=ACT.Identity, bias=v2["bias"][:, m: m + 1])
-                nc.sync.dma_start(out=out[m * P: (m + 1) * P, pair * 2 * P: (pair + 1) * 2 * P], in_=logits[:])
-            leave_bank(("y", pair, half))
+                    nc.scalar.activation(out=dst, in_=src, func=ACT.Identity, bias=v2["bias"][:, m: m + 1])
+                if not joined:
+                    nc.sync.dma_start(out=rows[:, m, first * P: first * P + width], in_=dst)
+            if joined:
+                nc.sync.dma_start(out=rows[:, blocks[0]: blocks[-1] + 1, first * P: first * P + width], in_=both[:])
+            leave_bank(("y", first, blocks[0]))
 
         nc.gpsimd.memset(tab_plane[:], 0)
         nc.gpsimd.memset(tab2_plane[:], 0)
@@ -241,9 +252,10 @@ def tile_list_gated_link_logits_kernel(tc, tab_words, tab_scales, offs, wa, wb_w
         for s in range(4):
             nc.sync.dma_start(out=tab_plane[s: P: PASS1_ROW, :], in_=tab_rows[s])
         nc.sync.dma_start(out=tab_w[0][:], in_=words(tab_words[0]))
-        nc.sync.dma_start(out=wg_w[:], in_=wg_words.bitcast(I32).rearrange("a p c -> p a c"))
+        nc.sync.dma_start(out=wg_w[0][:], in_=wg_words[0].bitcast(I32))
         load_weight_plane(wg_plane, 0, wg_scales)
         nc.sync.dma_start(out=tab_w[1][:], in_=words(tab_words[1]))
+        nc.sync.dma_start(out=wg_w[1][:], in_=wg_words[1].bitcast(I32))
         make_identity(nc, ident[:])
 
         nc.vector.tensor_copy(v_plane0[:], tab_plane[:].bitcast(U8).indirect(idx[:]))
@@ -255,89 +267,79 @@ def tile_list_gated_link_logits_kernel(tc, tab_words, tab_scales, offs, wa, wb_w
         load_weight_plane(wb_plane, WB_ROW, wb_scales)
         load_wa(0)
 
-        halves = ((0, UNITS // 2), (UNITS // 2, UNITS))
-        for first, end in halves:
+        for first, end in ((0, 2), (2, 4), (4, 8)):
             gather_words(0, first, end)
         load_wa(1)
         for u in range(EARLY_GATES):
             product("z", u, (0,))
-        for first, end in halves:
-            gather_words(1, first, end)
+        for first in range(0, UNITS, 2):
+            gather_words(1, first, first + 2)
         tab2_w = sbuf("tab2_w", [P, T2], I32, over="tab_w1", skip=2 * S2)
         nc.sync.dma_start(out=tab2_w[:], in_=words(tab2_words[0]))
         v2["bias"] = sbuf("bias_col", [P, S2 // P], F32, over="tab_w1", skip=S2)
         with nc.allow_non_contiguous_dma(reason="one bias value to a partition"):
             nc.sync.dma_start(out=v2["bias"][:], in_=bias.rearrange("(m p) -> p m", p=P))
-        v2["s"] = sbuf("v2_s", [P, S2], U8, over="tab_w1")
+        v2["s"] = sbuf("v2_s", [P, S2], U8)
         nc.vector.tensor_copy(v2["s"][:], tab2_plane[:].bitcast(U8).indirect(idx2[:]))
 
         for u in range(EARLY_GATES):
             product("z", u, (1,))
-        for u in range(4):
             sigmoid(u)
-        for u in range(4):
+        for u in range(UNITS):
             product("b", u)
         round_wa(0, nc.gpsimd)
-        round_wa(1, nc.vector)
-        for u in range(3):
+        for u in range(EARLY_GATES):
             b_term(u)
-        for a in range(PASSES):
-            quantise_wa(a)
-        sigmoid(4, over="wa_raw0")
-        product("b", 4)
-        sigmoid(5, over="wa_raw1")
-        product("b", 5)
+        quantise_wa(0)
+        round_wa(1, nc.vector)
         for u in range(EARLY_GATES, UNITS):
             product("z", u)
-            sigmoid(u, over="wa_raw1", skip=(u - 5) * term_bytes)
-        product("b", 6)
-        for u in range(4):
-            product("a", u)
-        b_term(3, over="wa_bf1")
-
-        a_term(0)
-        a_term(1)
-        v2["w"] = sbuf("v2_w", [P, S2], U32, over="gate0")
+            sigmoid(u, over="wa_raw1", skip=(u - EARLY_GATES) * term_bytes)
+        quantise_wa(1)
+        for a in range(PASSES):
+            for u in range(4):
+                product("a", u, (a,))
+        v2["w"] = sbuf("v2_w", [P, S2], U32)
         nc.vector.tensor_copy(v2["w"][:], tab2_w[:].bitcast(U32).indirect(idx2[:]))
-        turn_summed(0)
-        turn_summed(1)
         product("a", 4)
+        a_term(1)
+        subtract(1, nc.gpsimd)
+        a_term(0, over="tab2_w")
         a_term(2)
-        a_term(3)
-        b_term(4, over="gate1")
-        turn_summed(2)
-        turn_summed(3)
-        quantise_h(0)
+        subtract(2, nc.gpsimd)
         product("a", 5)
-        score(0)
-
-        a_term(4)
-        subtract(4, nc.gpsimd)
-        b_term(5, over="h_bf0")
-        for half in range(2):
-            finish(0, half, nc.scalar)
+        turn_summed(0)
+        turn_subtracted(1, 1)
+        a_term(3)
         product("a", 6)
-        quantise_h(1)
+        b_term(6, over="gate2")
+        a_term(4)
+        turn_summed(3)
+        turn_subtracted(2, 1)
+        quantise_h(0)
+        subtract(4, nc.gpsimd, over="h_bf0")
         a_term(5)
-        b_term(6, over="gate4")
-        subtract(5, nc.gpsimd)
-        product("b", 7)
         product("a", 7)
-        score(1)
-
+        score(0)
         a_term(6)
-        b_term(7)
+        b_term(7, over="h_bf0", skip=2 * H)
         a_term(7)
-        subtract(7, nc.vector)
-        finish(1, 0, nc.scalar)
-        turn_subtracted(4, 2)
-        turn_summed(6)
         quantise_h(2)
-        turn_subtracted(7, 1)
-        finish(1, 1, nc.vector)
+        subtract(6, nc.vector, over="gate7")
+        subtract(7, nc.vector)
+        finish(0, (0, 1), nc.scalar)
+        finish(0, (2, 3), nc.scalar)
+        turn_summed(5)
+        turn_subtracted(4, 1)
         score(2)
-        quantise_h(3)
-        score(3)
-        for pair in (2, 3):
-            finish(pair, 0, nc.scalar)
-            finish(pair, 1, nc.vector)
+        turn_subtracted(6, 2)
+        finish(2, (0, 1), nc.vector)
+        quantise_h(4)
+        finish(2, (2, 3), nc.vector)
+        score(4)
+        quantise_h(6)
+        finish(4, (0, 1), nc.scalar)
+        finish(4, (2, 3), nc.vector)
+        score(6, blocks_a_bank=1)
+        for m in range(4):
+            finish(6, (m,), (nc.scalar, nc.vector)[m % 2])

@@ -56,13 +56,16 @@ def tile_list_gated_link_logits_kernel(tc, tab_words, tab_scales, offs, wa, wb_w
 
         free_banks = list(range(BANKS))
         bank_of = {}
+        left_by = {}
 
-        def take_bank(key):
-            bank_of[key] = free_banks.pop(0)
+        def take_bank(key, after=None):
+            bank_of[key] = free_banks[0] if after is None else left_by[after]
+            free_banks.remove(bank_of[key])
             return psum.tile([P, BANK_COLUMNS], F32, name=key[0], tag="bank%d" % bank_of[key])
 
         def leave_bank(key):
-            free_banks.append(bank_of.pop(key))
+            left_by[key] = bank_of.pop(key)
+            free_banks.append(left_by[key])
 
         table_bytes = 4 * T
         term_bytes = 4 * H
@@ -106,10 +109,10 @@ def tile_list_gated_link_logits_kernel(tc, tab_words, tab_scales, offs, wa, wb_w
                 return wb_w[:, a, :].bitcast(FP8X4), wb_plane[WB_ROW:, a, :].bitcast(U8)
             return wa_w[a][:].bitcast(FP8X4), wa_s[a][:]
 
-        def product(kind, u, passes=range(PASSES)):
+        def product(kind, u, passes=range(PASSES), after=None):
             for a in passes:
                 if a == 0:
-                    acc[kind, u] = take_bank((kind, u))
+                    acc[kind, u] = take_bank((kind, u), after)
                 rhs, rhs_scale = weight(kind, a)
                 v_plane = (v_plane0[:], v_plane1[:].bitcast(U8))[a]
                 nc.tensor.matmul_mx(out=acc[kind, u][:], lhsT=v_w[u, a].bitcast(FP8X4),
@@ -174,12 +177,12 @@ def tile_list_gated_link_logits_kernel(tc, tab_words, tab_scales, offs, wa, wb_w
         def h_slice(first, units):
             pair = first // 2
             if pair not in h_bf:
-                h_bf[pair] = sbuf("h_bf%d" % pair, [P, 2 * 4 * P], BF16, room=2 * H + term_bytes)
+                h_bf[pair] = sbuf("h_bf%d" % pair, [P, 2 * 4 * P], BF16)
             start = 4 * P * (first % 2)
             return h_bf[pair][:, start: start + 4 * P * units]
 
-        def turn_summed(u):
-            bank = take_bank(("turned", u))
+        def turn_summed(u, after=None):
+            bank = take_bank(("turned", u), after)
             for n, part in enumerate((b_part[u], a_part[u])):
                 for t in range(4):
                     nc.tensor.matmul(bank[:, t * P: (t + 1) * P], part[:, t * P: (t + 1) * P], ident[:],
@@ -189,17 +192,17 @@ def tile_list_gated_link_logits_kernel(tc, tab_words, tab_scales, offs, wa, wb_w
             leave_bank(("turned", u))
 
         def subtract(u, engine, over=None):
-            h_rows[u] = sbuf("h_rows%d" % u, [P, H], BF16, over=over)
+            h_rows[u] = sbuf("h_rows%d" % u, [P, H], BF16, over=over, room=term_bytes)
             engine.tensor_tensor(out=h_rows[u][:], in0=a_part[u][:], in1=b_part[u][:], op=ALU.subtract)
 
-        def turn_subtracted(first, units):
-            bank = take_bank(("turned", first))
+        def turn_subtracted(first, units, after=None, copy=nc.scalar.copy):
+            bank = take_bank(("turned", first), after)
             for n in range(units):
                 for w in range(2):
                     nc.tensor.transpose(bank[:, (2 * n + w) * P: (2 * n + w + 1) * P],
                                         h_rows[first + n][:].bitcast(F32)[:, w * P: (w + 1) * P], ident[:])
-            nc.scalar.copy(out=h_slice(first, units).bitcast(F32).rearrange("p (n j w) -> p n j w", j=P, w=2),
-                           in_=bank[:, 0: 2 * P * units].rearrange("p (n w j) -> p n j w", j=P, w=2))
+            copy(out=h_slice(first, units).bitcast(F32).rearrange("p (n j w) -> p n j w", j=P, w=2),
+                 in_=bank[:, 0: 2 * P * units].rearrange("p (n w j) -> p n j w", j=P, w=2))
             leave_bank(("turned", first))
 
         def quantise_h(first, units=2):
@@ -207,38 +210,39 @@ def tile_list_gated_link_logits_kernel(tc, tab_words, tab_scales, offs, wa, wb_w
             h_s[first] = sbuf("h_s%d" % first, [P, units * P], U8)
             nc.vector.quantize_mx(out=h_w[first][:].bitcast(FP8X4), scales=h_s[first][:], in_=h_slice(first, units))
 
-        def score(first, units=2, blocks_a_bank=2):
+        def score(first, units=2, blocks_a_bank=2, after=(None,) * 4):
             width = units * P
             for m in range(S2 // P):
                 n = m % blocks_a_bank
                 if n == 0:
-                    bank = take_bank(("y", first, m))
+                    bank = take_bank(("y", first, m), after[m // blocks_a_bank])
                 acc["y", first, m] = bank[:, n * width: (n + 1) * width]
                 nc.tensor.matmul_mx(out=acc["y", first, m],
                                     lhsT=v2["w"][:, m * P: (m + 1) * P].bitcast(FP8X4),
                                     lhsT_scale=v2["s"][V2_ROW:, m * P: (m + 1) * P],
                                     rhs=h_w[first][:].bitcast(FP8X4), rhs_scale=h_s[first][:], start=True, stop=True)
 
-        def finish(first, blocks, engine, units=2, joined=False):
+        def finish(first, blocks, engine, units=2, joined=False, over=None):
             width = units * P
             rows = out.rearrange("(m p) j -> p m j", p=P)
-            logits = [sbuf("logits%d_%d" % (first, m), [P, width], F32) for m in blocks]
             if joined:
                 both = sbuf("logits%d_%d" % (first, blocks[0]), [P, len(blocks), width], F32)
                 logits = [both[:, n, :] for n in range(len(blocks))]
             else:
-                logits = [tile[:] for tile in logits]
+                logits = [sbuf("logits%d_%d" % (first, m), [P, width], F32, over=over)[:] for m in blocks]
             for m, dst in zip(blocks, logits):
-                src = acc["y", first, m]
+                src = acc.pop(("y", first, m))
                 if engine is nc.vector:
                     nc.vector.tensor_scalar(out=dst, in0=src, scalar1=v2["bias"][:, m: m + 1], scalar2=None, op0=ALU.add)
                 else:
                     nc.scalar.activation(out=dst, in_=src, func=ACT.Identity, bias=v2["bias"][:, m: m + 1])
                 if not joined:
                     nc.sync.dma_start(out=rows[:, m, first * P: first * P + width], in_=dst)
+                opener = m if ("y", first, m) in bank_of else m - 1
+                if opener != m or ("y", first, m + 1) not in acc or ("y", first, m + 1) in bank_of:
+                    leave_bank(("y", first, opener))
             if joined:
                 nc.sync.dma_start(out=rows[:, blocks[0]: blocks[-1] + 1, first * P: first * P + width], in_=both[:])
-            leave_bank(("y", first, blocks[0]))
 
         nc.gpsimd.memset(tab_plane[:], 0)
         nc.gpsimd.memset(tab2_plane[:], 0)
@@ -302,44 +306,43 @@ def tile_list_gated_link_logits_kernel(tc, tab_words, tab_scales, offs, wa, wb_w
         v2["w"] = sbuf("v2_w", [P, S2], U32)
         nc.vector.tensor_copy(v2["w"][:], tab2_w[:].bitcast(U32).indirect(idx2[:]))
         product("a", 4)
+        product("a", 5)
         a_term(1)
         subtract(1, nc.gpsimd)
         a_term(0, over="tab2_w")
         a_term(2)
         subtract(2, nc.gpsimd)
-        product("a", 5)
         turn_summed(0)
-        turn_subtracted(1, 1)
-        a_term(3)
         product("a", 6)
+        a_term(3)
+        turn_subtracted(1, 1)
+        turn_summed(3, after=("a", 3))
+        turn_subtracted(2, 1, after=("turned", 0))
         b_term(6, over="gate2")
         a_term(4)
-        turn_summed(3)
-        turn_subtracted(2, 1)
+        product("a", 7, after=("b", 6))
+        a_term(5)
         quantise_h(0)
         subtract(4, nc.gpsimd, over="h_bf0")
-        a_term(5)
-        product("a", 7)
-        score(0)
-        a_term(6)
-        b_term(7, over="h_bf0", skip=2 * H)
+        score(0, after=(("a", 4), ("turned", 1)))
+        a_term(6, over="a_part3")
+        b_term(7, over="h_rows2")
         a_term(7)
         quantise_h(2)
         subtract(6, nc.vector, over="gate7")
         subtract(7, nc.vector)
-        finish(0, (0, 1), nc.scalar)
-        finish(0, (2, 3), nc.scalar)
-        turn_summed(5)
-        turn_subtracted(4, 1)
-        score(2)
-        turn_subtracted(6, 2)
-        finish(2, (0, 1), nc.vector)
+        finish(0, (0, 1, 2), nc.scalar)
+        turn_summed(5, after=("a", 5))
+        turn_subtracted(4, 1, after=("turned", 3))
+        finish(0, (3,), nc.scalar, over="a_part5")
+        score(2, after=(("turned", 2), ("a", 6)))
         quantise_h(4)
-        finish(2, (2, 3), nc.vector)
+        finish(2, (0, 1), nc.scalar)
+        finish(2, (2, 3), nc.scalar)
+        turn_subtracted(6, 2, copy=nc.vector.tensor_copy)
         score(4)
         quantise_h(6)
-        finish(4, (0, 1), nc.scalar)
-        finish(4, (2, 3), nc.vector)
+        finish(4, (0, 1, 2, 3), nc.scalar)
         score(6, blocks_a_bank=1)
         for m in range(4):
-            finish(6, (m,), (nc.scalar, nc.vector)[m % 2])
+            finish(6, (m,), nc.scalar if m == 2 else nc.vector)

@@ -30,7 +30,7 @@ V2_ROW = 8
 PASS1_ROW = 16
 EARLY_GATES = BANKS - 2
 SUMMED = (0, 3, 5)
-SCALAR_COLUMNS = (256, 192)
+SCALAR_COLUMNS = (304, 320)
 
 
 def tile_list_gated_link_logits_kernel(tc, tab_words, tab_scales, offs, wa, wb_words, wb_scales,
@@ -153,7 +153,7 @@ def tile_list_gated_link_logits_kernel(tc, tab_words, tab_scales, offs, wa, wb_w
             leave_bank(("a", u))
 
         def round_wa(a, helper):
-            wa_bf[a] = sbuf("wa_bf%d" % a, [P, 4 * H], BF16)
+            wa_bf[a] = sbuf("wa_bf%d" % a, [P, 4 * H], BF16, over=(None, "wa_bf0")[a])
             split = SCALAR_COLUMNS[a]
 
             def four_columns_at_a_time(first, end):
@@ -289,44 +289,46 @@ def tile_list_gated_link_logits_kernel(tc, tab_words, tab_scales, offs, wa, wb_w
         for u in range(EARLY_GATES):
             product("z", u, (1,))
             sigmoid(u)
-        for u in range(UNITS):
+        for u in range(5):
             product("b", u)
         round_wa(0, nc.gpsimd)
-        for u in range(EARLY_GATES):
+        for u in range(2):
+            b_term(u)
+        for u in range(EARLY_GATES, UNITS):
+            product("z", u, after=("b", u - EARLY_GATES))
+            sigmoid(u)
+        for u in range(5, UNITS):
+            product("b", u)
+        for u in range(2, 5):
             b_term(u)
         quantise_wa(0)
-        round_wa(1, nc.vector)
-        for u in range(EARLY_GATES, UNITS):
-            product("z", u)
-            sigmoid(u, over="wa_raw1", skip=(u - EARLY_GATES) * term_bytes)
+        round_wa(1, nc.gpsimd)
+        for u in range(5, UNITS):
+            b_term(u)
         quantise_wa(1)
         for a in range(PASSES):
-            for u in range(4):
+            for u in (1, 0, 2, 3, 4, 5):
                 product("a", u, (a,))
         v2["w"] = sbuf("v2_w", [P, S2], U32)
         nc.vector.tensor_copy(v2["w"][:], tab2_w[:].bitcast(U32).indirect(idx2[:]))
-        product("a", 4)
-        product("a", 5)
         a_term(1)
         subtract(1, nc.gpsimd)
         a_term(0, over="tab2_w")
         a_term(2)
         subtract(2, nc.gpsimd)
-        turn_summed(0)
-        product("a", 6)
+        turn_summed(0, after=("a", 1))
+        product("a", 6, after=("a", 0))
         a_term(3)
-        turn_subtracted(1, 1)
+        turn_subtracted(1, 1, after=("a", 2))
         turn_summed(3, after=("a", 3))
         turn_subtracted(2, 1, after=("turned", 0))
-        b_term(6, over="gate2")
         a_term(4)
-        product("a", 7, after=("b", 6))
+        product("a", 7, after=("a", 4))
         a_term(5)
         quantise_h(0)
         subtract(4, nc.gpsimd, over="h_bf0")
-        score(0, after=(("a", 4), ("turned", 1)))
+        score(0)
         a_term(6, over="a_part3")
-        b_term(7, over="h_rows2")
         a_term(7)
         quantise_h(2)
         subtract(6, nc.vector, over="gate7")

@@ -210,37 +210,36 @@ def tile_list_gated_link_logits_kernel(tc, tab_words, tab_scales, offs, wa, wb_w
             h_s[first] = sbuf("h_s%d" % first, [P, units * P], U8)
             nc.vector.quantize_mx(out=h_w[first][:].bitcast(FP8X4), scales=h_s[first][:], in_=h_slice(first, units))
 
-        def score(first, units=2, blocks_a_bank=2, after=(None,) * 4):
+        def score(first, units=2, banks=((0, 1), (2, 3)), after=(None,) * 4):
             width = units * P
-            for m in range(S2 // P):
-                n = m % blocks_a_bank
-                if n == 0:
-                    bank = take_bank(("y", first, m), after[m // blocks_a_bank])
-                acc["y", first, m] = bank[:, n * width: (n + 1) * width]
-                nc.tensor.matmul_mx(out=acc["y", first, m],
-                                    lhsT=v2["w"][:, m * P: (m + 1) * P].bitcast(FP8X4),
-                                    lhsT_scale=v2["s"][V2_ROW:, m * P: (m + 1) * P],
-                                    rhs=h_w[first][:].bitcast(FP8X4), rhs_scale=h_s[first][:], start=True, stop=True)
+            for blocks, left in zip(banks, after):
+                bank = take_bank(("y", first, blocks), left)
+                for n, m in enumerate(blocks):
+                    acc["y", first, m] = (bank[:, n * width: (n + 1) * width], blocks)
+                    nc.tensor.matmul_mx(out=acc["y", first, m][0],
+                                        lhsT=v2["w"][:, m * P: (m + 1) * P].bitcast(FP8X4),
+                                        lhsT_scale=v2["s"][V2_ROW:, m * P: (m + 1) * P],
+                                        rhs=h_w[first][:].bitcast(FP8X4), rhs_scale=h_s[first][:], start=True, stop=True)
 
         def finish(first, blocks, engine, units=2, joined=False, over=None):
             width = units * P
             rows = out.rearrange("(m p) j -> p m j", p=P)
             if joined:
-                both = sbuf("logits%d_%d" % (first, blocks[0]), [P, len(blocks), width], F32)
+                both = sbuf("logits%d_%d" % (first, blocks[0]), [P, len(blocks), width], F32, over=over)
                 logits = [both[:, n, :] for n in range(len(blocks))]
             else:
-                logits = [sbuf("logits%d_%d" % (first, m), [P, width], F32, over=over)[:] for m in blocks]
+                logits = [sbuf("logits%d_%d" % (first, m), [P, width], F32, over=over, skip=4 * width * n)[:]
+                          for n, m in enumerate(blocks)]
             for m, dst in zip(blocks, logits):
-                src = acc.pop(("y", first, m))
+                src, neighbours = acc.pop(("y", first, m))
                 if engine is nc.vector:
                     nc.vector.tensor_scalar(out=dst, in0=src, scalar1=v2["bias"][:, m: m + 1], scalar2=None, op0=ALU.add)
                 else:
                     nc.scalar.activation(out=dst, in_=src, func=ACT.Identity, bias=v2["bias"][:, m: m + 1])
                 if not joined:
                     nc.sync.dma_start(out=rows[:, m, first * P: first * P + width], in_=dst)
-                opener = m if ("y", first, m) in bank_of else m - 1
-                if opener != m or ("y", first, m + 1) not in acc or ("y", first, m + 1) in bank_of:
-                    leave_bank(("y", first, opener))
+                if not any(("y", first, other) in acc for other in neighbours):
+                    leave_bank(("y", first, neighbours))
             if joined:
                 nc.sync.dma_start(out=rows[:, blocks[0]: blocks[-1] + 1, first * P: first * P + width], in_=both[:])
 
@@ -254,7 +253,7 @@ def tile_list_gated_link_logits_kernel(tc, tab_words, tab_scales, offs, wa, wb_w
         nc.sync.dma_start(idx2[:], offs2)
         tab_rows = tab_scales.bitcast(I32).rearrange("a (q s) c -> s q a c", s=4)
         for s in range(4):
-            nc.sync.dma_start(out=tab_plane[s: P: PASS1_ROW, :], in_=tab_rows[s])
+            (nc.sync, nc.scalar)[s % 2].dma_start(out=tab_plane[s: P: PASS1_ROW, :], in_=tab_rows[s])
         nc.sync.dma_start(out=tab_w[0][:], in_=words(tab_words[0]))
         nc.sync.dma_start(out=wg_w[0][:], in_=wg_words[0].bitcast(I32))
         load_weight_plane(wg_plane, 0, wg_scales)
@@ -327,16 +326,16 @@ def tile_list_gated_link_logits_kernel(tc, tab_words, tab_scales, offs, wa, wb_w
         a_term(5)
         quantise_h(0)
         subtract(4, nc.gpsimd, over="h_bf0")
-        score(0)
+        score(0, banks=((0, 1), (2,), (3,)))
         a_term(6, over="a_part3")
         a_term(7)
+        finish(0, (3,), nc.vector)
         quantise_h(2)
         subtract(6, nc.vector, over="gate7")
         subtract(7, nc.vector)
         finish(0, (0, 1, 2), nc.scalar)
         turn_summed(5, after=("a", 5))
         turn_subtracted(4, 1, after=("turned", 3))
-        finish(0, (3,), nc.scalar, over="a_part5")
         score(2, after=(("turned", 2), ("a", 6)))
         quantise_h(4)
         finish(2, (0, 1), nc.scalar)
@@ -344,7 +343,8 @@ def tile_list_gated_link_logits_kernel(tc, tab_words, tab_scales, offs, wa, wb_w
         turn_subtracted(6, 2, copy=nc.vector.tensor_copy)
         score(4)
         quantise_h(6)
-        finish(4, (0, 1, 2, 3), nc.scalar)
-        score(6, blocks_a_bank=1)
+        finish(4, (0, 1), nc.scalar)
+        finish(4, (2, 3), nc.vector, over="h_bf3")
+        score(6, banks=((0,), (1,), (2,), (3,)))
         for m in range(4):
-            finish(6, (m,), nc.scalar if m == 2 else nc.vector)
+            finish(6, (m,), (nc.scalar, nc.vector)[m % 2])

@@ -253,7 +253,7 @@ def tile_list_gated_link_logits_kernel(tc, tab_words, tab_scales, offs, wa, wb_w
         nc.sync.dma_start(idx2[:], offs2)
         tab_rows = tab_scales.bitcast(I32).rearrange("a (q s) c -> s q a c", s=4)
         for s in range(4):
-            (nc.sync, nc.scalar)[s % 2].dma_start(out=tab_plane[s: P: PASS1_ROW, :], in_=tab_rows[s])
+            nc.sync.dma_start(out=tab_plane[s: P: PASS1_ROW, :], in_=tab_rows[s])
         nc.sync.dma_start(out=tab_w[0][:], in_=words(tab_words[0]))
         nc.sync.dma_start(out=wg_w[0][:], in_=wg_words[0].bitcast(I32))
         load_weight_plane(wg_plane, 0, wg_scales)

@@ -338,13 +338,13 @@ def tile_list_gated_link_logits_kernel(tc, tab_words, tab_scales, offs, wa, wb_w
         turn_subtracted(4, 1, after=("turned", 3))
         score(2, after=(("turned", 2), ("a", 6)))
         quantise_h(4)
-        finish(2, (0, 1), nc.scalar)
-        finish(2, (2, 3), nc.scalar)
+        finish(2, (0, 1), nc.scalar, joined=True)
+        finish(2, (2, 3), nc.scalar, joined=True)
         turn_subtracted(6, 2, copy=nc.vector.tensor_copy)
         score(4)
         quantise_h(6)
-        finish(4, (0, 1), nc.scalar)
-        finish(4, (2, 3), nc.vector, over="h_bf3")
+        finish(4, (0, 1), nc.scalar, joined=True)
+        finish(4, (2, 3), nc.vector, joined=True, over="h_bf3")
         score(6, banks=((0,), (1,), (2,), (3,)))
         for m in range(4):
             finish(6, (m,), (nc.scalar, nc.vector)[m % 2])

@@ -31,6 +31,7 @@ PASS1_ROW = 16
 EARLY_GATES = BANKS - 2
 SUMMED = (0, 3, 5)
 SCALAR_COLUMNS = (304, 320)
+WARM_PASSES = 5
 
 
 def tile_list_gated_link_logits_kernel(tc, tab_words, tab_scales, offs, wa, wb_words, wb_scales,
@@ -260,6 +261,17 @@ def tile_list_gated_link_logits_kernel(tc, tab_words, tab_scales, offs, wa, wb_w
         nc.sync.dma_start(out=tab_w[1][:], in_=words(tab_words[1]))
         nc.sync.dma_start(out=wg_w[1][:], in_=wg_words[1].bitcast(I32))
         make_identity(nc, ident[:])
+
+        zeros = sbuf("zeros", [P, 4 * BANK_COLUMNS], BF16)
+        warm_w = sbuf("warm_w", [P, BANK_COLUMNS], U32)
+        warm_s = sbuf("warm_s", [P, BANK_COLUMNS], U8)
+        nc.gpsimd.memset(zeros[:].bitcast(I32), 0)
+        nc.vector.quantize_mx(out=warm_w[:].bitcast(FP8X4), scales=warm_s[:], in_=zeros[:])
+        warm_bank = take_bank(("warm",))
+        for n in range(WARM_PASSES):
+            nc.tensor.matmul_mx(out=warm_bank[:], lhsT=warm_w[:, 0:P].bitcast(FP8X4), lhsT_scale=warm_s[:, 0:P],
+                                rhs=warm_w[:].bitcast(FP8X4), rhs_scale=warm_s[:], start=True, stop=True)
+        leave_bank(("warm",))
 
         nc.vector.tensor_copy(v_plane0[:], tab_plane[:].bitcast(U8).indirect(idx[:]))
         nc.sync.dma_start(out=v_plane1[0: P - PASS1_ROW, :], in_=v_plane0[PASS1_ROW:, :].bitcast(I32))

@@ -317,9 +317,10 @@ def tile_list_gated_link_logits_kernel(tc, tab_words, tab_scales, offs, wa, wb_w
         for u in range(5, UNITS):
             b_term(u)
         quantise_wa(1)
-        for a in range(PASSES):
-            for u in (1, 0, 2, 3, 4, 5):
-                product("a", u, (a,))
+        for u in (1, 0, 2, 3, 4, 5, 6, 7):
+            product("a", u, (0,))
+        for u in (1, 0, 2, 3, 4, 5):
+            product("a", u, (1,))
         v2["w"] = sbuf("v2_w", [P, S2], U32)
         nc.vector.tensor_copy(v2["w"][:], tab2_w[:].bitcast(U32).indirect(idx2[:]))
         a_term(1)
@@ -328,19 +329,19 @@ def tile_list_gated_link_logits_kernel(tc, tab_words, tab_scales, offs, wa, wb_w
         a_term(2)
         subtract(2, nc.gpsimd)
         turn_summed(0, after=("a", 1))
-        product("a", 6, after=("a", 0))
+        product("a", 6, (1,))
         a_term(3)
         turn_subtracted(1, 1, after=("a", 2))
         turn_summed(3, after=("a", 3))
         turn_subtracted(2, 1, after=("turned", 0))
         a_term(4)
-        product("a", 7, after=("a", 4))
+        product("a", 7, (1,))
         a_term(5)
         quantise_h(0)
         subtract(4, nc.gpsimd, over="h_bf0")
-        score(0, banks=((0, 1), (2,), (3,)))
+        score(0, banks=((0, 1), (2,), (3,)), after=(("a", 0), ("turned", 1), ("a", 4)))
         a_term(6, over="a_part3")
-        a_term(7)
+        a_term(7, over="b_part3")
         finish(0, (3,), nc.vector)
         quantise_h(2)
         subtract(6, nc.vector, over="gate7")

@@ -22,6 +22,7 @@ P = 128
 PASS_K = 4 * P
 PASSES = K // PASS_K
 UNITS = S // P
+PAIR = 2 * P
 BANKS = 8
 BANK_COLUMNS = 512
 LIST_ROWS = 16
@@ -29,6 +30,7 @@ WB_ROW = 4
 V2_ROW = 8
 PASS1_ROW = 16
 EARLY_GATES = BANKS - 2
+EARLY_B = 5
 SUMMED = (0, 3, 5)
 SCALAR_COLUMNS = (304, 320)
 WARM_PASSES = 5
@@ -130,13 +132,13 @@ def tile_list_gated_link_logits_kernel(tc, tab_words, tab_scales, offs, wa, wb_w
                 return tile[:].rearrange("j (t p) -> j t p", t=4)
             return tile[:].rearrange("j (w p e) -> j w p e", w=2, e=2)
 
-        def sigmoid(u, over=None, skip=0):
-            gate[u] = sbuf("gate%d" % u, [P, H], F32, over=over, skip=skip)
+        def sigmoid(u):
+            gate[u] = sbuf("gate%d" % u, [P, H], F32)
             nc.scalar.activation(out=stored(u, gate[u]), in_=from_bank(u, acc["z", u]), func=ACT.Sigmoid)
             leave_bank(("z", u))
 
-        def b_term(u, over=None, skip=0):
-            b_part[u] = sbuf("b_part%d" % u, [P, H], F32, over=over, skip=skip)
+        def b_term(u):
+            b_part[u] = sbuf("b_part%d" % u, [P, H], F32)
             dst, g, b = stored(u, b_part[u]), stored(u, gate[u]), from_bank(u, acc["b", u])
             parts = [(dst, g, b)] if u in SUMMED else [(dst[:, w], g[:, w], b[:, w]) for w in range(2)]
             for dst_part, g_part, b_bank in parts:
@@ -153,22 +155,14 @@ def tile_list_gated_link_logits_kernel(tc, tab_words, tab_scales, offs, wa, wb_w
                 nc.vector.tensor_tensor(out=dst, in0=a_bank, in1=g, op=ALU.mult)
             leave_bank(("a", u))
 
-        def round_wa(a, helper):
+        def round_wa(a):
             wa_bf[a] = sbuf("wa_bf%d" % a, [P, 4 * H], BF16, over=(None, "wa_bf0")[a])
             split = SCALAR_COLUMNS[a]
-
-            def four_columns_at_a_time(first, end):
-                return (wa_bf[a][:, 4 * first: 4 * end].rearrange("p (c x t) -> p c t x", x=4, t=4),
-                        wa_raw[a][:, :, first:end].rearrange("p t (c x) -> p c t x", x=4))
-
-            dst, src = four_columns_at_a_time(0, split)
-            nc.scalar.copy(out=dst, in_=src)
-            if helper is nc.vector:
-                nc.vector.tensor_copy(*four_columns_at_a_time(split, H))
-            else:
-                nc.gpsimd.tensor_scalar(out=wa_bf[a][:, 4 * split:].rearrange("p (c t) -> p c t", t=4),
-                                        in0=wa_raw[a][:, :, split:].rearrange("p t c -> p c t"),
-                                        scalar1=1.0, scalar2=0.0, op0=ALU.mult, op1=ALU.add)
+            nc.scalar.copy(out=wa_bf[a][:, 0: 4 * split].rearrange("p (c x t) -> p c t x", x=4, t=4),
+                           in_=wa_raw[a][:, :, 0:split].rearrange("p t (c x) -> p c t x", x=4))
+            nc.gpsimd.tensor_scalar(out=wa_bf[a][:, 4 * split:].rearrange("p (c t) -> p c t", t=4),
+                                    in0=wa_raw[a][:, :, split:].rearrange("p t c -> p c t"),
+                                    scalar1=1.0, scalar2=0.0, op0=ALU.mult, op1=ALU.add)
 
         def quantise_wa(a):
             wa_w[a] = sbuf("wa_w%d" % a, [P, H], U32)
@@ -182,7 +176,7 @@ def tile_list_gated_link_logits_kernel(tc, tab_words, tab_scales, offs, wa, wb_w
             start = 4 * P * (first % 2)
             return h_bf[pair][:, start: start + 4 * P * units]
 
-        def turn_summed(u, after=None):
+        def turn_summed(u, after):
             bank = take_bank(("turned", u), after)
             for n, part in enumerate((b_part[u], a_part[u])):
                 for t in range(4):
@@ -206,31 +200,28 @@ def tile_list_gated_link_logits_kernel(tc, tab_words, tab_scales, offs, wa, wb_w
                  in_=bank[:, 0: 2 * P * units].rearrange("p (n w j) -> p n j w", j=P, w=2))
             leave_bank(("turned", first))
 
-        def quantise_h(first, units=2):
-            h_w[first] = sbuf("h_w%d" % first, [P, units * P], U32)
-            h_s[first] = sbuf("h_s%d" % first, [P, units * P], U8)
-            nc.vector.quantize_mx(out=h_w[first][:].bitcast(FP8X4), scales=h_s[first][:], in_=h_slice(first, units))
+        def quantise_h(first):
+            h_w[first] = sbuf("h_w%d" % first, [P, PAIR], U32)
+            h_s[first] = sbuf("h_s%d" % first, [P, PAIR], U8)
+            nc.vector.quantize_mx(out=h_w[first][:].bitcast(FP8X4), scales=h_s[first][:], in_=h_slice(first, 2))
 
-        def score(first, units=2, banks=((0, 1), (2, 3)), after=(None,) * 4):
-            width = units * P
+        def score(first, banks=((0, 1), (2, 3)), after=(None, None, None, None)):
             for blocks, left in zip(banks, after):
                 bank = take_bank(("y", first, blocks), left)
                 for n, m in enumerate(blocks):
-                    acc["y", first, m] = (bank[:, n * width: (n + 1) * width], blocks)
+                    acc["y", first, m] = (bank[:, n * PAIR: (n + 1) * PAIR], blocks)
                     nc.tensor.matmul_mx(out=acc["y", first, m][0],
                                         lhsT=v2["w"][:, m * P: (m + 1) * P].bitcast(FP8X4),
                                         lhsT_scale=v2["s"][V2_ROW:, m * P: (m + 1) * P],
                                         rhs=h_w[first][:].bitcast(FP8X4), rhs_scale=h_s[first][:], start=True, stop=True)
 
-        def finish(first, blocks, engine, units=2, joined=False, over=None):
-            width = units * P
+        def finish(first, blocks, engine, joined=False, over=None):
             rows = out.rearrange("(m p) j -> p m j", p=P)
             if joined:
-                both = sbuf("logits%d_%d" % (first, blocks[0]), [P, len(blocks), width], F32, over=over)
+                both = sbuf("logits%d_%d" % (first, blocks[0]), [P, len(blocks), PAIR], F32, over=over)
                 logits = [both[:, n, :] for n in range(len(blocks))]
             else:
-                logits = [sbuf("logits%d_%d" % (first, m), [P, width], F32, over=over, skip=4 * width * n)[:]
-                          for n, m in enumerate(blocks)]
+                logits = [sbuf("logits%d_%d" % (first, m), [P, PAIR], F32)[:] for m in blocks]
             for m, dst in zip(blocks, logits):
                 src, neighbours = acc.pop(("y", first, m))
                 if engine is nc.vector:
@@ -238,11 +229,11 @@ def tile_list_gated_link_logits_kernel(tc, tab_words, tab_scales, offs, wa, wb_w
                 else:
                     nc.scalar.activation(out=dst, in_=src, func=ACT.Identity, bias=v2["bias"][:, m: m + 1])
                 if not joined:
-                    nc.sync.dma_start(out=rows[:, m, first * P: first * P + width], in_=dst)
+                    nc.sync.dma_start(out=rows[:, m, first * P: first * P + PAIR], in_=dst)
                 if not any(("y", first, other) in acc for other in neighbours):
                     leave_bank(("y", first, neighbours))
             if joined:
-                nc.sync.dma_start(out=rows[:, blocks[0]: blocks[-1] + 1, first * P: first * P + width], in_=both[:])
+                nc.sync.dma_start(out=rows[:, blocks[0]: blocks[-1] + 1, first * P: first * P + PAIR], in_=both[:])
 
         nc.gpsimd.memset(tab_plane[:], 0)
         nc.gpsimd.memset(tab2_plane[:], 0)
@@ -265,7 +256,8 @@ def tile_list_gated_link_logits_kernel(tc, tab_words, tab_scales, offs, wa, wb_w
         zeros = sbuf("zeros", [P, 4 * BANK_COLUMNS], BF16)
         warm_w = sbuf("warm_w", [P, BANK_COLUMNS], U32)
         warm_s = sbuf("warm_s", [P, BANK_COLUMNS], U8)
-        nc.gpsimd.memset(zeros[:].bitcast(I32), 0)
+        nc.vector.memset(zeros[:].bitcast(I32)[:, 0:BANK_COLUMNS], 0)
+        nc.gpsimd.memset(zeros[:].bitcast(I32)[:, BANK_COLUMNS:], 0)
         nc.vector.quantize_mx(out=warm_w[:].bitcast(FP8X4), scales=warm_s[:], in_=zeros[:])
         warm_bank = take_bank(("warm",))
         for n in range(WARM_PASSES):
@@ -300,29 +292,31 @@ def tile_list_gated_link_logits_kernel(tc, tab_words, tab_scales, offs, wa, wb_w
         for u in range(EARLY_GATES):
             product("z", u, (1,))
             sigmoid(u)
-        for u in range(5):
+        for u in range(EARLY_B):
             product("b", u)
-        round_wa(0, nc.gpsimd)
-        for u in range(2):
+        round_wa(0)
+        for u in range(UNITS - EARLY_GATES):
             b_term(u)
         for u in range(EARLY_GATES, UNITS):
             product("z", u, after=("b", u - EARLY_GATES))
             sigmoid(u)
-        for u in range(5, UNITS):
+        for u in range(EARLY_B, UNITS):
             product("b", u)
-        for u in range(2, 5):
+        for u in range(UNITS - EARLY_GATES, EARLY_B):
             b_term(u)
         quantise_wa(0)
-        round_wa(1, nc.gpsimd)
-        for u in range(5, UNITS):
+        round_wa(1)
+        for u in range(EARLY_B, UNITS):
             b_term(u)
         quantise_wa(1)
+
         for u in (1, 0, 2, 3, 4, 5, 6, 7):
             product("a", u, (0,))
         for u in (1, 0, 2, 3, 4, 5):
             product("a", u, (1,))
         v2["w"] = sbuf("v2_w", [P, S2], U32)
         nc.vector.tensor_copy(v2["w"][:], tab2_w[:].bitcast(U32).indirect(idx2[:]))
+
         a_term(1)
         subtract(1, nc.gpsimd)
         a_term(0, over="tab2_w")
@@ -338,6 +332,7 @@ def tile_list_gated_link_logits_kernel(tc, tab_words, tab_scales, offs, wa, wb_w
         product("a", 7, (1,))
         a_term(5)
         quantise_h(0)
+
         subtract(4, nc.gpsimd, over="h_bf0")
         score(0, banks=((0, 1), (2,), (3,)), after=(("a", 0), ("turned", 1), ("a", 4)))
         a_term(6, over="a_part3")
@@ -353,11 +348,12 @@ def tile_list_gated_link_logits_kernel(tc, tab_words, tab_scales, offs, wa, wb_w
         quantise_h(4)
         finish(2, (0, 1), nc.scalar, joined=True)
         finish(2, (2, 3), nc.scalar, joined=True)
+
         turn_subtracted(6, 2, copy=nc.vector.tensor_copy)
         score(4)
         quantise_h(6)
         finish(4, (0, 1), nc.scalar, joined=True)
         finish(4, (2, 3), nc.vector, joined=True, over="h_bf3")
         score(6, banks=((0,), (1,), (2,), (3,)))
-        for m in range(4):
+        for m in range(S2 // P):
             finish(6, (m,), (nc.scalar, nc.vector)[m % 2])

@@ -33,7 +33,6 @@ EARLY_GATES = BANKS - 2
 EARLY_B = 5
 SUMMED = (0, 3, 5)
 SCALAR_COLUMNS = (304, 320)
-WARM_PASSES = 5
 
 
 def tile_list_gated_link_logits_kernel(tc, tab_words, tab_scales, offs, wa, wb_words, wb_scales,
@@ -252,18 +251,6 @@ def tile_list_gated_link_logits_kernel(tc, tab_words, tab_scales, offs, wa, wb_w
         nc.sync.dma_start(out=tab_w[1][:], in_=words(tab_words[1]))
         nc.sync.dma_start(out=wg_w[1][:], in_=wg_words[1].bitcast(I32))
         make_identity(nc, ident[:])
-
-        zeros = sbuf("zeros", [P, 4 * BANK_COLUMNS], BF16)
-        warm_w = sbuf("warm_w", [P, BANK_COLUMNS], U32)
-        warm_s = sbuf("warm_s", [P, BANK_COLUMNS], U8)
-        nc.vector.memset(zeros[:].bitcast(I32)[:, 0:BANK_COLUMNS], 0)
-        nc.gpsimd.memset(zeros[:].bitcast(I32)[:, BANK_COLUMNS:], 0)
-        nc.vector.quantize_mx(out=warm_w[:].bitcast(FP8X4), scales=warm_s[:], in_=zeros[:])
-        warm_bank = take_bank(("warm",))
-        for n in range(WARM_PASSES):
-            nc.tensor.matmul_mx(out=warm_bank[:], lhsT=warm_w[:, 0:P].bitcast(FP8X4), lhsT_scale=warm_s[:, 0:P],
-                                rhs=warm_w[:].bitcast(FP8X4), rhs_scale=warm_s[:], start=True, stop=True)
-        leave_bank(("warm",))
 
         nc.vector.tensor_copy(v_plane0[:], tab_plane[:].bitcast(U8).indirect(idx[:]))
         nc.sync.dma_start(out=v_plane1[0: P - PASS1_ROW, :], in_=v_plane0[PASS1_ROW:, :].bitcast(I32))

from contextlib import ExitStack

import concourse.mybir as mybir
from concourse.masks import make_identity

K, H, T, S, T2, S2 = 1024, 512, 2048, 1024, 2048, 512
FLOPS = 2 * (3 * K * H * S + H * S2 * S)

F32 = mybir.dt.float32
BF16 = mybir.dt.bfloat16
I32 = mybir.dt.int32
U32 = mybir.dt.uint32
U16 = mybir.dt.uint16
U8 = mybir.dt.uint8
FP8X4 = mybir.dt.float8_e4m3fn_x4
FP4X4 = mybir.dt.float4_e2m1fn_x4
ALU = mybir.AluOpType
ACT = mybir.ActivationFunctionType
WIDTH = {F32: 4, I32: 4, U32: 4, BF16: 2, U8: 1}

P = 128
PASS_K = 4 * P
PASSES = K // PASS_K
UNITS = S // P
PAIR = 2 * P
BANKS = 8
BANK_COLUMNS = 512
LIST_ROWS = 16
WB_ROW = 4
V2_ROW = 8
PASS1_ROW = 16
EARLY_GATES = BANKS - 2
EARLY_B = 5
SUMMED = (0, 3, 5)
SCALAR_COLUMNS = (304, 320)


def tile_list_gated_link_logits_kernel(tc, tab_words, tab_scales, offs, wa, wb_words, wb_scales,
                                                   wg_words, wg_scales, tab2_words, tab2_scales, offs2, bias, out):
    nc = tc.nc
    with ExitStack() as ctx:
        lists = ctx.enter_context(tc.tile_pool(name="lists", bufs=1))
        sb = ctx.enter_context(tc.tile_pool(name="sb", bufs=1))
        psum = ctx.enter_context(tc.psum_pool(name="psum", bufs=1))

        address = {"free": 0}

        def sbuf(name, shape, dtype, over=None, skip=0, room=0):
            if over is None:
                size = WIDTH[dtype]
                for n in shape[1:]:
                    size *= n
                address[name] = address["free"]
                address["free"] += max(size, room)
            else:
                address[name] = address[over] + skip
            return sb.tile(shape, dtype, name=name, offset=address[name], align_bytes=64)

        free_banks = list(range(BANKS))
        bank_of = {}
        left_by = {}

        def take_bank(key, after=None):
            bank_of[key] = free_banks[0] if after is None else left_by[after]
            free_banks.remove(bank_of[key])
            return psum.tile([P, BANK_COLUMNS], F32, name=key[0], tag="bank%d" % bank_of[key])

        def leave_bank(key):
            left_by[key] = bank_of.pop(key)
            free_banks.append(left_by[key])

        table_bytes = 4 * T
        term_bytes = 4 * H
        idx = lists.tile([P, S // LIST_ROWS], U16, name="idx")
        idx2 = lists.tile([P, S2 // LIST_ROWS], U16, name="idx2")
        tab_plane = sbuf("tab_plane", [P, T // 4], I32, room=table_bytes)
        tab_w = [sbuf("tab_w0", [P, T], I32), sbuf("tab_w1", [P, T], I32, room=table_bytes + 2 * S2)]
        tab2_plane = sbuf("tab2_plane", [P, T2 // 4], I32)
        wg_plane = sbuf("wg_plane", [P, PASSES, H // 4], I32)
        wb_plane = sbuf("wb_plane", [P, PASSES, H // 4], I32)
        wg_w = [sbuf("wg_w%d" % a, [P, H // 2], I32) for a in range(PASSES)]
        wb_w = sbuf("wb_w", [P, PASSES, H], I32)
        v_plane0 = sbuf("v_plane0", [P, S], U8)
        v_plane1 = sbuf("v_plane1", [P, S // 4], I32)
        ident = sbuf("ident", [P, P], F32)
        v_w, acc, gate, a_part, b_part, wa_raw, wa_bf, wa_w, wa_s, v2, h_rows, h_bf, h_w, h_s = [{} for n in range(14)]

        def words(w):
            return w.rearrange("p t i -> p (t i)").bitcast(I32)

        def load_weight_plane(plane, row, scales):
            rows = scales.bitcast(I32).rearrange("a (q s) c -> s q a c", s=4)
            for s in range(4):
                nc.sync.dma_start(out=plane[row + s: P: 32, :, :], in_=rows[s])

        def load_wa(a):
            wa_raw[a] = sbuf("wa_raw%d" % a, [P, 4, H], F32, over=("tab_plane", "tab_w0")[a])
            nc.sync.dma_start(out=wa_raw[a][:], in_=wa[PASS_K * a: PASS_K * (a + 1), :].rearrange("(p t) c -> p t c", t=4))

        def gather_words(a, first, end):
            tile = sbuf("v_w%d_%d" % (a, first), [P, (end - first) * P], U32)
            offsets = idx[:, first * P // LIST_ROWS: end * P // LIST_ROWS]
            nc.vector.tensor_copy(tile[:], tab_w[a][:].bitcast(U32).indirect(offsets))
            for u in range(first, end):
                v_w[u, a] = tile[:, (u - first) * P: (u - first + 1) * P]

        def weight(kind, a):
            if kind == "z":
                return wg_w[a][:].bitcast(U8).bitcast(FP4X4), wg_plane[:, a, :].bitcast(U8)
            if kind == "b":
                return wb_w[:, a, :].bitcast(FP8X4), wb_plane[WB_ROW:, a, :].bitcast(U8)
            return wa_w[a][:].bitcast(FP8X4), wa_s[a][:]

        def product(kind, u, passes=range(PASSES), after=None):
            for a in passes:
                if a == 0:
                    acc[kind, u] = take_bank((kind, u), after)
                rhs, rhs_scale = weight(kind, a)
                v_plane = (v_plane0[:], v_plane1[:].bitcast(U8))[a]
                nc.tensor.matmul_mx(out=acc[kind, u][:], lhsT=v_w[u, a].bitcast(FP8X4),
                                    lhsT_scale=v_plane[:, u * P: (u + 1) * P], rhs=rhs, rhs_scale=rhs_scale,
                                    start=(a == 0), stop=(a == PASSES - 1))

        def from_bank(u, tile):
            if u in SUMMED:
                return tile[:].rearrange("j (p t) -> j t p", t=4)
            return tile[:].rearrange("j (p w e) -> j w p e", w=2, e=2)

        def stored(u, tile):
            if u in SUMMED:
                return tile[:].rearrange("j (t p) -> j t p", t=4)
            return tile[:].rearrange("j (w p e) -> j w p e", w=2, e=2)

        def sigmoid(u):
            gate[u] = sbuf("gate%d" % u, [P, H], F32)
            nc.scalar.activation(out=stored(u, gate[u]), in_=from_bank(u, acc["z", u]), func=ACT.Sigmoid)
            leave_bank(("z", u))

        def b_term(u):
            b_part[u] = sbuf("b_part%d" % u, [P, H], F32)
            dst, g, b = stored(u, b_part[u]), stored(u, gate[u]), from_bank(u, acc["b", u])
            parts = [(dst, g, b)] if u in SUMMED else [(dst[:, w], g[:, w], b[:, w]) for w in range(2)]
            for dst_part, g_part, b_bank in parts:
                nc.vector.scalar_tensor_tensor(out=dst_part, in0=g_part, scalar=1.0, in1=b_bank,
                                               op0=ALU.subtract, op1=ALU.mult)
            leave_bank(("b", u))

        def a_term(u, over=None):
            a_part[u] = sbuf("a_part%d" % u, [P, H], F32, over=over)
            dst, g, a_bank = stored(u, a_part[u]), stored(u, gate[u]), from_bank(u, acc["a", u])
            if u in SUMMED:
                nc.vector.scalar_tensor_tensor(out=dst, in0=g, scalar=-1.0, in1=a_bank, op0=ALU.mult, op1=ALU.mult)
            else:
                nc.vector.tensor_tensor(out=dst, in0=a_bank, in1=g, op=ALU.mult)
            leave_bank(("a", u))

        def round_wa(a):
            wa_bf[a] = sbuf("wa_bf%d" % a, [P, 4 * H], BF16, over=(None, "wa_bf0")[a])
            split = SCALAR_COLUMNS[a]
            nc.scalar.copy(out=wa_bf[a][:, 0: 4 * split].rearrange("p (c x t) -> p c t x", x=4, t=4),
                           in_=wa_raw[a][:, :, 0:split].rearrange("p t (c x) -> p c t x", x=4))
            nc.gpsimd.tensor_scalar(out=wa_bf[a][:, 4 * split:].rearrange("p (c t) -> p c t", t=4),
                                    in0=wa_raw[a][:, :, split:].rearrange("p t c -> p c t"),
                                    scalar1=1.0, scalar2=0.0, op0=ALU.mult, op1=ALU.add)

        def quantise_wa(a):
            wa_w[a] = sbuf("wa_w%d" % a, [P, H], U32)
            wa_s[a] = sbuf("wa_s%d" % a, [P, H], U8)
            nc.vector.quantize_mx(out=wa_w[a][:].bitcast(FP8X4), scales=wa_s[a][:], in_=wa_bf[a][:])

        def h_slice(first, units):
            pair = first // 2
            if pair not in h_bf:
                h_bf[pair] = sbuf("h_bf%d" % pair, [P, 2 * 4 * P], BF16)
            start = 4 * P * (first % 2)
            return h_bf[pair][:, start: start + 4 * P * units]

        def turn_summed(u, after):
            bank = take_bank(("turned", u), after)
            for n, part in enumerate((b_part[u], a_part[u])):
                for t in range(4):
                    nc.tensor.matmul(bank[:, t * P: (t + 1) * P], part[:, t * P: (t + 1) * P], ident[:],
                                     is_transpose=True, start=(n == 0 and t == 0), stop=(n == 1 and t == 3))
            nc.scalar.activation(out=h_slice(u, 1).rearrange("p (j t) -> p j t", t=4),
                                 in_=bank[:].rearrange("p (t j) -> p j t", t=4), func=ACT.Copy, scale=-1.0)
            leave_bank(("turned", u))

        def subtract(u, engine, over=None):
            h_rows[u] = sbuf("h_rows%d" % u, [P, H], BF16, over=over, room=term_bytes)
            engine.tensor_tensor(out=h_rows[u][:], in0=a_part[u][:], in1=b_part[u][:], op=ALU.subtract)

        def turn_subtracted(first, units, after=None, copy=nc.scalar.copy):
            bank = take_bank(("turned", first), after)
            for n in range(units):
                for w in range(2):
                    nc.tensor.transpose(bank[:, (2 * n + w) * P: (2 * n + w + 1) * P],
                                        h_rows[first + n][:].bitcast(F32)[:, w * P: (w + 1) * P], ident[:])
            copy(out=h_slice(first, units).bitcast(F32).rearrange("p (n j w) -> p n j w", j=P, w=2),
                 in_=bank[:, 0: 2 * P * units].rearrange("p (n w j) -> p n j w", j=P, w=2))
            leave_bank(("turned", first))

        def quantise_h(first):
            h_w[first] = sbuf("h_w%d" % first, [P, PAIR], U32)
            h_s[first] = sbuf("h_s%d" % first, [P, PAIR], U8)
            nc.vector.quantize_mx(out=h_w[first][:].bitcast(FP8X4), scales=h_s[first][:], in_=h_slice(first, 2))

        def score(first, banks=((0, 1), (2, 3)), after=(None, None, None, None)):
            for blocks, left in zip(banks, after):
                bank = take_bank(("y", first, blocks), left)
                for n, m in enumerate(blocks):
                    acc["y", first, m] = (bank[:, n * PAIR: (n + 1) * PAIR], blocks)
                    nc.tensor.matmul_mx(out=acc["y", first, m][0],
                                        lhsT=v2["w"][:, m * P: (m + 1) * P].bitcast(FP8X4),
                                        lhsT_scale=v2["s"][V2_ROW:, m * P: (m + 1) * P],
                                        rhs=h_w[first][:].bitcast(FP8X4), rhs_scale=h_s[first][:], start=True, stop=True)

        def finish(first, blocks, engine, joined=False, over=None):
            rows = out.rearrange("(m p) j -> p m j", p=P)
            if joined:
                both = sbuf("logits%d_%d" % (first, blocks[0]), [P, len(blocks), PAIR], F32, over=over)
                logits = [both[:, n, :] for n in range(len(blocks))]
            else:
                logits = [sbuf("logits%d_%d" % (first, m), [P, PAIR], F32)[:] for m in blocks]
            for m, dst in zip(blocks, logits):
                src, neighbours = acc.pop(("y", first, m))
                if engine is nc.vector:
                    nc.vector.tensor_scalar(out=dst, in0=src, scalar1=v2["bias"][:, m: m + 1], scalar2=None, op0=ALU.add)
                else:
                    nc.scalar.activation(out=dst, in_=src, func=ACT.Identity, bias=v2["bias"][:, m: m + 1])
                if not joined:
                    nc.sync.dma_start(out=rows[:, m, first * P: first * P + PAIR], in_=dst)
                if not any(("y", first, other) in acc for other in neighbours):
                    leave_bank(("y", first, neighbours))
            if joined:
                nc.sync.dma_start(out=rows[:, blocks[0]: blocks[-1] + 1, first * P: first * P + PAIR], in_=both[:])

        nc.gpsimd.memset(tab_plane[:], 0)
        nc.gpsimd.memset(tab2_plane[:], 0)
        nc.vector.memset(wg_plane[:], 0)
        nc.vector.memset(wb_plane[:], 0)
        nc.vector.memset(v_plane1[:], 0)

        nc.sync.dma_start(idx[:], offs)
        nc.sync.dma_start(idx2[:], offs2)
        tab_rows = tab_scales.bitcast(I32).rearrange("a (q s) c -> s q a c", s=4)
        for s in range(4):
            nc.sync.dma_start(out=tab_plane[s: P: PASS1_ROW, :], in_=tab_rows[s])
        nc.sync.dma_start(out=tab_w[0][:], in_=words(tab_words[0]))
        nc.sync.dma_start(out=wg_w[0][:], in_=wg_words[0].bitcast(I32))
        load_weight_plane(wg_plane, 0, wg_scales)
        nc.sync.dma_start(out=tab_w[1][:], in_=words(tab_words[1]))
        nc.sync.dma_start(out=wg_w[1][:], in_=wg_words[1].bitcast(I32))
        make_identity(nc, ident[:])

        nc.vector.tensor_copy(v_plane0[:], tab_plane[:].bitcast(U8).indirect(idx[:]))
        nc.sync.dma_start(out=v_plane1[0: P - PASS1_ROW, :], in_=v_plane0[PASS1_ROW:, :].bitcast(I32))
        tab2_rows = tab2_scales[0].bitcast(I32).rearrange("(q s) c -> s q c", s=4)
        for s in range(4):
            nc.sync.dma_start(out=tab2_plane[V2_ROW + s: P: 32, :], in_=tab2_rows[s])
        nc.sync.dma_start(out=wb_w[:], in_=wb_words.rearrange("a p c i -> p a (c i)").bitcast(I32))
        load_weight_plane(wb_plane, WB_ROW, wb_scales)
        load_wa(0)

        for first, end in ((0, 2), (2, 4), (4, 8)):
            gather_words(0, first, end)
        load_wa(1)
        for u in range(EARLY_GATES):
            product("z", u, (0,))
        for first in range(0, UNITS, 2):
            gather_words(1, first, first + 2)
        tab2_w = sbuf("tab2_w", [P, T2], I32, over="tab_w1", skip=2 * S2)
        nc.sync.dma_start(out=tab2_w[:], in_=words(tab2_words[0]))
        v2["bias"] = sbuf("bias_col", [P, S2 // P], F32, over="tab_w1", skip=S2)
        with nc.allow_non_contiguous_dma(reason="one bias value to a partition"):
            nc.sync.dma_start(out=v2["bias"][:], in_=bias.rearrange("(m p) -> p m", p=P))
        v2["s"] = sbuf("v2_s", [P, S2], U8)
        nc.vector.tensor_copy(v2["s"][:], tab2_plane[:].bitcast(U8).indirect(idx2[:]))

        for u in range(EARLY_GATES):
            product("z", u, (1,))
            sigmoid(u)
        for u in range(EARLY_B):
            product("b", u)
        round_wa(0)
        for u in range(UNITS - EARLY_GATES):
            b_term(u)
        for u in range(EARLY_GATES, UNITS):
            product("z", u, after=("b", u - EARLY_GATES))
            sigmoid(u)
        for u in range(EARLY_B, UNITS):
            product("b", u)
        for u in range(UNITS - EARLY_GATES, EARLY_B):
            b_term(u)
        quantise_wa(0)
        round_wa(1)
        for u in range(EARLY_B, UNITS):
            b_term(u)
        quantise_wa(1)

        for u in (1, 0, 2, 3, 4, 5, 6, 7):
            product("a", u, (0,))
        for u in (1, 0, 2, 3, 4, 5):
            product("a", u, (1,))
        v2["w"] = sbuf("v2_w", [P, S2], U32)
        nc.vector.tensor_copy(v2["w"][:], tab2_w[:].bitcast(U32).indirect(idx2[:]))

        a_term(1)
        subtract(1, nc.gpsimd)
        a_term(0, over="tab2_w")
        a_term(2)
        subtract(2, nc.gpsimd)
        turn_summed(0, after=("a", 1))
        product("a", 6, (1,))
        a_term(3)
        turn_subtracted(1, 1, after=("a", 2))
        turn_summed(3, after=("a", 3))
        turn_subtracted(2, 1, after=("turned", 0))
        a_term(4)
        product("a", 7, (1,))
        a_term(5)
        quantise_h(0)

        subtract(4, nc.gpsimd, over="h_bf0")
        score(0, banks=((0, 1), (2,), (3,)), after=(("a", 0), ("turned", 1), ("a", 4)))
        a_term(6, over="a_part3")
        a_term(7, over="b_part3")
        finish(0, (3,), nc.vector)
        quantise_h(2)
        subtract(6, nc.vector, over="gate7")
        subtract(7, nc.vector)
        finish(0, (0, 1, 2), nc.scalar)
        turn_summed(5, after=("a", 5))
        turn_subtracted(4, 1, after=("turned", 3))
        score(2, after=(("turned", 2), ("a", 6)))
        quantise_h(4)
        finish(2, (0, 1), nc.scalar, joined=True)
        finish(2, (2, 3), nc.scalar, joined=True)

        turn_subtracted(6, 2, copy=nc.vector.tensor_copy)
        score(4)
        quantise_h(6)
        finish(4, (0, 1), nc.scalar, joined=True)
        finish(4, (2, 3), nc.vector, joined=True, over="h_bf3")
        score(6, banks=((0,), (1,), (2,), (3,)))
        for m in range(S2 // P):
            finish(6, (m,), (nc.scalar, nc.vector)[m % 2])
